import numpy as np
import ml_dtypes


def mxq(x, axis, fmt="e4m3"):
    dtype, down = {"e4m3": (ml_dtypes.float8_e4m3fn, 7), "e5m2": (ml_dtypes.float8_e5m2, 14)}[fmt]
    v = np.moveaxis(np.asarray(x, np.float32).astype(ml_dtypes.bfloat16).astype(np.float64), axis, -1)
    blocks = v.reshape(v.shape[:-1] + (-1, 32))
    amax = np.abs(blocks).max(-1, keepdims=True)
    byte = np.maximum(np.where(amax > 0, np.frexp(amax)[1] - 1 + 127, 0) - down, 1)
    scale = np.exp2(byte - 127.0)
    codes = (blocks / scale).astype(np.float32).astype(dtype).astype(np.float64)
    return np.moveaxis((codes * scale).reshape(v.shape), -1, axis)


WIDE = False


def mx_kscale(k):
    if not WIDE:
        return np.ones(k)
    levels = np.array([30, -30])
    if k % 512:
        return np.exp2(np.random.permutation(np.resize(levels, k // 32))).repeat(32)
    a = np.empty((k // 512, 16))
    for p in range(k // 512):
        a[p, :8] = np.random.permutation(np.resize(levels, 8))
        for g in range(8):
            far = levels[np.abs(levels - a[p, g]) >= 10]
            a[p, g + 8] = far[np.random.randint(len(far))]
    return np.exp2(a.ravel()).repeat(32)


BF16 = ml_dtypes.bfloat16


def bf(x):
    return np.asarray(x, np.float32).astype(BF16)


def f64(x):
    return np.asarray(x).astype(np.float64)


E2M1 = np.array([0.0, 0.5, 1.0, 1.5, 2.0, 3.0, 4.0, 6.0, -0.0, -0.5, -1.0, -1.5, -2.0, -3.0, -4.0, -6.0])


def pack_weight(w, fmt):
    k, n = w.shape
    w = f64(bf(w)).reshape(k // 32, 32, n)
    amax = np.abs(w).max(1)
    if fmt == "e4m3":
        byte = np.frexp(amax)[1] - 1 + 127 - 7
    else:
        mant, ex = np.frexp(amax / 6.0)
        byte = np.where(mant > 0.5, ex, ex - 1) + 127
    byte = np.clip(np.where(amax > 0, byte, 1), 1, 254)
    scaled = (w * np.exp2(127.0 - byte)[:, None, :]).reshape(k, n).astype(np.float32)
    by_word = np.ascontiguousarray(scaled.reshape(k // 512, 128, 4, n).transpose(0, 1, 3, 2))
    if fmt == "e4m3":
        words = by_word.astype(ml_dtypes.float8_e4m3fn).view(np.uint8)
    else:
        c = by_word.astype(ml_dtypes.float4_e2m1fn).view(np.uint8) & 0xF
        words = c[..., 0::2] | (c[..., 1::2] << 4)
    return np.ascontiguousarray(words), np.ascontiguousarray(byte.astype(np.uint8).reshape(k // 512, 16, n))


def unpack_weight(words, scales, fmt):
    g, p, n, _ = words.shape
    if fmt == "e4m3":
        vals = np.ascontiguousarray(words).view(ml_dtypes.float8_e4m3fn).astype(np.float64)
    else:
        nib = np.empty((g, p, n, 4), np.uint8)
        nib[..., 0::2] = words & 0xF
        nib[..., 1::2] = words >> 4
        vals = E2M1[nib]
    vals = vals * np.repeat(np.exp2(scales.astype(np.float64) - 127.0), 8, axis=1)[..., None]
    return vals.transpose(0, 1, 3, 2).reshape(g * 512, n)
def pack4(w):
    words, scales = pack_weight(w, "e2m1")
    return words.reshape(words.shape[0], 128, -1), scales


def unpack4(words, scales):
    return unpack_weight(words.reshape(words.shape[0], 128, -1, 2), scales, "e2m1")


K, B = 2048, 512


def setup_inputs():
    s = mx_kscale(K)
    operator = np.random.standard_normal((K, K)) / np.sqrt(K) / s[:, None] / s
    a_words, a_scales = pack4(operator)
    return {"dirs": bf(np.random.standard_normal((K, B)) * K ** -0.25 * s[:, None]),
            "a_words": a_words,
            "a_scales": a_scales,
            "pot": bf(0.5 * np.random.standard_normal(K) / (s * s)),
            "rho": bf(1 + 0.1 * np.random.standard_normal(B))}


def reference(dirs, a_words, a_scales, pot, rho):
    d = f64(dirs)
    r = f64(rho)
    dq = mxq(d, 0, "e4m3")
    a = unpack4(a_words, a_scales)
    applied = a.T @ dq
    w = applied + f64(pot)[:, None] * d
    h = dq.T @ mxq(w, 0, "e5m2")
    return h * r[:, None] * r

@@ -1,0 +1,290 @@
+from contextlib import ExitStack
+
+import concourse.mybir as mybir
+from concourse.masks import make_identity
+
+K, B = 2048, 512
+FLOPS = 2 * K * K * B + 2 * K * B * B
+
+F32 = mybir.dt.float32
+BF16 = mybir.dt.bfloat16
+U32 = mybir.dt.uint32
+I32 = mybir.dt.int32
+U8 = mybir.dt.uint8
+E4M3X4 = mybir.dt.float8_e4m3fn_x4
+E5M2X4 = mybir.dt.float8_e5m2_x4
+E2M1X4 = mybir.dt.float4_e2m1fn_x4
+MULT = mybir.AluOpType.mult
+ADD = mybir.AluOpType.add
+
+P = 128
+SLOTS = 4
+GROUPS = range(K // (P * SLOTS))
+RUN_GROUPS = GROUPS[1:]
+HALF = K // 2
+BANKS = 8
+EARLY_TILES = 6
+V_COLS_BY_PASS = (320, 192, 192, 192)
+V_COLS = 192
+
+
+def tile_scaled_block_projection_s9_kernel(tc, dirs, a_words, a_scales, pot, rho, out):
+    nc = tc.nc
+    with ExitStack() as ctx:
+        keep = ctx.enter_context(tc.tile_pool(name="keep", bufs=1))
+        psum = ctx.enter_context(tc.psum_pool(name="psum", bufs=1))
+        ctx.enter_context(tc.manual_schedule())
+
+        def sb(shape, dtype, name):
+            return keep.tile(shape, dtype, name=name, tag=name, align_bytes=64)
+
+        def bank(i, shape=(P, B), dtype=F32):
+            return psum.tile(list(shape), dtype, name="bank%d" % i, tag="bank%d" % i)
+
+        d_raw = [sb([P, SLOTS, B], BF16, "d_raw%d" % g) for g in GROUPS]
+        d_mix = [sb([P, B, SLOTS], BF16, "d_mix%d" % g) for g in GROUPS]
+        d_codes = [sb([P, B], U32, "d_codes%d" % g) for g in GROUPS]
+        d_scales = [sb([P, B], U8, "d_scales%d" % g) for g in GROUPS]
+        e_raw = d_raw[:1] + [sb([P, SLOTS, B], BF16, "e_raw%d" % j) for j in RUN_GROUPS]
+        e_mix = d_mix[:1] + [sb([P, B, SLOTS], BF16, "e_mix%d" % j) for j in RUN_GROUPS]
+        e_codes = d_codes[:1] + [sb([P, B], U32, "e_codes%d" % j) for j in RUN_GROUPS]
+        e_scales = d_scales[:1] + [sb([P, B], U8, "e_scales%d" % j) for j in RUN_GROUPS]
+        w_raw = [sb([P, SLOTS, B], BF16, "w_raw%d" % j) for j in GROUPS]
+        w_mix = [sb([P, B, SLOTS], BF16, "w_mix%d" % j) for j in GROUPS]
+        w_codes = [sb([P, B], U32, "w_codes%d" % j) for j in GROUPS]
+        w_scales = [sb([P, B], U8, "w_scales%d" % j) for j in GROUPS]
+        a_raw = [sb([P, 2 * K], U8, "a_raw%d" % g) for g in GROUPS]
+        a_moved = [[sb([P, 2 * B], U8, "a_moved%d_%d" % (g, j)) for j in (0, 1)] for g in GROUPS]
+        a_late = [sb([P, 2 * HALF], U8, "a_late%d" % g) for g in GROUPS]
+        s_raw = [sb([P, len(GROUPS), HALF], U8, "s_raw%d" % h) for h in (0, 1)]
+        s_moved = [sb([P, len(GROUPS), B], U8, "s_moved%d" % j) for j in (0, 1)]
+        s_late = sb([P, len(GROUPS), HALF], U8, "s_late")
+        rows = sb([P, K // len(GROUPS)], BF16, "rows")
+        rows_straight = sb([P, SLOTS, P], BF16, "rows_straight")
+        rows_runs = sb([P, SLOTS, P], BF16, "rows_runs")
+        ident = sb([P, P], BF16, "ident")
+        pot_straight = sb([P, SLOTS], F32, "pot_straight")
+        pot_runs = sb([P, SLOTS, len(GROUPS)], F32, "pot_runs")
+        rho_part = sb([P, B // P], F32, "rho_part")
+        rho_all = sb([P, B], BF16, "rho_all")
+
+
+        def load_a(g, half):
+            nc.sync.dma_start(
+                out=a_raw[g][:, 2 * HALF * half : 2 * HALF * (half + 1)].bitcast(I32),
+                in_=a_words[g][:, 2 * HALF * half : 2 * HALF * (half + 1)].bitcast(I32),
+            )
+
+        def load_a_scales(half):
+            for q in range(4):
+                nc.sync.dma_start(
+                    out=s_raw[half][32 * q : 32 * q + 4, :, :].bitcast(I32),
+                    in_=a_scales[:, 4 * q : 4 * q + 4, HALF * half : HALF * (half + 1)]
+                    .rearrange("g r n -> r g n")
+                    .bitcast(I32),
+                )
+
+        def load_d(g):
+            rows_of_d = dirs[512 * g : 512 * (g + 1), :]
+            nc.sync.dma_start(out=d_raw[g][:], in_=rows_of_d.rearrange("(p t) b -> p t b", t=SLOTS))
+
+        def load_e(j):
+            by_r = dirs[512 * j : 512 * (j + 1), :].rearrange("(s t r) b -> r s t b", t=SLOTS, r=4)
+            for r in range(4):
+                nc.sync.dma_start(out=e_raw[j][r:P:4, :, :], in_=by_r[r])
+
+        nc.vector.memset(rows[:], 0.0)
+        for half in (0, 1):
+            nc.vector.memset(s_raw[half][:].rearrange("p g n -> p (g n)").bitcast(I32), 0)
+        make_identity(nc, ident[:])
+
+        for g in GROUPS:
+            load_a(g, 0)
+            if g == 0:
+                nc.sync.dma_start(out=rows[0:4, :], in_=pot.rearrange("(j x) -> j x", x=512))
+                nc.sync.dma_start(out=rows[4:5, :], in_=rho.rearrange("(o x) -> o x", o=1))
+            load_d(g)
+            if g == 0:
+                load_a_scales(0)
+        load_e(1)
+        load_a(0, 1)
+        load_a_scales(1)
+        load_e(2)
+        for g in GROUPS[1:]:
+            load_a(g, 1)
+        load_e(3)
+        nc.sync.dma_start(out=rho_all[:], in_=rho.partition_broadcast(P))
+
+
+        nc.scalar.copy(out=rows_straight[:], in_=rows[:].rearrange("p (m t) -> p t m", t=SLOTS))
+        nc.scalar.copy(
+            out=rows_runs[:].rearrange("p t (s r) -> p t s r", r=4),
+            in_=rows[:].rearrange("p (s t r) -> p t s r", t=SLOTS, r=4),
+        )
+        turned_pot = bank(6, (P, 2, SLOTS, P), BF16)
+        turned_rho = bank(7, (P, B // P, P), BF16)
+        for t in range(SLOTS):
+            nc.tensor.transpose(turned_pot[:, 0, t, :], rows_straight[:, t, :], ident[:])
+            nc.tensor.transpose(turned_pot[:, 1, t, :], rows_runs[:, t, :], ident[:])
+        for m in range(B // P):
+            nc.tensor.transpose(turned_rho[:, m, :], rows[:, P * m : P * (m + 1)], ident[:])
+
+
+        def interleave(mix, raw, v_cols):
+            for copy, lo, hi in ((nc.vector.tensor_copy, 0, v_cols), (nc.scalar.copy, v_cols, B)):
+                if lo < hi:
+                    copy(
+                        out=mix[:, lo:hi, :].rearrange("p (c i) t -> p c t i", i=4),
+                        in_=raw[:, :, lo:hi].rearrange("p t (c i) -> p c t i", i=4),
+                    )
+
+        def quantize(codes, scales, mix, fmt):
+            nc.vector.quantize_mx(
+                out=codes[:].bitcast(fmt), scales=scales[:], in_=mix[:].rearrange("p b t -> p (b t)")
+            )
+
+        def move_words_straight(g):
+            nc.vector.tensor_copy(
+                out=a_moved[g][0][:].rearrange("p (t m e) -> p t m e", t=SLOTS, e=2),
+                in_=a_raw[g][:, 0 : 2 * B].rearrange("p (m t e) -> p t m e", t=SLOTS, e=2),
+            )
+
+        def move_scales_straight():
+            nc.vector.tensor_copy(
+                out=s_moved[0][:].rearrange("p g (t m) -> p g t m", t=SLOTS),
+                in_=s_raw[0][:, :, 0:B].rearrange("p g (m t) -> p g t m", t=SLOTS),
+            )
+
+        def move_words_runs(dst, src):
+            nc.vector.tensor_copy(
+                out=dst.bitcast(I32).rearrange("p (j t s e) -> p j t s e", t=SLOTS, s=P // 4, e=2),
+                in_=src.bitcast(I32).rearrange("p (j s t e) -> p j t s e", t=SLOTS, s=P // 4, e=2),
+            )
+
+        def move_scales_runs(dst, src):
+            nc.vector.tensor_copy(
+                out=dst.bitcast(I32).rearrange("p g (j t s) -> p g j t s", t=SLOTS, s=P // 4),
+                in_=src.bitcast(I32).rearrange("p g (j s t) -> p g j t s", t=SLOTS, s=P // 4),
+            )
+
+        def move_early_words(g):
+            move_words_straight(g)
+            move_words_runs(a_moved[g][1][:], a_raw[g][:, 2 * B : 4 * B])
+
+        def first_product(acc, i, g):
+            j, t = divmod(i, SLOTS)
+            if j < 2:
+                words, scales, c = a_moved[g][j], s_moved[j], P * t
+            else:
+                words, scales, c = a_late[g], s_late, P * (i - 2 * SLOTS)
+            nc.tensor.matmul_mx(
+                out=acc[:],
+                lhsT=words[:, 2 * c : 2 * (c + P)].bitcast(E2M1X4),
+                lhsT_scale=scales[:, g, c : c + P],
+                rhs=d_codes[g][:].bitcast(E4M3X4),
+                rhs_scale=d_scales[g][:],
+                start=(g == 0),
+                stop=(g == len(GROUPS) - 1),
+            )
+
+        def add_potential(acc, i):
+            j, t = divmod(i, SLOTS)
+            nc.vector.scalar_tensor_tensor(
+                out=w_raw[j][:, t, :],
+                in0=e_raw[j][:, t, :],
+                scalar=pot_straight[:, t : t + 1] if j == 0 else pot_runs[:, t, j : j + 1],
+                in1=acc[:],
+                op0=MULT,
+                op1=ADD,
+            )
+
+        def second_product(acc, m, j):
+            cols = slice(P * m, P * (m + 1))
+            nc.tensor.matmul_mx(
+                out=acc[:],
+                lhsT=e_codes[j][:, cols].bitcast(E4M3X4),
+                lhsT_scale=e_scales[j][:, cols],
+                rhs=w_codes[j][:].bitcast(E5M2X4),
+                rhs_scale=w_scales[j][:],
+                start=(j == 0),
+                stop=(j == len(GROUPS) - 1),
+            )
+
+        def finish(acc, m):
+            res = sb([P, B], F32, "res%d" % m)
+            nc.vector.scalar_tensor_tensor(
+                out=res[:], in0=acc[:], scalar=rho_part[:, m : m + 1], in1=rho_all[:], op0=MULT, op1=MULT
+            )
+            nc.sync.dma_start(out=out[P * m : P * (m + 1), :], in_=res[:])
+
+
+        acc = [bank(i) for i in range(EARLY_TILES)]
+        move_early_words(0)
+        for g in GROUPS:
+            interleave(d_mix[g], d_raw[g], V_COLS_BY_PASS[g])
+            if 0 < g < len(GROUPS) - 1:
+                move_early_words(g + 1)
+            if g == len(GROUPS) - 1:
+                move_words_runs(a_late[0][:], a_raw[0][:, 2 * HALF :])
+            quantize(d_codes[g], d_scales[g], d_mix[g], E4M3X4)
+            if g == 0:
+                move_scales_straight()
+                move_scales_runs(s_moved[1][:], s_raw[0][:, :, B:])
+                move_early_words(1)
+            for i in range(EARLY_TILES):
+                first_product(acc[i], i, g)
+        nc.scalar.copy(out=pot_straight[:], in_=turned_pot[:, 0, :, 0])
+        nc.scalar.copy(out=pot_runs[:], in_=turned_pot[:, 1, :, 0 : len(GROUPS)])
+        nc.scalar.copy(out=rho_part[:], in_=turned_rho[:, :, 4])
+        for i in range(EARLY_TILES, BANKS):
+            acc.append(bank(i))
+            for g in GROUPS:
+                first_product(acc[i], i, g)
+
+
+        interleave(e_mix[1], e_raw[1], 0)
+        interleave(e_mix[2], e_raw[2], 0)
+        for i in range(SLOTS):
+            add_potential(acc[i], i)
+        interleave(w_mix[0], w_raw[0], 0)
+        move_scales_runs(s_late[:], s_raw[1][:])
+        for g in GROUPS[1:]:
+            move_words_runs(a_late[g][:], a_raw[g][:, 2 * HALF :])
+            add_potential(acc[SLOTS + g - 1], SLOTS + g - 1)
+        add_potential(acc[7], 7)
+
+
+        acc += [bank(i - BANKS) for i in range(8, 12)]
+        for g in GROUPS:
+            for i in range(8, 12):
+                first_product(acc[i], i, g)
+        interleave(e_mix[3], e_raw[3], 0)
+        interleave(w_mix[1], w_raw[1], 0)
+        quantize(w_codes[0], w_scales[0], w_mix[0], E5M2X4)
+        quantize(e_codes[1], e_scales[1], e_mix[1], E4M3X4)
+        for i in range(12, 16):
+            acc.append(bank(i - BANKS))
+            for g in GROUPS:
+                first_product(acc[i], i, g)
+        for i in range(8, 12):
+            add_potential(acc[i], i)
+        interleave(w_mix[2], w_raw[2], 0)
+        quantize(e_codes[2], e_scales[2], e_mix[2], E4M3X4)
+        h_acc = [bank(m) for m in range(4)]
+        for m in range(4):
+            second_product(h_acc[m], m, 0)
+        for i in range(12, 16):
+            add_potential(acc[i], i)
+        quantize(w_codes[1], w_scales[1], w_mix[1], E5M2X4)
+        for m in range(4):
+            second_product(h_acc[m], m, 1)
+        interleave(w_mix[3], w_raw[3], V_COLS)
+        quantize(w_codes[2], w_scales[2], w_mix[2], E5M2X4)
+        quantize(e_codes[3], e_scales[3], e_mix[3], E4M3X4)
+        for m in range(4):
+            second_product(h_acc[m], m, 2)
+        quantize(w_codes[3], w_scales[3], w_mix[3], E5M2X4)
+        for m in range(4):
+            second_product(h_acc[m], m, 3)
+        for m in range(4):
+            finish(h_acc[m], m)

@@ -9,6 +9,7 @@ FLOPS = 2 * K * K * B + 2 * K * B * B
 F32 = mybir.dt.float32
 BF16 = mybir.dt.bfloat16
 U32 = mybir.dt.uint32
+U16 = mybir.dt.uint16
 I32 = mybir.dt.int32
 U8 = mybir.dt.uint8
 E4M3X4 = mybir.dt.float8_e4m3fn_x4
@@ -19,13 +20,11 @@ ADD = mybir.AluOpType.add
 
 P = 128
 SLOTS = 4
-GROUPS = range(K // (P * SLOTS))
-RUN_GROUPS = GROUPS[1:]
+G = P * SLOTS
+GROUPS = range(K // G)
+LAST = len(GROUPS) - 1
 HALF = K // 2
-BANKS = 8
-EARLY_TILES = 6
-V_COLS_BY_PASS = (320, 192, 192, 192)
-V_COLS = 192
+V_COLS = 320
 
 
 def tile_scaled_block_projection_s9_kernel(tc, dirs, a_words, a_scales, pot, rho, out):
@@ -45,37 +44,23 @@ def tile_scaled_block_projection_s9_kernel(tc, dirs, a_words, a_scales, pot, rho
         d_mix = [sb([P, B, SLOTS], BF16, "d_mix%d" % g) for g in GROUPS]
         d_codes = [sb([P, B], U32, "d_codes%d" % g) for g in GROUPS]
         d_scales = [sb([P, B], U8, "d_scales%d" % g) for g in GROUPS]
-        e_raw = d_raw[:1] + [sb([P, SLOTS, B], BF16, "e_raw%d" % j) for j in RUN_GROUPS]
-        e_mix = d_mix[:1] + [sb([P, B, SLOTS], BF16, "e_mix%d" % j) for j in RUN_GROUPS]
-        e_codes = d_codes[:1] + [sb([P, B], U32, "e_codes%d" % j) for j in RUN_GROUPS]
-        e_scales = d_scales[:1] + [sb([P, B], U8, "e_scales%d" % j) for j in RUN_GROUPS]
+        d_nat = {j: sb([P, SLOTS, B], BF16, "d_nat%d" % j) for j in GROUPS[:LAST]}
+        w_nat = {j: [sb([P, B], BF16, "w_nat%d_%d" % (j, u)) for u in range(SLOTS)] for j in GROUPS[:LAST]}
         w_raw = [sb([P, SLOTS, B], BF16, "w_raw%d" % j) for j in GROUPS]
         w_mix = [sb([P, B, SLOTS], BF16, "w_mix%d" % j) for j in GROUPS]
         w_codes = [sb([P, B], U32, "w_codes%d" % j) for j in GROUPS]
         w_scales = [sb([P, B], U8, "w_scales%d" % j) for j in GROUPS]
-        a_raw = [sb([P, 2 * K], U8, "a_raw%d" % g) for g in GROUPS]
-        a_moved = [[sb([P, 2 * B], U8, "a_moved%d_%d" % (g, j)) for j in (0, 1)] for g in GROUPS]
-        a_late = [sb([P, 2 * HALF], U8, "a_late%d" % g) for g in GROUPS]
+        a_early = [sb([P, 2 * HALF], U8, "a_early%d" % g) for g in GROUPS]
+        a_late = [sb([P, len(GROUPS), 2 * G], U8, "a_late%d" % j) for j in (0, 1)]
+        a_moved = sb([P, len(GROUPS), 2 * G], U8, "a_moved")
         s_raw = [sb([P, len(GROUPS), HALF], U8, "s_raw%d" % h) for h in (0, 1)]
-        s_moved = [sb([P, len(GROUPS), B], U8, "s_moved%d" % j) for j in (0, 1)]
-        s_late = sb([P, len(GROUPS), HALF], U8, "s_late")
-        rows = sb([P, K // len(GROUPS)], BF16, "rows")
-        rows_straight = sb([P, SLOTS, P], BF16, "rows_straight")
-        rows_runs = sb([P, SLOTS, P], BF16, "rows_runs")
+        s_moved = sb([P, len(GROUPS), G], U8, "s_moved")
+        rows = sb([P, G], BF16, "rows")
         ident = sb([P, P], BF16, "ident")
-        pot_straight = sb([P, SLOTS], F32, "pot_straight")
-        pot_runs = sb([P, SLOTS, len(GROUPS)], F32, "pot_runs")
-        rho_part = sb([P, B // P], F32, "rho_part")
+        cols = sb([P, 2, SLOTS, len(GROUPS) + 1], F32, "cols")
         rho_all = sb([P, B], BF16, "rho_all")
 
-
-        def load_a(g, half):
-            nc.sync.dma_start(
-                out=a_raw[g][:, 2 * HALF * half : 2 * HALF * (half + 1)].bitcast(I32),
-                in_=a_words[g][:, 2 * HALF * half : 2 * HALF * (half + 1)].bitcast(I32),
-            )
-
-        def load_a_scales(half):
+        def load_scales(half):
             for q in range(4):
                 nc.sync.dma_start(
                     out=s_raw[half][32 * q : 32 * q + 4, :, :].bitcast(I32),
@@ -84,207 +69,181 @@ def tile_scaled_block_projection_s9_kernel(tc, dirs, a_words, a_scales, pot, rho
                     .bitcast(I32),
                 )
 
+        def load_a_early(g):
+            nc.sync.dma_start(out=a_early[g][:].bitcast(I32), in_=a_words[g][:, 0 : 2 * HALF].bitcast(I32))
+
+        def load_a_late(j):
+            lo = 2 * G * j
+            nc.sync.dma_start(
+                out=a_late[j - 2][:].bitcast(I32),
+                in_=a_words[:, :, lo : lo + 2 * G].rearrange("g p n -> p g n").bitcast(I32),
+            )
+
         def load_d(g):
-            rows_of_d = dirs[512 * g : 512 * (g + 1), :]
-            nc.sync.dma_start(out=d_raw[g][:], in_=rows_of_d.rearrange("(p t) b -> p t b", t=SLOTS))
+            nc.sync.dma_start(out=d_raw[g][:], in_=dirs[G * g : G * (g + 1), :].rearrange("(p t) b -> p t b", t=SLOTS))
 
-        def load_e(j):
-            by_r = dirs[512 * j : 512 * (j + 1), :].rearrange("(s t r) b -> r s t b", t=SLOTS, r=4)
-            for r in range(4):
-                nc.sync.dma_start(out=e_raw[j][r:P:4, :, :], in_=by_r[r])
+        def load_d_nat(j):
+            nc.sync.dma_start(out=d_nat[j][:], in_=dirs[G * j : G * (j + 1), :].rearrange("(u p) b -> p u b", p=P))
 
-        nc.vector.memset(rows[:], 0.0)
+        nc.gpsimd.memset(rows[:], 0.0)
         for half in (0, 1):
             nc.vector.memset(s_raw[half][:].rearrange("p g n -> p (g n)").bitcast(I32), 0)
         make_identity(nc, ident[:])
 
+        nc.scalar.dma_start(out=rows[0:4, :], in_=pot.rearrange("(j x) -> j x", x=G))
+        nc.scalar.dma_start(out=rows[4:5, :], in_=rho.rearrange("(o x) -> o x", o=1))
         for g in GROUPS:
-            load_a(g, 0)
-            if g == 0:
-                nc.sync.dma_start(out=rows[0:4, :], in_=pot.rearrange("(j x) -> j x", x=512))
-                nc.sync.dma_start(out=rows[4:5, :], in_=rho.rearrange("(o x) -> o x", o=1))
             load_d(g)
+            load_a_early(g)
             if g == 0:
-                load_a_scales(0)
-        load_e(1)
-        load_a(0, 1)
-        load_a_scales(1)
-        load_e(2)
-        for g in GROUPS[1:]:
-            load_a(g, 1)
-        load_e(3)
+                load_scales(0)
+            if g == 1:
+                load_a_late(3)
+                load_scales(1)
+        load_d_nat(0)
+        load_d_nat(1)
+        load_a_late(2)
+        load_d_nat(2)
         nc.sync.dma_start(out=rho_all[:], in_=rho.partition_broadcast(P))
 
+        turned = bank(7, (P, 2, SLOTS, P), BF16)
+        for u in range(SLOTS):
+            nc.tensor.transpose(turned[:, 0, u, :], rows[:, P * u : P * (u + 1)], ident[:])
+            nc.tensor.transpose(turned[:, 1, u, :], rows[:, u:G:SLOTS], ident[:])
 
-        nc.scalar.copy(out=rows_straight[:], in_=rows[:].rearrange("p (m t) -> p t m", t=SLOTS))
-        nc.scalar.copy(
-            out=rows_runs[:].rearrange("p t (s r) -> p t s r", r=4),
-            in_=rows[:].rearrange("p (s t r) -> p t s r", t=SLOTS, r=4),
-        )
-        turned_pot = bank(6, (P, 2, SLOTS, P), BF16)
-        turned_rho = bank(7, (P, B // P, P), BF16)
-        for t in range(SLOTS):
-            nc.tensor.transpose(turned_pot[:, 0, t, :], rows_straight[:, t, :], ident[:])
-            nc.tensor.transpose(turned_pot[:, 1, t, :], rows_runs[:, t, :], ident[:])
-        for m in range(B // P):
-            nc.tensor.transpose(turned_rho[:, m, :], rows[:, P * m : P * (m + 1)], ident[:])
+        def interleave(copy, mix, raw, lo, hi):
+            copy(
+                out=mix[:, lo:hi, :].rearrange("p (c i) t -> p c t i", i=4),
+                in_=raw[:, :, lo:hi].rearrange("p t (c i) -> p c t i", i=4),
+            )
 
-
-        def interleave(mix, raw, v_cols):
-            for copy, lo, hi in ((nc.vector.tensor_copy, 0, v_cols), (nc.scalar.copy, v_cols, B)):
-                if lo < hi:
-                    copy(
-                        out=mix[:, lo:hi, :].rearrange("p (c i) t -> p c t i", i=4),
-                        in_=raw[:, :, lo:hi].rearrange("p t (c i) -> p c t i", i=4),
-                    )
+        def interleave_shared(mix, raw, v_cols):
+            interleave(nc.vector.tensor_copy, mix, raw, 0, v_cols)
+            interleave(nc.scalar.copy, mix, raw, v_cols, B)
 
         def quantize(codes, scales, mix, fmt):
             nc.vector.quantize_mx(
                 out=codes[:].bitcast(fmt), scales=scales[:], in_=mix[:].rearrange("p b t -> p (b t)")
             )
 
-        def move_words_straight(g):
+        def loaded(j, g):
+            if j < 2:
+                words = a_early[g][:, 2 * G * j : 2 * G * (j + 1)]
+            else:
+                words = a_late[j - 2][:, g, :]
+            return words, s_raw[j // 2][:, g, G * (j % 2) : G * (j % 2 + 1)]
+
+        def move_words(lo, hi):
             nc.vector.tensor_copy(
-                out=a_moved[g][0][:].rearrange("p (t m e) -> p t m e", t=SLOTS, e=2),
-                in_=a_raw[g][:, 0 : 2 * B].rearrange("p (m t e) -> p t m e", t=SLOTS, e=2),
+                out=a_moved[:, lo:hi, :].bitcast(U16).rearrange("p g (t m) -> p g t m", t=SLOTS),
+                in_=a_late[1][:, lo:hi, :].bitcast(U16).rearrange("p g (m t) -> p g t m", t=SLOTS),
             )
 
-        def move_scales_straight():
+        def move_scales(lo, hi):
             nc.vector.tensor_copy(
-                out=s_moved[0][:].rearrange("p g (t m) -> p g t m", t=SLOTS),
-                in_=s_raw[0][:, :, 0:B].rearrange("p g (m t) -> p g t m", t=SLOTS),
+                out=s_moved[:, lo:hi, :].rearrange("p g (t m) -> p g t m", t=SLOTS),
+                in_=s_raw[1][:, lo:hi, G:].rearrange("p g (m t) -> p g t m", t=SLOTS),
             )
-
-        def move_words_runs(dst, src):
-            nc.vector.tensor_copy(
-                out=dst.bitcast(I32).rearrange("p (j t s e) -> p j t s e", t=SLOTS, s=P // 4, e=2),
-                in_=src.bitcast(I32).rearrange("p (j s t e) -> p j t s e", t=SLOTS, s=P // 4, e=2),
-            )
-
-        def move_scales_runs(dst, src):
-            nc.vector.tensor_copy(
-                out=dst.bitcast(I32).rearrange("p g (j t s) -> p g j t s", t=SLOTS, s=P // 4),
-                in_=src.bitcast(I32).rearrange("p g (j s t) -> p g j t s", t=SLOTS, s=P // 4),
-            )
-
-        def move_early_words(g):
-            move_words_straight(g)
-            move_words_runs(a_moved[g][1][:], a_raw[g][:, 2 * B : 4 * B])
 
         def first_product(acc, i, g):
-            j, t = divmod(i, SLOTS)
-            if j < 2:
-                words, scales, c = a_moved[g][j], s_moved[j], P * t
-            else:
-                words, scales, c = a_late[g], s_late, P * (i - 2 * SLOTS)
+            j, u = divmod(i, SLOTS)
+            words, scales = loaded(j, g) if j < LAST else (a_moved[:, g, :], s_moved[:, g, :])
+            c = P * u
             nc.tensor.matmul_mx(
                 out=acc[:],
                 lhsT=words[:, 2 * c : 2 * (c + P)].bitcast(E2M1X4),
-                lhsT_scale=scales[:, g, c : c + P],
+                lhsT_scale=scales[:, c : c + P],
                 rhs=d_codes[g][:].bitcast(E4M3X4),
                 rhs_scale=d_scales[g][:],
                 start=(g == 0),
-                stop=(g == len(GROUPS) - 1),
+                stop=(g == LAST),
             )
 
         def add_potential(acc, i):
-            j, t = divmod(i, SLOTS)
+            j, u = divmod(i, SLOTS)
+            if j < LAST:
+                dst, src, order = w_nat[j][u][:], d_nat[j][:, u, :], 0
+            else:
+                dst, src, order = w_raw[j][:, u, :], d_raw[j][:, u, :], 1
             nc.vector.scalar_tensor_tensor(
-                out=w_raw[j][:, t, :],
-                in0=e_raw[j][:, t, :],
-                scalar=pot_straight[:, t : t + 1] if j == 0 else pot_runs[:, t, j : j + 1],
-                in1=acc[:],
-                op0=MULT,
-                op1=ADD,
+                out=dst, in0=src, scalar=cols[:, order, u, j : j + 1], in1=acc[:], op0=MULT, op1=ADD
             )
 
+        def regroup(j, u):
+            nc.sync.dma_start(out=w_raw[j][32 * u : 32 * (u + 1), :, :], in_=w_nat[j][u][:])
+
         def second_product(acc, m, j):
-            cols = slice(P * m, P * (m + 1))
+            sl = slice(P * m, P * (m + 1))
             nc.tensor.matmul_mx(
                 out=acc[:],
-                lhsT=e_codes[j][:, cols].bitcast(E4M3X4),
-                lhsT_scale=e_scales[j][:, cols],
+                lhsT=d_codes[j][:, sl].bitcast(E4M3X4),
+                lhsT_scale=d_scales[j][:, sl],
                 rhs=w_codes[j][:].bitcast(E5M2X4),
                 rhs_scale=w_scales[j][:],
                 start=(j == 0),
-                stop=(j == len(GROUPS) - 1),
+                stop=(j == LAST),
             )
 
         def finish(acc, m):
             res = sb([P, B], F32, "res%d" % m)
             nc.vector.scalar_tensor_tensor(
-                out=res[:], in0=acc[:], scalar=rho_part[:, m : m + 1], in1=rho_all[:], op0=MULT, op1=MULT
+                out=res[:], in0=acc[:], scalar=cols[:, 0, m, 4:5], in1=rho_all[:], op0=MULT, op1=MULT
             )
             nc.sync.dma_start(out=out[P * m : P * (m + 1), :], in_=res[:])
 
+        def quantize_w(j):
+            quantize(w_codes[j], w_scales[j], w_mix[j], E5M2X4)
 
-        acc = [bank(i) for i in range(EARLY_TILES)]
-        move_early_words(0)
+        acc = {}
+
+        def whole_tile(i):
+            acc[i] = bank(i % 8)
+            for g in GROUPS:
+                first_product(acc[i], i, g)
+
+        def drain(i):
+            add_potential(acc[i], i)
+            if i // SLOTS < LAST:
+                regroup(i // SLOTS, i % SLOTS)
+
         for g in GROUPS:
-            interleave(d_mix[g], d_raw[g], V_COLS_BY_PASS[g])
-            if 0 < g < len(GROUPS) - 1:
-                move_early_words(g + 1)
-            if g == len(GROUPS) - 1:
-                move_words_runs(a_late[0][:], a_raw[0][:, 2 * HALF :])
-            quantize(d_codes[g], d_scales[g], d_mix[g], E4M3X4)
+            interleave_shared(d_mix[g], d_raw[g], V_COLS if g < 2 else B // 2)
             if g == 0:
-                move_scales_straight()
-                move_scales_runs(s_moved[1][:], s_raw[0][:, :, B:])
-                move_early_words(1)
-            for i in range(EARLY_TILES):
+                nc.scalar.copy(out=cols[:], in_=turned[:, :, :, 0 : len(GROUPS) + 1])
+                for i in range(8):
+                    acc[i] = bank(i)
+            if g >= 2:
+                move_words(2 * (g - 2), 2 * (g - 1))
+            quantize(d_codes[g], d_scales[g], d_mix[g], E4M3X4)
+            if g >= 2:
+                move_scales(2 * (g - 2), 2 * (g - 1))
+            for i in range(8) if g < 2 else range(4):
                 first_product(acc[i], i, g)
-        nc.scalar.copy(out=pot_straight[:], in_=turned_pot[:, 0, :, 0])
-        nc.scalar.copy(out=pot_runs[:], in_=turned_pot[:, 1, :, 0 : len(GROUPS)])
-        nc.scalar.copy(out=rho_part[:], in_=turned_rho[:, :, 4])
-        for i in range(EARLY_TILES, BANKS):
-            acc.append(bank(i))
-            for g in GROUPS:
-                first_product(acc[i], i, g)
-
-
-        interleave(e_mix[1], e_raw[1], 0)
-        interleave(e_mix[2], e_raw[2], 0)
-        for i in range(SLOTS):
-            add_potential(acc[i], i)
-        interleave(w_mix[0], w_raw[0], 0)
-        move_scales_runs(s_late[:], s_raw[1][:])
-        for g in GROUPS[1:]:
-            move_words_runs(a_late[g][:], a_raw[g][:, 2 * HALF :])
-            add_potential(acc[SLOTS + g - 1], SLOTS + g - 1)
-        add_potential(acc[7], 7)
-
-
-        acc += [bank(i - BANKS) for i in range(8, 12)]
-        for g in GROUPS:
-            for i in range(8, 12):
-                first_product(acc[i], i, g)
-        interleave(e_mix[3], e_raw[3], 0)
-        interleave(w_mix[1], w_raw[1], 0)
-        quantize(w_codes[0], w_scales[0], w_mix[0], E5M2X4)
-        quantize(e_codes[1], e_scales[1], e_mix[1], E4M3X4)
-        for i in range(12, 16):
-            acc.append(bank(i - BANKS))
-            for g in GROUPS:
-                first_product(acc[i], i, g)
-        for i in range(8, 12):
-            add_potential(acc[i], i)
-        interleave(w_mix[2], w_raw[2], 0)
-        quantize(e_codes[2], e_scales[2], e_mix[2], E4M3X4)
+        for i in range(4, 8):
+            first_product(acc[i], i, 2)
+            first_product(acc[i], i, 3)
+        for i in range(8):
+            drain(i)
+        interleave(nc.scalar.copy, w_mix[0], w_raw[0], 0, B)
+        interleave(nc.scalar.copy, w_mix[1], w_raw[1], 0, B)
+        for i in range(8, 15):
+            whole_tile(i)
+            if i == 12:
+                quantize_w(0)
+            if i == 14:
+                quantize_w(1)
+            drain(i)
+        whole_tile(15)
+        interleave_shared(w_mix[2], w_raw[2], B // 2)
+        drain(15)
         h_acc = [bank(m) for m in range(4)]
-        for m in range(4):
-            second_product(h_acc[m], m, 0)
-        for i in range(12, 16):
-            add_potential(acc[i], i)
-        quantize(w_codes[1], w_scales[1], w_mix[1], E5M2X4)
-        for m in range(4):
-            second_product(h_acc[m], m, 1)
-        interleave(w_mix[3], w_raw[3], V_COLS)
-        quantize(w_codes[2], w_scales[2], w_mix[2], E5M2X4)
-        quantize(e_codes[3], e_scales[3], e_mix[3], E4M3X4)
+        for j in (0, 1):
+            for m in range(4):
+                second_product(h_acc[m], m, j)
+        quantize_w(2)
+        interleave_shared(w_mix[3], w_raw[3], V_COLS)
+        quantize_w(3)
         for m in range(4):
             second_product(h_acc[m], m, 2)
-        quantize(w_codes[3], w_scales[3], w_mix[3], E5M2X4)
-        for m in range(4):
             second_product(h_acc[m], m, 3)
-        for m in range(4):
             finish(h_acc[m], m)

@@ -1,7 +1,6 @@
 from contextlib import ExitStack
 
 import concourse.mybir as mybir
-from concourse.masks import make_identity
 
 K, B = 2048, 512
 FLOPS = 2 * K * K * B + 2 * K * B * B
@@ -19,11 +18,14 @@ MULT = mybir.AluOpType.mult
 ADD = mybir.AluOpType.add
 
 P = 128
+QUAD = 32
 SLOTS = 4
 G = P * SLOTS
 GROUPS = range(K // G)
 LAST = len(GROUPS) - 1
 HALF = K // 2
+MOVED = (1, 3)
+UNMOVED = (0, 2)
 V_COLS = 320
 
 
@@ -37,46 +39,45 @@ def tile_scaled_block_projection_s9_kernel(tc, dirs, a_words, a_scales, pot, rho
         def sb(shape, dtype, name):
             return keep.tile(shape, dtype, name=name, tag=name, align_bytes=64)
 
-        def bank(i, shape=(P, B), dtype=F32):
-            return psum.tile(list(shape), dtype, name="bank%d" % i, tag="bank%d" % i)
+        def bank(i):
+            return psum.tile([P, B], F32, name="bank%d" % i, tag="bank%d" % i)
 
         d_raw = [sb([P, SLOTS, B], BF16, "d_raw%d" % g) for g in GROUPS]
         d_mix = [sb([P, B, SLOTS], BF16, "d_mix%d" % g) for g in GROUPS]
         d_codes = [sb([P, B], U32, "d_codes%d" % g) for g in GROUPS]
         d_scales = [sb([P, B], U8, "d_scales%d" % g) for g in GROUPS]
-        d_nat = {j: sb([P, SLOTS, B], BF16, "d_nat%d" % j) for j in GROUPS[:LAST]}
-        w_nat = {j: [sb([P, B], BF16, "w_nat%d_%d" % (j, u)) for u in range(SLOTS)] for j in GROUPS[:LAST]}
+        d_nat = {j: sb([P, SLOTS, B], BF16, "d_nat%d" % j) for j in UNMOVED}
+        w_nat = {j: [sb([P, B], BF16, "w_nat%d_%d" % (j, u)) for u in range(SLOTS)] for j in UNMOVED}
         w_raw = [sb([P, SLOTS, B], BF16, "w_raw%d" % j) for j in GROUPS]
         w_mix = [sb([P, B, SLOTS], BF16, "w_mix%d" % j) for j in GROUPS]
         w_codes = [sb([P, B], U32, "w_codes%d" % j) for j in GROUPS]
         w_scales = [sb([P, B], U8, "w_scales%d" % j) for j in GROUPS]
         a_early = [sb([P, 2 * HALF], U8, "a_early%d" % g) for g in GROUPS]
-        a_late = [sb([P, len(GROUPS), 2 * G], U8, "a_late%d" % j) for j in (0, 1)]
-        a_moved = sb([P, len(GROUPS), 2 * G], U8, "a_moved")
+        a_late = [sb([P, 2, 2 * HALF], U8, "a_late%d" % x) for x in (0, 1)]
+        a_moved = {j: sb([P, len(GROUPS), 2 * G], U8, "a_moved%d" % j) for j in MOVED}
         s_raw = [sb([P, len(GROUPS), HALF], U8, "s_raw%d" % h) for h in (0, 1)]
-        s_moved = sb([P, len(GROUPS), G], U8, "s_moved")
-        rows = sb([P, G], BF16, "rows")
-        ident = sb([P, P], BF16, "ident")
-        cols = sb([P, 2, SLOTS, len(GROUPS) + 1], F32, "cols")
+        s_moved = {j: sb([P, len(GROUPS), G], U8, "s_moved%d" % j) for j in MOVED}
+        nat_rows = sb([P, QUAD], BF16, "nat_rows")
+        nat_cols = sb([P, QUAD], BF16, "nat_cols")
+        seg_rows = sb([P, P], BF16, "seg_rows")
+        seg_slots = sb([P, SLOTS, QUAD], BF16, "seg_slots")
+        seg_cols = sb([P, SLOTS, QUAD], BF16, "seg_cols")
         rho_all = sb([P, B], BF16, "rho_all")
 
         def load_scales(half):
-            for q in range(4):
+            for r in range(4):
                 nc.sync.dma_start(
-                    out=s_raw[half][32 * q : 32 * q + 4, :, :].bitcast(I32),
-                    in_=a_scales[:, 4 * q : 4 * q + 4, HALF * half : HALF * (half + 1)]
-                    .rearrange("g r n -> r g n")
-                    .bitcast(I32),
+                    out=s_raw[half][r:P:QUAD, :, :].bitcast(I32),
+                    in_=a_scales[:, r:16:4, HALF * half : HALF * (half + 1)].rearrange("g q n -> q g n").bitcast(I32),
                 )
 
         def load_a_early(g):
             nc.sync.dma_start(out=a_early[g][:].bitcast(I32), in_=a_words[g][:, 0 : 2 * HALF].bitcast(I32))
 
-        def load_a_late(j):
-            lo = 2 * G * j
+        def load_a_late(x):
             nc.sync.dma_start(
-                out=a_late[j - 2][:].bitcast(I32),
-                in_=a_words[:, :, lo : lo + 2 * G].rearrange("g p n -> p g n").bitcast(I32),
+                out=a_late[x][:].bitcast(I32),
+                in_=a_words[2 * x : 2 * x + 2, :, 2 * HALF :].rearrange("g p n -> p g n").bitcast(I32),
             )
 
         def load_d(g):
@@ -85,31 +86,20 @@ def tile_scaled_block_projection_s9_kernel(tc, dirs, a_words, a_scales, pot, rho
         def load_d_nat(j):
             nc.sync.dma_start(out=d_nat[j][:], in_=dirs[G * j : G * (j + 1), :].rearrange("(u p) b -> p u b", p=P))
 
-        nc.gpsimd.memset(rows[:], 0.0)
-        for half in (0, 1):
-            nc.vector.memset(s_raw[half][:].rearrange("p g n -> p (g n)").bitcast(I32), 0)
-        make_identity(nc, ident[:])
+        def load_tables():
+            nc.sync.dma_start(out=seg_rows[0:P:8, :], in_=pot.rearrange("(j q x) -> q j x", q=4, x=P))
+            nc.sync.dma_start(out=nat_rows[0:P:2, :], in_=pot.rearrange("(i q c) -> q i c", q=4, c=QUAD))
+            nc.sync.dma_start(out=nat_rows[1:P:8, :], in_=rho.rearrange("(m q c) -> q m c", q=4, c=QUAD))
 
-        nc.scalar.dma_start(out=rows[0:4, :], in_=pot.rearrange("(j x) -> j x", x=G))
-        nc.scalar.dma_start(out=rows[4:5, :], in_=rho.rearrange("(o x) -> o x", o=1))
-        for g in GROUPS:
-            load_d(g)
-            load_a_early(g)
-            if g == 0:
-                load_scales(0)
-            if g == 1:
-                load_a_late(3)
-                load_scales(1)
-        load_d_nat(0)
-        load_d_nat(1)
-        load_a_late(2)
-        load_d_nat(2)
-        nc.sync.dma_start(out=rho_all[:], in_=rho.partition_broadcast(P))
+        def turn_tables():
+            nc.scalar.copy(out=seg_slots[:], in_=seg_rows[:].rearrange("p (c t) -> p t c", t=SLOTS))
+            nc.vector.transpose(out=nat_cols[:], in_=nat_rows[:])
+            nc.vector.transpose(
+                out=seg_cols[:].rearrange("p t k -> p (t k)"), in_=seg_slots[:].rearrange("p t c -> p (t c)")
+            )
 
-        turned = bank(7, (P, 2, SLOTS, P), BF16)
-        for u in range(SLOTS):
-            nc.tensor.transpose(turned[:, 0, u, :], rows[:, P * u : P * (u + 1)], ident[:])
-            nc.tensor.transpose(turned[:, 1, u, :], rows[:, u:G:SLOTS], ident[:])
+        def zero(tile):
+            nc.vector.memset(tile.bitcast(I32), 0)
 
         def interleave(copy, mix, raw, lo, hi):
             copy(
@@ -126,28 +116,38 @@ def tile_scaled_block_projection_s9_kernel(tc, dirs, a_words, a_scales, pot, rho
                 out=codes[:].bitcast(fmt), scales=scales[:], in_=mix[:].rearrange("p b t -> p (b t)")
             )
 
-        def loaded(j, g):
-            if j < 2:
-                words = a_early[g][:, 2 * G * j : 2 * G * (j + 1)]
-            else:
-                words = a_late[j - 2][:, g, :]
-            return words, s_raw[j // 2][:, g, G * (j % 2) : G * (j % 2 + 1)]
+        def loaded_words(j, g):
+            half = a_early[g][:] if j < 2 else a_late[g // 2][:, g % 2, :]
+            return half[:, 2 * G * (j % 2) : 2 * G * (j % 2 + 1)]
 
-        def move_words(lo, hi):
+        def loaded_scales(j):
+            return s_raw[j // 2][:, :, G * (j % 2) : G * (j % 2 + 1)]
+
+        def move_words(j, g):
             nc.vector.tensor_copy(
-                out=a_moved[:, lo:hi, :].bitcast(U16).rearrange("p g (t m) -> p g t m", t=SLOTS),
-                in_=a_late[1][:, lo:hi, :].bitcast(U16).rearrange("p g (m t) -> p g t m", t=SLOTS),
+                out=a_moved[j][:, g, :].bitcast(U16).rearrange("p (t m) -> p t m", t=SLOTS),
+                in_=loaded_words(j, g).bitcast(U16).rearrange("p (m t) -> p t m", t=SLOTS),
             )
 
-        def move_scales(lo, hi):
+        def move_late_words(j, x):
+            cols = slice(2 * G * (j % 2), 2 * G * (j % 2 + 1))
             nc.vector.tensor_copy(
-                out=s_moved[:, lo:hi, :].rearrange("p g (t m) -> p g t m", t=SLOTS),
-                in_=s_raw[1][:, lo:hi, G:].rearrange("p g (m t) -> p g t m", t=SLOTS),
+                out=a_moved[j][:, 2 * x : 2 * x + 2, :].bitcast(U16).rearrange("p g (t m) -> p g t m", t=SLOTS),
+                in_=a_late[x][:, :, cols].bitcast(U16).rearrange("p g (m t) -> p g t m", t=SLOTS),
+            )
+
+        def move_scales(j, lo, hi):
+            nc.vector.tensor_copy(
+                out=s_moved[j][:, lo:hi, :].rearrange("p g (t m) -> p g t m", t=SLOTS),
+                in_=loaded_scales(j)[:, lo:hi, :].rearrange("p g (m t) -> p g t m", t=SLOTS),
             )
 
         def first_product(acc, i, g):
             j, u = divmod(i, SLOTS)
-            words, scales = loaded(j, g) if j < LAST else (a_moved[:, g, :], s_moved[:, g, :])
+            if j in MOVED:
+                words, scales = a_moved[j][:, g, :], s_moved[j][:, g, :]
+            else:
+                words, scales = loaded_words(j, g), loaded_scales(j)[:, g, :]
             c = P * u
             nc.tensor.matmul_mx(
                 out=acc[:],
@@ -159,20 +159,17 @@ def tile_scaled_block_projection_s9_kernel(tc, dirs, a_words, a_scales, pot, rho
                 stop=(g == LAST),
             )
 
-        def add_potential(acc, i):
+        def drain(i):
             j, u = divmod(i, SLOTS)
-            if j < LAST:
-                dst, src, order = w_nat[j][u][:], d_nat[j][:, u, :], 0
+            if j in MOVED:
+                dst, src, factor = w_raw[j][:, u, :], d_raw[j][:, u, :], seg_cols[:, u, 8 * j : 8 * j + 1]
             else:
-                dst, src, order = w_raw[j][:, u, :], d_raw[j][:, u, :], 1
-            nc.vector.scalar_tensor_tensor(
-                out=dst, in0=src, scalar=cols[:, order, u, j : j + 1], in1=acc[:], op0=MULT, op1=ADD
-            )
+                dst, src, factor = w_nat[j][u][:], d_nat[j][:, u, :], nat_cols[:, 2 * i : 2 * i + 1]
+            nc.vector.scalar_tensor_tensor(out=dst, in0=src, scalar=factor, in1=acc[i][:], op0=MULT, op1=ADD)
+            if j in UNMOVED:
+                nc.sync.dma_start(out=w_raw[j][QUAD * u : QUAD * (u + 1), :, :], in_=w_nat[j][u][:])
 
-        def regroup(j, u):
-            nc.sync.dma_start(out=w_raw[j][32 * u : 32 * (u + 1), :, :], in_=w_nat[j][u][:])
-
-        def second_product(acc, m, j):
+        def second_product(acc, m, j, start, stop):
             sl = slice(P * m, P * (m + 1))
             nc.tensor.matmul_mx(
                 out=acc[:],
@@ -180,70 +177,96 @@ def tile_scaled_block_projection_s9_kernel(tc, dirs, a_words, a_scales, pot, rho
                 lhsT_scale=d_scales[j][:, sl],
                 rhs=w_codes[j][:].bitcast(E5M2X4),
                 rhs_scale=w_scales[j][:],
-                start=(j == 0),
-                stop=(j == LAST),
+                start=start,
+                stop=stop,
             )
 
         def finish(acc, m):
             res = sb([P, B], F32, "res%d" % m)
             nc.vector.scalar_tensor_tensor(
-                out=res[:], in0=acc[:], scalar=cols[:, 0, m, 4:5], in1=rho_all[:], op0=MULT, op1=MULT
+                out=res[:], in0=acc[:], scalar=nat_cols[:, 8 * m + 1 : 8 * m + 2], in1=rho_all[:], op0=MULT, op1=MULT
             )
             nc.sync.dma_start(out=out[P * m : P * (m + 1), :], in_=res[:])
+
+        def quantize_d(g):
+            quantize(d_codes[g], d_scales[g], d_mix[g], E4M3X4)
 
         def quantize_w(j):
             quantize(w_codes[j], w_scales[j], w_mix[j], E5M2X4)
 
+        def interleave_w(j):
+            interleave(nc.scalar.copy, w_mix[j], w_raw[j], 0, B)
+
         acc = {}
 
-        def whole_tile(i):
-            acc[i] = bank(i % 8)
+        def whole_tile(i, b):
+            acc[i] = bank(b)
             for g in GROUPS:
                 first_product(acc[i], i, g)
 
-        def drain(i):
-            add_potential(acc[i], i)
-            if i // SLOTS < LAST:
-                regroup(i // SLOTS, i % SLOTS)
+        zero(s_raw[0][:].rearrange("p g n -> p (g n)"))
+        zero(nat_rows[:])
+        zero(seg_rows[:])
+        zero(s_raw[1][:].rearrange("p g n -> p (g n)"))
 
         for g in GROUPS:
-            interleave_shared(d_mix[g], d_raw[g], V_COLS if g < 2 else B // 2)
+            load_d(g)
+            load_a_early(g)
             if g == 0:
-                nc.scalar.copy(out=cols[:], in_=turned[:, :, :, 0 : len(GROUPS) + 1])
-                for i in range(8):
-                    acc[i] = bank(i)
-            if g >= 2:
-                move_words(2 * (g - 2), 2 * (g - 1))
-            quantize(d_codes[g], d_scales[g], d_mix[g], E4M3X4)
-            if g >= 2:
-                move_scales(2 * (g - 2), 2 * (g - 1))
-            for i in range(8) if g < 2 else range(4):
+                load_scales(0)
+        load_tables()
+        load_scales(1)
+        load_a_late(0)
+        load_a_late(1)
+        load_d_nat(0)
+        load_d_nat(2)
+
+        for i in range(8):
+            acc[i] = bank(i)
+        for g in GROUPS:
+            interleave_shared(d_mix[g], d_raw[g], V_COLS if g == 0 else B // 2)
+            if g > 0:
+                move_words(1, g)
+            quantize_d(g)
+            if g == 0:
+                move_words(1, g)
+            if g < 2:
+                move_scales(1, 2 * g, 2 * g + 2)
+            for i in range(8) if g < 2 else range(4, 8):
                 first_product(acc[i], i, g)
-        for i in range(4, 8):
+        turn_tables()
+        for i in range(4):
             first_product(acc[i], i, 2)
             first_product(acc[i], i, 3)
-        for i in range(8):
+        for i in range(4, 8):
             drain(i)
-        interleave(nc.scalar.copy, w_mix[0], w_raw[0], 0, B)
-        interleave(nc.scalar.copy, w_mix[1], w_raw[1], 0, B)
-        for i in range(8, 15):
-            whole_tile(i)
-            if i == 12:
-                quantize_w(0)
-            if i == 14:
-                quantize_w(1)
+        interleave_w(1)
+        move_scales(3, 0, 4)
+        for i in range(4):
             drain(i)
-        whole_tile(15)
+        interleave_w(0)
+        for i in range(8, 12):
+            whole_tile(i, i - 4)
+            drain(i)
+            if i < 10:
+                move_late_words(3, i - 8)
+        nc.sync.dma_start(out=rho_all[:], in_=rho.partition_broadcast(P))
+        for i in range(12, 15):
+            whole_tile(i, i - 12)
+            if i < 14:
+                quantize_w(13 - i)
+            drain(i)
+        whole_tile(15, 3)
         interleave_shared(w_mix[2], w_raw[2], B // 2)
         drain(15)
-        h_acc = [bank(m) for m in range(4)]
-        for j in (0, 1):
+        h_acc = [bank(4 + m) for m in range(4)]
+        for j in (1, 0):
             for m in range(4):
-                second_product(h_acc[m], m, j)
+                second_product(h_acc[m], m, j, j == 1, False)
         quantize_w(2)
         interleave_shared(w_mix[3], w_raw[3], V_COLS)
         quantize_w(3)
         for m in range(4):
-            second_product(h_acc[m], m, 2)
-            second_product(h_acc[m], m, 3)
+            second_product(h_acc[m], m, 2, False, False)
+            second_product(h_acc[m], m, 3, False, True)
             finish(h_acc[m], m)

@@ -62,6 +62,7 @@ def tile_scaled_block_projection_s9_kernel(tc, dirs, a_words, a_scales, pot, rho
         seg_rows = sb([P, P], BF16, "seg_rows")
         seg_slots = sb([P, SLOTS, QUAD], BF16, "seg_slots")
         seg_cols = sb([P, SLOTS, QUAD], BF16, "seg_cols")
+        rho_some = sb([P, B], BF16, "rho_some")
         rho_all = sb([P, B], BF16, "rho_all")
 
         def load_scales(half):
@@ -215,11 +216,13 @@ def tile_scaled_block_projection_s9_kernel(tc, dirs, a_words, a_scales, pot, rho
             if g == 0:
                 load_scales(0)
         load_tables()
+        nc.sync.dma_start(out=rho_some[0:P:8, :], in_=rho.partition_broadcast(P // 8))
         load_scales(1)
         load_a_late(0)
         load_a_late(1)
         load_d_nat(0)
         load_d_nat(2)
+        nc.sync.dma_start(out=rho_all[:], in_=rho_some[0:P:8, :].unsqueeze(1).to_broadcast([P // 8, 8, B]))
 
         for i in range(8):
             acc[i] = bank(i)
@@ -250,11 +253,12 @@ def tile_scaled_block_projection_s9_kernel(tc, dirs, a_words, a_scales, pot, rho
             drain(i)
             if i < 10:
                 move_late_words(3, i - 8)
-        nc.sync.dma_start(out=rho_all[:], in_=rho.partition_broadcast(P))
+            if i == 10:
+                quantize_w(1)
         for i in range(12, 15):
             whole_tile(i, i - 12)
-            if i < 14:
-                quantize_w(13 - i)
+            if i == 13:
+                quantize_w(0)
             drain(i)
         whole_tile(15, 3)
         interleave_shared(w_mix[2], w_raw[2], B // 2)

@@ -26,7 +26,9 @@ LAST = len(GROUPS) - 1
 HALF = K // 2
 MOVED = (1, 3)
 UNMOVED = (0, 2)
-V_COLS = 320
+V_SHARE = (320, 128, 192, 320)
+V_URGENT = 320
+V_W2 = 192
 
 
 def tile_scaled_block_projection_s9_kernel(tc, dirs, a_words, a_scales, pot, rho, out):
@@ -53,7 +55,7 @@ def tile_scaled_block_projection_s9_kernel(tc, dirs, a_words, a_scales, pot, rho
         w_codes = [sb([P, B], U32, "w_codes%d" % j) for j in GROUPS]
         w_scales = [sb([P, B], U8, "w_scales%d" % j) for j in GROUPS]
         a_early = [sb([P, 2 * HALF], U8, "a_early%d" % g) for g in GROUPS]
-        a_late = [sb([P, 2, 2 * HALF], U8, "a_late%d" % x) for x in (0, 1)]
+        a_late = {j: sb([P, len(GROUPS), 2 * G], U8, "a_late%d" % j) for j in (2, 3)}
         a_moved = {j: sb([P, len(GROUPS), 2 * G], U8, "a_moved%d" % j) for j in MOVED}
         s_raw = [sb([P, len(GROUPS), HALF], U8, "s_raw%d" % h) for h in (0, 1)]
         s_moved = {j: sb([P, len(GROUPS), G], U8, "s_moved%d" % j) for j in MOVED}
@@ -75,10 +77,10 @@ def tile_scaled_block_projection_s9_kernel(tc, dirs, a_words, a_scales, pot, rho
         def load_a_early(g):
             nc.sync.dma_start(out=a_early[g][:].bitcast(I32), in_=a_words[g][:, 0 : 2 * HALF].bitcast(I32))
 
-        def load_a_late(x):
+        def load_a_late(j):
             nc.sync.dma_start(
-                out=a_late[x][:].bitcast(I32),
-                in_=a_words[2 * x : 2 * x + 2, :, 2 * HALF :].rearrange("g p n -> p g n").bitcast(I32),
+                out=a_late[j][:].bitcast(I32),
+                in_=a_words[:, :, 2 * G * j : 2 * G * (j + 1)].rearrange("g p n -> p g n").bitcast(I32),
             )
 
         def load_d(g):
@@ -92,12 +94,17 @@ def tile_scaled_block_projection_s9_kernel(tc, dirs, a_words, a_scales, pot, rho
             nc.sync.dma_start(out=nat_rows[0:P:2, :], in_=pot.rearrange("(i q c) -> q i c", q=4, c=QUAD))
             nc.sync.dma_start(out=nat_rows[1:P:8, :], in_=rho.rearrange("(m q c) -> q m c", q=4, c=QUAD))
 
-        def turn_tables():
+        def spread_rho():
+            nc.sync.dma_start(out=rho_all[:], in_=rho_some[0:P:8, :].unsqueeze(1).to_broadcast([P // 8, 8, B]))
+
+        def turn_seg():
             nc.scalar.copy(out=seg_slots[:], in_=seg_rows[:].rearrange("p (c t) -> p t c", t=SLOTS))
-            nc.vector.transpose(out=nat_cols[:], in_=nat_rows[:])
             nc.vector.transpose(
                 out=seg_cols[:].rearrange("p t k -> p (t k)"), in_=seg_slots[:].rearrange("p t c -> p (t c)")
             )
+
+        def turn_nat():
+            nc.vector.transpose(out=nat_cols[:], in_=nat_rows[:])
 
         def zero(tile):
             nc.vector.memset(tile.bitcast(I32), 0)
@@ -118,8 +125,7 @@ def tile_scaled_block_projection_s9_kernel(tc, dirs, a_words, a_scales, pot, rho
             )
 
         def loaded_words(j, g):
-            half = a_early[g][:] if j < 2 else a_late[g // 2][:, g % 2, :]
-            return half[:, 2 * G * (j % 2) : 2 * G * (j % 2 + 1)]
+            return a_early[g][:, 2 * G * j : 2 * G * (j + 1)] if j < 2 else a_late[j][:, g, :]
 
         def loaded_scales(j):
             return s_raw[j // 2][:, :, G * (j % 2) : G * (j % 2 + 1)]
@@ -131,10 +137,9 @@ def tile_scaled_block_projection_s9_kernel(tc, dirs, a_words, a_scales, pot, rho
             )
 
         def move_late_words(j, x):
-            cols = slice(2 * G * (j % 2), 2 * G * (j % 2 + 1))
             nc.vector.tensor_copy(
                 out=a_moved[j][:, 2 * x : 2 * x + 2, :].bitcast(U16).rearrange("p g (t m) -> p g t m", t=SLOTS),
-                in_=a_late[x][:, :, cols].bitcast(U16).rearrange("p g (m t) -> p g t m", t=SLOTS),
+                in_=a_late[j][:, 2 * x : 2 * x + 2, :].bitcast(U16).rearrange("p g (m t) -> p g t m", t=SLOTS),
             )
 
         def move_scales(j, lo, hi):
@@ -189,6 +194,20 @@ def tile_scaled_block_projection_s9_kernel(tc, dirs, a_words, a_scales, pot, rho
             )
             nc.sync.dma_start(out=out[P * m : P * (m + 1), :], in_=res[:])
 
+        def quantize_halves(codes, scales, mix, fmt):
+            for lo in (0, B // 2):
+                hi = lo + B // 2
+                nc.vector.quantize_mx(
+                    out=codes[:, lo:hi].bitcast(fmt),
+                    scales=scales[:, lo:hi],
+                    in_=mix[:, lo:hi, :].rearrange("p b t -> p (b t)"),
+                )
+
+        def interleave_urgent(mix, raw):
+            interleave(nc.vector.tensor_copy, mix, raw, 0, B // 2)
+            interleave(nc.vector.tensor_copy, mix, raw, B // 2, V_URGENT)
+            interleave(nc.scalar.copy, mix, raw, V_URGENT, B)
+
         def quantize_d(g):
             quantize(d_codes[g], d_scales[g], d_mix[g], E4M3X4)
 
@@ -215,61 +234,64 @@ def tile_scaled_block_projection_s9_kernel(tc, dirs, a_words, a_scales, pot, rho
             load_a_early(g)
             if g == 0:
                 load_scales(0)
-        load_tables()
-        nc.sync.dma_start(out=rho_some[0:P:8, :], in_=rho.partition_broadcast(P // 8))
-        load_scales(1)
-        load_a_late(0)
-        load_a_late(1)
+            if g == 2:
+                load_tables()
         load_d_nat(0)
+        load_a_late(2)
+        load_scales(1)
+        load_a_late(3)
         load_d_nat(2)
-        nc.sync.dma_start(out=rho_all[:], in_=rho_some[0:P:8, :].unsqueeze(1).to_broadcast([P // 8, 8, B]))
+        nc.sync.dma_start(out=rho_some[0:P:8, :], in_=rho.partition_broadcast(P // 8))
 
         for i in range(8):
             acc[i] = bank(i)
         for g in GROUPS:
-            interleave_shared(d_mix[g], d_raw[g], V_COLS if g == 0 else B // 2)
-            if g > 0:
-                move_words(1, g)
-            quantize_d(g)
             if g == 0:
+                interleave_urgent(d_mix[g], d_raw[g])
+                quantize_halves(d_codes[g], d_scales[g], d_mix[g], E4M3X4)
                 move_words(1, g)
+            else:
+                interleave_shared(d_mix[g], d_raw[g], V_SHARE[g])
+                move_words(1, g)
+                quantize_d(g)
             if g < 2:
                 move_scales(1, 2 * g, 2 * g + 2)
+            if g == 2:
+                turn_seg()
             for i in range(8) if g < 2 else range(4, 8):
                 first_product(acc[i], i, g)
-        turn_tables()
+        turn_nat()
         for i in range(4):
             first_product(acc[i], i, 2)
             first_product(acc[i], i, 3)
         for i in range(4, 8):
             drain(i)
         interleave_w(1)
-        move_scales(3, 0, 4)
         for i in range(4):
             drain(i)
+        spread_rho()
         interleave_w(0)
+        move_late_words(3, 0)
+        move_late_words(3, 1)
         for i in range(8, 12):
             whole_tile(i, i - 4)
             drain(i)
-            if i < 10:
-                move_late_words(3, i - 8)
-            if i == 10:
-                quantize_w(1)
-        for i in range(12, 15):
+            if i == 8:
+                move_scales(3, 0, 4)
+        for i in range(12, 16):
             whole_tile(i, i - 12)
-            if i == 13:
-                quantize_w(0)
+            if i in (12, 14):
+                quantize_w(1 if i == 12 else 0)
+            if i == 15:
+                interleave_shared(w_mix[2], w_raw[2], V_W2)
             drain(i)
-        whole_tile(15, 3)
-        interleave_shared(w_mix[2], w_raw[2], B // 2)
-        drain(15)
         h_acc = [bank(4 + m) for m in range(4)]
         for j in (1, 0):
             for m in range(4):
                 second_product(h_acc[m], m, j, j == 1, False)
         quantize_w(2)
-        interleave_shared(w_mix[3], w_raw[3], V_COLS)
-        quantize_w(3)
+        interleave_urgent(w_mix[3], w_raw[3])
+        quantize_halves(w_codes[3], w_scales[3], w_mix[3], E5M2X4)
         for m in range(4):
             second_product(h_acc[m], m, 2, False, False)
             second_product(h_acc[m], m, 3, False, True)

@@ -24,11 +24,10 @@ G = P * SLOTS
 GROUPS = range(K // G)
 LAST = len(GROUPS) - 1
 HALF = K // 2
-MOVED = (1, 3)
-UNMOVED = (0, 2)
+MOVED = (1, 2, 3)
+UNMOVED = (0,)
 V_SHARE = (320, 128, 192, 320)
 V_URGENT = 320
-V_W2 = 192
 
 
 def tile_scaled_block_projection_s9_kernel(tc, dirs, a_words, a_scales, pot, rho, out):
@@ -57,8 +56,11 @@ def tile_scaled_block_projection_s9_kernel(tc, dirs, a_words, a_scales, pot, rho
         a_early = [sb([P, 2 * HALF], U8, "a_early%d" % g) for g in GROUPS]
         a_late = {j: sb([P, len(GROUPS), 2 * G], U8, "a_late%d" % j) for j in (2, 3)}
         a_moved = {j: sb([P, len(GROUPS), 2 * G], U8, "a_moved%d" % j) for j in MOVED}
-        s_raw = [sb([P, len(GROUPS), HALF], U8, "s_raw%d" % h) for h in (0, 1)]
-        s_moved = {j: sb([P, len(GROUPS), G], U8, "s_moved%d" % j) for j in MOVED}
+        s_early = sb([P, len(GROUPS), HALF], U8, "s_early")
+        s_one = sb([P, len(GROUPS), G], U8, "s_one")
+        s_packed = sb([P, G], U8, "s_packed")
+        s_packed_moved = sb([P, G], U8, "s_packed_moved")
+        s_late = sb([P, len(GROUPS), 2, G], U8, "s_late")
         nat_rows = sb([P, QUAD], BF16, "nat_rows")
         nat_cols = sb([P, QUAD], BF16, "nat_cols")
         seg_rows = sb([P, P], BF16, "seg_rows")
@@ -67,11 +69,32 @@ def tile_scaled_block_projection_s9_kernel(tc, dirs, a_words, a_scales, pot, rho
         rho_some = sb([P, B], BF16, "rho_some")
         rho_all = sb([P, B], BF16, "rho_all")
 
-        def load_scales(half):
+        def load_early_scales():
             for r in range(4):
                 nc.sync.dma_start(
-                    out=s_raw[half][r:P:QUAD, :, :].bitcast(I32),
-                    in_=a_scales[:, r:16:4, HALF * half : HALF * (half + 1)].rearrange("g q n -> q g n").bitcast(I32),
+                    out=s_early[r:P:QUAD, :, :].bitcast(I32),
+                    in_=a_scales[:, r:16:4, 0:HALF].rearrange("g q n -> q g n").bitcast(I32),
+                )
+
+        def load_packed_scales():
+            for x in (0, 1):
+                lo = HALF + G * x
+                nc.sync.dma_start(
+                    out=s_packed[x:P:2, :].bitcast(I32),
+                    in_=a_scales[:, :, lo : lo + G].rearrange("g q n -> q g n").bitcast(I32),
+                )
+
+        def move_packed_scales():
+            nc.vector.tensor_copy(
+                out=s_packed_moved[:].rearrange("p (t m) -> p t m", t=SLOTS),
+                in_=s_packed[:].rearrange("p (m t) -> p t m", t=SLOTS),
+            )
+
+        def spread_packed_scales():
+            for q in range(4):
+                nc.sync.dma_start(
+                    out=s_late[QUAD * q : QUAD * q + 4, :, :, :].rearrange("r g x n -> r (g x n)").bitcast(I32),
+                    in_=s_packed_moved[QUAD * q : QUAD * (q + 1), :].bitcast(I32),
                 )
 
         def load_a_early(g):
@@ -127,8 +150,10 @@ def tile_scaled_block_projection_s9_kernel(tc, dirs, a_words, a_scales, pot, rho
         def loaded_words(j, g):
             return a_early[g][:, 2 * G * j : 2 * G * (j + 1)] if j < 2 else a_late[j][:, g, :]
 
-        def loaded_scales(j):
-            return s_raw[j // 2][:, :, G * (j % 2) : G * (j % 2 + 1)]
+        def plane(j, g):
+            if j == 0:
+                return s_early[:, g, 0:G]
+            return s_one[:, g, :] if j == 1 else s_late[:, g, j - 2, :]
 
         def move_words(j, g):
             nc.vector.tensor_copy(
@@ -142,18 +167,16 @@ def tile_scaled_block_projection_s9_kernel(tc, dirs, a_words, a_scales, pot, rho
                 in_=a_late[j][:, 2 * x : 2 * x + 2, :].bitcast(U16).rearrange("p g (m t) -> p g t m", t=SLOTS),
             )
 
-        def move_scales(j, lo, hi):
+        def move_scales(lo, hi):
             nc.vector.tensor_copy(
-                out=s_moved[j][:, lo:hi, :].rearrange("p g (t m) -> p g t m", t=SLOTS),
-                in_=loaded_scales(j)[:, lo:hi, :].rearrange("p g (m t) -> p g t m", t=SLOTS),
+                out=s_one[:, lo:hi, :].rearrange("p g (t m) -> p g t m", t=SLOTS),
+                in_=s_early[:, lo:hi, G:].rearrange("p g (m t) -> p g t m", t=SLOTS),
             )
 
         def first_product(acc, i, g):
             j, u = divmod(i, SLOTS)
-            if j in MOVED:
-                words, scales = a_moved[j][:, g, :], s_moved[j][:, g, :]
-            else:
-                words, scales = loaded_words(j, g), loaded_scales(j)[:, g, :]
+            words = a_moved[j][:, g, :] if j in MOVED else loaded_words(j, g)
+            scales = plane(j, g)
             c = P * u
             nc.tensor.matmul_mx(
                 out=acc[:],
@@ -224,24 +247,22 @@ def tile_scaled_block_projection_s9_kernel(tc, dirs, a_words, a_scales, pot, rho
             for g in GROUPS:
                 first_product(acc[i], i, g)
 
-        zero(s_raw[0][:].rearrange("p g n -> p (g n)"))
+        zero(s_early[:].rearrange("p g n -> p (g n)"))
         zero(nat_rows[:])
         zero(seg_rows[:])
-        zero(s_raw[1][:].rearrange("p g n -> p (g n)"))
+        zero(s_late[:].rearrange("p g x n -> p (g x n)"))
 
         for g in GROUPS:
             load_d(g)
             load_a_early(g)
             if g == 0:
-                load_scales(0)
+                load_early_scales()
+            if g == 1:
+                load_packed_scales()
             if g == 2:
                 load_tables()
-        load_d_nat(0)
         load_a_late(2)
-        load_scales(1)
-        load_a_late(3)
-        load_d_nat(2)
-        nc.sync.dma_start(out=rho_some[0:P:8, :], in_=rho.partition_broadcast(P // 8))
+        load_d_nat(0)
 
         for i in range(8):
             acc[i] = bank(i)
@@ -255,8 +276,12 @@ def tile_scaled_block_projection_s9_kernel(tc, dirs, a_words, a_scales, pot, rho
                 move_words(1, g)
                 quantize_d(g)
             if g < 2:
-                move_scales(1, 2 * g, 2 * g + 2)
+                move_scales(2 * g, 2 * g + 2)
             if g == 2:
+                move_packed_scales()
+                spread_packed_scales()
+                load_a_late(3)
+                nc.sync.dma_start(out=rho_some[0:P:8, :], in_=rho.partition_broadcast(P // 8))
                 turn_seg()
             for i in range(8) if g < 2 else range(4, 8):
                 first_product(acc[i], i, g)
@@ -264,26 +289,26 @@ def tile_scaled_block_projection_s9_kernel(tc, dirs, a_words, a_scales, pot, rho
         for i in range(4):
             first_product(acc[i], i, 2)
             first_product(acc[i], i, 3)
+        move_late_words(2, 0)
         for i in range(4, 8):
             drain(i)
+            if i == 5:
+                move_late_words(2, 1)
         interleave_w(1)
         for i in range(4):
             drain(i)
         spread_rho()
         interleave_w(0)
-        move_late_words(3, 0)
-        move_late_words(3, 1)
         for i in range(8, 12):
             whole_tile(i, i - 4)
             drain(i)
-            if i == 8:
-                move_scales(3, 0, 4)
+            if i in (8, 9):
+                move_late_words(3, i - 8)
+        interleave_w(2)
         for i in range(12, 16):
             whole_tile(i, i - 12)
             if i in (12, 14):
                 quantize_w(1 if i == 12 else 0)
-            if i == 15:
-                interleave_shared(w_mix[2], w_raw[2], V_W2)
             drain(i)
         h_acc = [bank(4 + m) for m in range(4)]
         for j in (1, 0):

@@ -53,7 +53,8 @@ def tile_scaled_block_projection_s9_kernel(tc, dirs, a_words, a_scales, pot, rho
         w_mix = [sb([P, B, SLOTS], BF16, "w_mix%d" % j) for j in GROUPS]
         w_codes = [sb([P, B], U32, "w_codes%d" % j) for j in GROUPS]
         w_scales = [sb([P, B], U8, "w_scales%d" % j) for j in GROUPS]
-        a_early = [sb([P, 2 * HALF], U8, "a_early%d" % g) for g in GROUPS]
+        a_first = sb([P, 2 * HALF], U8, "a_first")
+        a_early = sb([P, LAST, 2 * HALF], U8, "a_early")
         a_late = {j: sb([P, len(GROUPS), 2 * G], U8, "a_late%d" % j) for j in (2, 3)}
         a_moved = {j: sb([P, len(GROUPS), 2 * G], U8, "a_moved%d" % j) for j in MOVED}
         s_early = sb([P, len(GROUPS), HALF], U8, "s_early")
@@ -97,8 +98,13 @@ def tile_scaled_block_projection_s9_kernel(tc, dirs, a_words, a_scales, pot, rho
                     in_=s_packed_moved[QUAD * q : QUAD * (q + 1), :].bitcast(I32),
                 )
 
-        def load_a_early(g):
-            nc.sync.dma_start(out=a_early[g][:].bitcast(I32), in_=a_words[g][:, 0 : 2 * HALF].bitcast(I32))
+        def load_a_first():
+            nc.sync.dma_start(out=a_first[:].bitcast(I32), in_=a_words[0][:, 0 : 2 * HALF].bitcast(I32))
+
+        def load_a_early():
+            nc.sync.dma_start(
+                out=a_early[:].bitcast(I32), in_=a_words[1:, :, 0 : 2 * HALF].rearrange("g p n -> p g n").bitcast(I32)
+            )
 
         def load_a_late(j):
             nc.sync.dma_start(
@@ -148,7 +154,10 @@ def tile_scaled_block_projection_s9_kernel(tc, dirs, a_words, a_scales, pot, rho
             )
 
         def loaded_words(j, g):
-            return a_early[g][:, 2 * G * j : 2 * G * (j + 1)] if j < 2 else a_late[j][:, g, :]
+            if j >= 2:
+                return a_late[j][:, g, :]
+            half = a_first[:] if g == 0 else a_early[:, g - 1, :]
+            return half[:, 2 * G * j : 2 * G * (j + 1)]
 
         def plane(j, g):
             if j == 0:
@@ -252,17 +261,16 @@ def tile_scaled_block_projection_s9_kernel(tc, dirs, a_words, a_scales, pot, rho
         zero(seg_rows[:])
         zero(s_late[:].rearrange("p g x n -> p (g x n)"))
 
-        for g in GROUPS:
-            load_d(g)
-            load_a_early(g)
-            if g == 0:
-                load_early_scales()
-            if g == 1:
-                load_packed_scales()
-            if g == 2:
-                load_tables()
+        load_d(0)
+        load_a_first()
+        load_early_scales()
+        load_d(1)
+        load_a_early()
+        load_packed_scales()
+        load_d(2)
+        load_d(3)
+        load_tables()
         load_a_late(2)
-        load_d_nat(0)
 
         for i in range(8):
             acc[i] = bank(i)
@@ -277,14 +285,15 @@ def tile_scaled_block_projection_s9_kernel(tc, dirs, a_words, a_scales, pot, rho
                 quantize_d(g)
             if g < 2:
                 move_scales(2 * g, 2 * g + 2)
-            if g == 2:
+            if g == 1:
                 move_packed_scales()
                 spread_packed_scales()
+                load_d_nat(0)
                 load_a_late(3)
                 nc.sync.dma_start(out=rho_some[0:P:8, :], in_=rho.partition_broadcast(P // 8))
-                turn_seg()
             for i in range(8) if g < 2 else range(4, 8):
                 first_product(acc[i], i, g)
+        turn_seg()
         turn_nat()
         for i in range(4):
             first_product(acc[i], i, 2)

@@ -271,6 +271,7 @@ def tile_scaled_block_projection_s9_kernel(tc, dirs, a_words, a_scales, pot, rho
         load_d(3)
         load_tables()
         load_a_late(2)
+        load_d_nat(0)
 
         for i in range(8):
             acc[i] = bank(i)
@@ -288,38 +289,31 @@ def tile_scaled_block_projection_s9_kernel(tc, dirs, a_words, a_scales, pot, rho
             if g == 1:
                 move_packed_scales()
                 spread_packed_scales()
-                load_d_nat(0)
                 load_a_late(3)
                 nc.sync.dma_start(out=rho_some[0:P:8, :], in_=rho.partition_broadcast(P // 8))
-            for i in range(8) if g < 2 else range(4, 8):
+            for i in range(8):
                 first_product(acc[i], i, g)
         turn_seg()
         turn_nat()
-        for i in range(4):
-            first_product(acc[i], i, 2)
-            first_product(acc[i], i, 3)
         move_late_words(2, 0)
-        for i in range(4, 8):
+        move_late_words(2, 1)
+        for i in range(8):
             drain(i)
-            if i == 5:
-                move_late_words(2, 1)
         interleave_w(1)
-        for i in range(4):
-            drain(i)
         spread_rho()
         interleave_w(0)
         for i in range(8, 12):
-            whole_tile(i, i - 4)
+            whole_tile(i, i - 8)
             drain(i)
             if i in (8, 9):
                 move_late_words(3, i - 8)
         interleave_w(2)
         for i in range(12, 16):
-            whole_tile(i, i - 12)
+            whole_tile(i, i - 8)
             if i in (12, 14):
                 quantize_w(1 if i == 12 else 0)
             drain(i)
-        h_acc = [bank(4 + m) for m in range(4)]
+        h_acc = [bank(m) for m in range(4)]
         for j in (1, 0):
             for m in range(4):
                 second_product(h_acc[m], m, j, j == 1, False)

@@ -28,6 +28,7 @@ MOVED = (1, 2, 3)
 UNMOVED = (0,)
 V_SHARE = (320, 128, 192, 320)
 V_URGENT = 320
+V_W2 = 128
 
 
 def tile_scaled_block_projection_s9_kernel(tc, dirs, a_words, a_scales, pot, rho, out):
@@ -47,14 +48,13 @@ def tile_scaled_block_projection_s9_kernel(tc, dirs, a_words, a_scales, pot, rho
         d_mix = [sb([P, B, SLOTS], BF16, "d_mix%d" % g) for g in GROUPS]
         d_codes = [sb([P, B], U32, "d_codes%d" % g) for g in GROUPS]
         d_scales = [sb([P, B], U8, "d_scales%d" % g) for g in GROUPS]
-        d_nat = {j: sb([P, SLOTS, B], BF16, "d_nat%d" % j) for j in UNMOVED}
+        d_nat = [sb([P, 2, B], BF16, "d_nat%d" % x) for x in (0, 1)]
         w_nat = {j: [sb([P, B], BF16, "w_nat%d_%d" % (j, u)) for u in range(SLOTS)] for j in UNMOVED}
         w_raw = [sb([P, SLOTS, B], BF16, "w_raw%d" % j) for j in GROUPS]
         w_mix = [sb([P, B, SLOTS], BF16, "w_mix%d" % j) for j in GROUPS]
         w_codes = [sb([P, B], U32, "w_codes%d" % j) for j in GROUPS]
         w_scales = [sb([P, B], U8, "w_scales%d" % j) for j in GROUPS]
-        a_first = sb([P, 2 * HALF], U8, "a_first")
-        a_early = sb([P, LAST, 2 * HALF], U8, "a_early")
+        a_early = [sb([P, 2 * HALF], U8, "a_early%d" % g) for g in GROUPS]
         a_late = {j: sb([P, len(GROUPS), 2 * G], U8, "a_late%d" % j) for j in (2, 3)}
         a_moved = {j: sb([P, len(GROUPS), 2 * G], U8, "a_moved%d" % j) for j in MOVED}
         s_early = sb([P, len(GROUPS), HALF], U8, "s_early")
@@ -98,13 +98,8 @@ def tile_scaled_block_projection_s9_kernel(tc, dirs, a_words, a_scales, pot, rho
                     in_=s_packed_moved[QUAD * q : QUAD * (q + 1), :].bitcast(I32),
                 )
 
-        def load_a_first():
-            nc.sync.dma_start(out=a_first[:].bitcast(I32), in_=a_words[0][:, 0 : 2 * HALF].bitcast(I32))
-
-        def load_a_early():
-            nc.sync.dma_start(
-                out=a_early[:].bitcast(I32), in_=a_words[1:, :, 0 : 2 * HALF].rearrange("g p n -> p g n").bitcast(I32)
-            )
+        def load_a_early(g):
+            nc.sync.dma_start(out=a_early[g][:].bitcast(I32), in_=a_words[g][:, 0 : 2 * HALF].bitcast(I32))
 
         def load_a_late(j):
             nc.sync.dma_start(
@@ -115,12 +110,13 @@ def tile_scaled_block_projection_s9_kernel(tc, dirs, a_words, a_scales, pot, rho
         def load_d(g):
             nc.sync.dma_start(out=d_raw[g][:], in_=dirs[G * g : G * (g + 1), :].rearrange("(p t) b -> p t b", t=SLOTS))
 
-        def load_d_nat(j):
-            nc.sync.dma_start(out=d_nat[j][:], in_=dirs[G * j : G * (j + 1), :].rearrange("(u p) b -> p u b", p=P))
+        def load_d_nat(x):
+            rows = dirs[2 * P * x : 2 * P * (x + 1), :]
+            nc.sync.dma_start(out=d_nat[x][:], in_=rows.rearrange("(u p) b -> p u b", p=P))
 
         def load_tables():
             nc.sync.dma_start(out=seg_rows[0:P:8, :], in_=pot.rearrange("(j q x) -> q j x", q=4, x=P))
-            nc.sync.dma_start(out=nat_rows[0:P:2, :], in_=pot.rearrange("(i q c) -> q i c", q=4, c=QUAD))
+            nc.sync.dma_start(out=nat_rows[0:P:8, :], in_=pot[0:G].rearrange("(u q c) -> q u c", q=4, c=QUAD))
             nc.sync.dma_start(out=nat_rows[1:P:8, :], in_=rho.rearrange("(m q c) -> q m c", q=4, c=QUAD))
 
         def spread_rho():
@@ -154,10 +150,7 @@ def tile_scaled_block_projection_s9_kernel(tc, dirs, a_words, a_scales, pot, rho
             )
 
         def loaded_words(j, g):
-            if j >= 2:
-                return a_late[j][:, g, :]
-            half = a_first[:] if g == 0 else a_early[:, g - 1, :]
-            return half[:, 2 * G * j : 2 * G * (j + 1)]
+            return a_early[g][:, 2 * G * j : 2 * G * (j + 1)] if j < 2 else a_late[j][:, g, :]
 
         def plane(j, g):
             if j == 0:
@@ -202,7 +195,7 @@ def tile_scaled_block_projection_s9_kernel(tc, dirs, a_words, a_scales, pot, rho
             if j in MOVED:
                 dst, src, factor = w_raw[j][:, u, :], d_raw[j][:, u, :], seg_cols[:, u, 8 * j : 8 * j + 1]
             else:
-                dst, src, factor = w_nat[j][u][:], d_nat[j][:, u, :], nat_cols[:, 2 * i : 2 * i + 1]
+                dst, src, factor = w_nat[j][u][:], d_nat[u // 2][:, u % 2, :], nat_cols[:, 8 * u : 8 * u + 1]
             nc.vector.scalar_tensor_tensor(out=dst, in0=src, scalar=factor, in1=acc[i][:], op0=MULT, op1=ADD)
             if j in UNMOVED:
                 nc.sync.dma_start(out=w_raw[j][QUAD * u : QUAD * (u + 1), :, :], in_=w_nat[j][u][:])
@@ -261,14 +254,13 @@ def tile_scaled_block_projection_s9_kernel(tc, dirs, a_words, a_scales, pot, rho
         zero(seg_rows[:])
         zero(s_late[:].rearrange("p g x n -> p (g x n)"))
 
-        load_d(0)
-        load_a_first()
-        load_early_scales()
-        load_d(1)
-        load_a_early()
-        load_packed_scales()
-        load_d(2)
-        load_d(3)
+        for g in GROUPS:
+            load_d(g)
+            load_a_early(g)
+            if g == 0:
+                load_early_scales()
+            if g == 1:
+                load_packed_scales()
         load_tables()
         load_a_late(2)
         load_d_nat(0)
@@ -276,7 +268,7 @@ def tile_scaled_block_projection_s9_kernel(tc, dirs, a_words, a_scales, pot, rho
         for i in range(8):
             acc[i] = bank(i)
         for g in GROUPS:
-            if g == 0:
+            if g in (0, LAST):
                 interleave_urgent(d_mix[g], d_raw[g])
                 quantize_halves(d_codes[g], d_scales[g], d_mix[g], E4M3X4)
                 move_words(1, g)
@@ -289,6 +281,7 @@ def tile_scaled_block_projection_s9_kernel(tc, dirs, a_words, a_scales, pot, rho
             if g == 1:
                 move_packed_scales()
                 spread_packed_scales()
+                load_d_nat(1)
                 load_a_late(3)
                 nc.sync.dma_start(out=rho_some[0:P:8, :], in_=rho.partition_broadcast(P // 8))
             for i in range(8):
@@ -307,11 +300,12 @@ def tile_scaled_block_projection_s9_kernel(tc, dirs, a_words, a_scales, pot, rho
             drain(i)
             if i in (8, 9):
                 move_late_words(3, i - 8)
-        interleave_w(2)
         for i in range(12, 16):
             whole_tile(i, i - 8)
             if i in (12, 14):
                 quantize_w(1 if i == 12 else 0)
+            if i == 15:
+                interleave_shared(w_mix[2], w_raw[2], V_W2)
             drain(i)
         h_acc = [bank(m) for m in range(4)]
         for j in (1, 0):

@@ -26,7 +26,7 @@ LAST = len(GROUPS) - 1
 HALF = K // 2
 MOVED = (1, 2, 3)
 UNMOVED = (0,)
-V_SHARE = (320, 128, 192, 320)
+V_SHARE = (320, 320, 256, 192)
 V_URGENT = 320
 V_W2 = 128
 
@@ -57,11 +57,11 @@ def tile_scaled_block_projection_s9_kernel(tc, dirs, a_words, a_scales, pot, rho
         a_early = [sb([P, 2 * HALF], U8, "a_early%d" % g) for g in GROUPS]
         a_late = {j: sb([P, len(GROUPS), 2 * G], U8, "a_late%d" % j) for j in (2, 3)}
         a_moved = {j: sb([P, len(GROUPS), 2 * G], U8, "a_moved%d" % j) for j in MOVED}
-        s_early = sb([P, len(GROUPS), HALF], U8, "s_early")
-        s_one = sb([P, len(GROUPS), G], U8, "s_one")
+        s_early = [sb([P, 2, HALF], U8, "s_early%d" % x) for x in (0, 1)]
+        s_one = [sb([P, 2, G], U8, "s_one%d" % x) for x in (0, 1)]
         s_packed = sb([P, G], U8, "s_packed")
         s_packed_moved = sb([P, G], U8, "s_packed_moved")
-        s_late = sb([P, len(GROUPS), 2, G], U8, "s_late")
+        s_late = {j: sb([P, len(GROUPS), G], U8, "s_late%d" % j) for j in (2, 3)}
         nat_rows = sb([P, QUAD], BF16, "nat_rows")
         nat_cols = sb([P, QUAD], BF16, "nat_cols")
         seg_rows = sb([P, P], BF16, "seg_rows")
@@ -70,11 +70,11 @@ def tile_scaled_block_projection_s9_kernel(tc, dirs, a_words, a_scales, pot, rho
         rho_some = sb([P, B], BF16, "rho_some")
         rho_all = sb([P, B], BF16, "rho_all")
 
-        def load_early_scales():
+        def load_early_scales(x):
             for r in range(4):
                 nc.sync.dma_start(
-                    out=s_early[r:P:QUAD, :, :].bitcast(I32),
-                    in_=a_scales[:, r:16:4, 0:HALF].rearrange("g q n -> q g n").bitcast(I32),
+                    out=s_early[x][r:P:QUAD, :, :].bitcast(I32),
+                    in_=a_scales[2 * x : 2 * x + 2, r:16:4, 0:HALF].rearrange("g q n -> q g n").bitcast(I32),
                 )
 
         def load_packed_scales():
@@ -91,11 +91,11 @@ def tile_scaled_block_projection_s9_kernel(tc, dirs, a_words, a_scales, pot, rho
                 in_=s_packed[:].rearrange("p (m t) -> p t m", t=SLOTS),
             )
 
-        def spread_packed_scales():
-            for q in range(4):
+        def spread_packed_scales(j):
+            for q in (0, 2, 1, 3):
                 nc.sync.dma_start(
-                    out=s_late[QUAD * q : QUAD * q + 4, :, :, :].rearrange("r g x n -> r (g x n)").bitcast(I32),
-                    in_=s_packed_moved[QUAD * q : QUAD * (q + 1), :].bitcast(I32),
+                    out=s_late[j][QUAD * q : QUAD * q + 4, :, :].rearrange("r g n -> r (g n)").bitcast(I32),
+                    in_=s_packed_moved[QUAD * q + j - 2 : QUAD * (q + 1) : 2, :].bitcast(I32),
                 )
 
         def load_a_early(g):
@@ -154,8 +154,8 @@ def tile_scaled_block_projection_s9_kernel(tc, dirs, a_words, a_scales, pot, rho
 
         def plane(j, g):
             if j == 0:
-                return s_early[:, g, 0:G]
-            return s_one[:, g, :] if j == 1 else s_late[:, g, j - 2, :]
+                return s_early[g // 2][:, g % 2, 0:G]
+            return s_one[g // 2][:, g % 2, :] if j == 1 else s_late[j][:, g, :]
 
         def move_words(j, g):
             nc.vector.tensor_copy(
@@ -169,10 +169,10 @@ def tile_scaled_block_projection_s9_kernel(tc, dirs, a_words, a_scales, pot, rho
                 in_=a_late[j][:, 2 * x : 2 * x + 2, :].bitcast(U16).rearrange("p g (m t) -> p g t m", t=SLOTS),
             )
 
-        def move_scales(lo, hi):
+        def move_scales(x):
             nc.vector.tensor_copy(
-                out=s_one[:, lo:hi, :].rearrange("p g (t m) -> p g t m", t=SLOTS),
-                in_=s_early[:, lo:hi, G:].rearrange("p g (m t) -> p g t m", t=SLOTS),
+                out=s_one[x][:].rearrange("p g (t m) -> p g t m", t=SLOTS),
+                in_=s_early[x][:, :, G:].rearrange("p g (m t) -> p g t m", t=SLOTS),
             )
 
         def first_product(acc, i, g):
@@ -249,65 +249,85 @@ def tile_scaled_block_projection_s9_kernel(tc, dirs, a_words, a_scales, pot, rho
             for g in GROUPS:
                 first_product(acc[i], i, g)
 
-        zero(s_early[:].rearrange("p g n -> p (g n)"))
+        for x in (0, 1):
+            zero(s_early[x][:].rearrange("p g n -> p (g n)"))
         zero(nat_rows[:])
         zero(seg_rows[:])
-        zero(s_late[:].rearrange("p g x n -> p (g x n)"))
+        for j in (2, 3):
+            zero(s_late[j][:].rearrange("p g n -> p (g n)"))
 
-        for g in GROUPS:
-            load_d(g)
-            load_a_early(g)
-            if g == 0:
-                load_early_scales()
-            if g == 1:
-                load_packed_scales()
+        load_d(0)
+        load_early_scales(0)
+        load_a_early(0)
+        load_d(1)
+        load_packed_scales()
+        load_a_early(1)
+        load_d(2)
+        load_d(3)
+        load_early_scales(1)
+        load_a_early(2)
+        load_a_early(3)
         load_tables()
         load_a_late(2)
-        load_d_nat(0)
 
         for i in range(8):
             acc[i] = bank(i)
-        for g in GROUPS:
-            if g in (0, LAST):
-                interleave_urgent(d_mix[g], d_raw[g])
-                quantize_halves(d_codes[g], d_scales[g], d_mix[g], E4M3X4)
-                move_words(1, g)
+        for g in (0, 1):
+            interleave_urgent(d_mix[g], d_raw[g])
+            quantize_halves(d_codes[g], d_scales[g], d_mix[g], E4M3X4)
+            move_words(1, g)
+            if g == 0:
+                move_scales(0)
             else:
-                interleave_shared(d_mix[g], d_raw[g], V_SHARE[g])
-                move_words(1, g)
-                quantize_d(g)
-            if g < 2:
-                move_scales(2 * g, 2 * g + 2)
-            if g == 1:
                 move_packed_scales()
-                spread_packed_scales()
+                spread_packed_scales(2)
+                load_d_nat(0)
                 load_d_nat(1)
                 load_a_late(3)
+                spread_packed_scales(3)
                 nc.sync.dma_start(out=rho_some[0:P:8, :], in_=rho.partition_broadcast(P // 8))
             for i in range(8):
                 first_product(acc[i], i, g)
+        interleave_shared(d_mix[2], d_raw[2], V_SHARE[2])
+        interleave_shared(d_mix[3], d_raw[3], V_SHARE[3])
+        quantize_d(2)
+        move_scales(1)
+        move_words(1, 2)
+        quantize_d(3)
+        move_words(1, 3)
         turn_seg()
         turn_nat()
-        move_late_words(2, 0)
-        move_late_words(2, 1)
-        for i in range(8):
+        for i in (0, 1):
+            first_product(acc[i], i, 2)
+        for i in range(4, 8):
+            first_product(acc[i], i, 2)
+            first_product(acc[i], i, 3)
+        for i in range(4):
+            if i > 1:
+                first_product(acc[i], i, 2)
+            first_product(acc[i], i, 3)
+        for i in range(4, 8):
+            if i in (4, 6):
+                move_late_words(2, i // 2 - 2)
             drain(i)
         interleave_w(1)
-        spread_rho()
-        interleave_w(0)
-        for i in range(8, 12):
-            whole_tile(i, i - 8)
+        for i in range(4):
             drain(i)
+        interleave_w(0)
+        spread_rho()
+        for i in range(8, 12):
+            whole_tile(i, i - 4)
             if i in (8, 9):
                 move_late_words(3, i - 8)
+            drain(i)
         for i in range(12, 16):
-            whole_tile(i, i - 8)
+            whole_tile(i, i - 12)
             if i in (12, 14):
                 quantize_w(1 if i == 12 else 0)
             if i == 15:
                 interleave_shared(w_mix[2], w_raw[2], V_W2)
             drain(i)
-        h_acc = [bank(m) for m in range(4)]
+        h_acc = [bank(4 + m) for m in range(4)]
         for j in (1, 0):
             for m in range(4):
                 second_product(h_acc[m], m, j, j == 1, False)

@@ -16,6 +16,7 @@ E5M2X4 = mybir.dt.float8_e5m2_x4
 E2M1X4 = mybir.dt.float4_e2m1fn_x4
 MULT = mybir.AluOpType.mult
 ADD = mybir.AluOpType.add
+COPY = mybir.ActivationFunctionType.Copy
 
 P = 128
 QUAD = 32
@@ -26,9 +27,10 @@ LAST = len(GROUPS) - 1
 HALF = K // 2
 MOVED = (1, 2, 3)
 UNMOVED = (0,)
-V_SHARE = (320, 320, 256, 192)
+V_SHARE = (320, 320, 256, 128)
 V_URGENT = 320
-V_W2 = 128
+V_W2 = 256
+SIDE = (4, 5, 6)
 
 
 def tile_scaled_block_projection_s9_kernel(tc, dirs, a_words, a_scales, pot, rho, out):
@@ -67,6 +69,9 @@ def tile_scaled_block_projection_s9_kernel(tc, dirs, a_words, a_scales, pot, rho
         seg_rows = sb([P, P], BF16, "seg_rows")
         seg_slots = sb([P, SLOTS, QUAD], BF16, "seg_slots")
         seg_cols = sb([P, SLOTS, QUAD], BF16, "seg_cols")
+        seg_f32 = sb([P, SLOTS, QUAD], F32, "seg_f32")
+        pot_d = {i: sb([P, B], F32, "pot_d%d" % i) for i in SIDE}
+        sums = {i: sb([P, B], F32, "sums%d" % i) for i in SIDE}
         rho_some = sb([P, B], BF16, "rho_some")
         rho_all = sb([P, B], BF16, "rho_all")
 
@@ -114,16 +119,20 @@ def tile_scaled_block_projection_s9_kernel(tc, dirs, a_words, a_scales, pot, rho
             rows = dirs[2 * P * x : 2 * P * (x + 1), :]
             nc.sync.dma_start(out=d_nat[x][:], in_=rows.rearrange("(u p) b -> p u b", p=P))
 
-        def load_tables():
+        def load_seg():
             nc.sync.dma_start(out=seg_rows[0:P:8, :], in_=pot.rearrange("(j q x) -> q j x", q=4, x=P))
+
+        def load_nat():
             nc.sync.dma_start(out=nat_rows[0:P:8, :], in_=pot[0:G].rearrange("(u q c) -> q u c", q=4, c=QUAD))
             nc.sync.dma_start(out=nat_rows[1:P:8, :], in_=rho.rearrange("(m q c) -> q m c", q=4, c=QUAD))
 
         def spread_rho():
             nc.sync.dma_start(out=rho_all[:], in_=rho_some[0:P:8, :].unsqueeze(1).to_broadcast([P // 8, 8, B]))
 
-        def turn_seg():
+        def sort_seg():
             nc.scalar.copy(out=seg_slots[:], in_=seg_rows[:].rearrange("p (c t) -> p t c", t=SLOTS))
+
+        def turn_seg():
             nc.vector.transpose(
                 out=seg_cols[:].rearrange("p t k -> p (t k)"), in_=seg_slots[:].rearrange("p t c -> p (t c)")
             )
@@ -163,10 +172,10 @@ def tile_scaled_block_projection_s9_kernel(tc, dirs, a_words, a_scales, pot, rho
                 in_=loaded_words(j, g).bitcast(U16).rearrange("p (m t) -> p t m", t=SLOTS),
             )
 
-        def move_late_words(j, x):
+        def move_late_words(j):
             nc.vector.tensor_copy(
-                out=a_moved[j][:, 2 * x : 2 * x + 2, :].bitcast(U16).rearrange("p g (t m) -> p g t m", t=SLOTS),
-                in_=a_late[j][:, 2 * x : 2 * x + 2, :].bitcast(U16).rearrange("p g (m t) -> p g t m", t=SLOTS),
+                out=a_moved[j][:].bitcast(U16).rearrange("p g (t m) -> p g t m", t=SLOTS),
+                in_=a_late[j][:].bitcast(U16).rearrange("p g (m t) -> p g t m", t=SLOTS),
             )
 
         def move_scales(x):
@@ -198,7 +207,19 @@ def tile_scaled_block_projection_s9_kernel(tc, dirs, a_words, a_scales, pot, rho
                 dst, src, factor = w_nat[j][u][:], d_nat[u // 2][:, u % 2, :], nat_cols[:, 8 * u : 8 * u + 1]
             nc.vector.scalar_tensor_tensor(out=dst, in0=src, scalar=factor, in1=acc[i][:], op0=MULT, op1=ADD)
             if j in UNMOVED:
-                nc.sync.dma_start(out=w_raw[j][QUAD * u : QUAD * (u + 1), :, :], in_=w_nat[j][u][:])
+                queue = nc.sync if u < 2 else nc.scalar
+                queue.dma_start(out=w_raw[j][QUAD * u : QUAD * (u + 1), :, :], in_=w_nat[j][u][:])
+
+        def potential(i):
+            j, u = divmod(i, SLOTS)
+            nc.scalar.activation(
+                out=pot_d[i][:], in_=d_raw[j][:, u, :], func=COPY, scale=seg_f32[:, u, 8 * j : 8 * j + 1]
+            )
+
+        def side_drain(i):
+            j, u = divmod(i, SLOTS)
+            nc.scalar.copy(out=sums[i][:], in_=acc[i][:])
+            nc.gpsimd.tensor_tensor(out=w_raw[j][:, u, :], in0=sums[i][:], in1=pot_d[i][:], op=ADD)
 
         def second_product(acc, m, j, start, stop):
             sl = slice(P * m, P * (m + 1))
@@ -249,14 +270,15 @@ def tile_scaled_block_projection_s9_kernel(tc, dirs, a_words, a_scales, pot, rho
             for g in GROUPS:
                 first_product(acc[i], i, g)
 
+        zero(seg_rows[:])
         for x in (0, 1):
             zero(s_early[x][:].rearrange("p g n -> p (g n)"))
-        zero(nat_rows[:])
-        zero(seg_rows[:])
         for j in (2, 3):
             zero(s_late[j][:].rearrange("p g n -> p (g n)"))
+        nc.scalar.copy(out=nat_rows[:], in_=s_late[2][:, 0, 0 : 2 * QUAD].bitcast(BF16))
 
         load_d(0)
+        load_seg()
         load_early_scales(0)
         load_a_early(0)
         load_d(1)
@@ -267,71 +289,81 @@ def tile_scaled_block_projection_s9_kernel(tc, dirs, a_words, a_scales, pot, rho
         load_early_scales(1)
         load_a_early(2)
         load_a_early(3)
-        load_tables()
         load_a_late(2)
+        load_nat()
+        load_d_nat(0)
+        load_d_nat(1)
 
         for i in range(8):
             acc[i] = bank(i)
-        for g in (0, 1):
-            interleave_urgent(d_mix[g], d_raw[g])
-            quantize_halves(d_codes[g], d_scales[g], d_mix[g], E4M3X4)
-            move_words(1, g)
-            if g == 0:
-                move_scales(0)
-            else:
-                move_packed_scales()
-                spread_packed_scales(2)
-                load_d_nat(0)
-                load_d_nat(1)
-                load_a_late(3)
-                spread_packed_scales(3)
-                nc.sync.dma_start(out=rho_some[0:P:8, :], in_=rho.partition_broadcast(P // 8))
-            for i in range(8):
-                first_product(acc[i], i, g)
+        interleave_urgent(d_mix[0], d_raw[0])
+        sort_seg()
+        quantize_halves(d_codes[0], d_scales[0], d_mix[0], E4M3X4)
+        move_words(1, 0)
+        move_scales(0)
+        turn_seg()
+        for i in range(8):
+            first_product(acc[i], i, 0)
+        interleave_shared(d_mix[1], d_raw[1], V_SHARE[1])
+        nc.scalar.copy(out=seg_f32[:], in_=seg_cols[:])
+        potential(4)
+        move_packed_scales()
+        spread_packed_scales(2)
+        load_a_late(3)
+        quantize_d(1)
+        move_words(1, 1)
+        for i in range(8):
+            first_product(acc[i], i, 1)
         interleave_shared(d_mix[2], d_raw[2], V_SHARE[2])
         interleave_shared(d_mix[3], d_raw[3], V_SHARE[3])
+        for i in SIDE[1:]:
+            potential(i)
         quantize_d(2)
         move_scales(1)
         move_words(1, 2)
         quantize_d(3)
         move_words(1, 3)
-        turn_seg()
+        for i in (0, 1, 4):
+            first_product(acc[i], i, 2)
+        for i in (4, 0, 1):
+            first_product(acc[i], i, 3)
+        for i in (5, 2, 6, 3, 7):
+            first_product(acc[i], i, 2)
+            first_product(acc[i], i, 3)
         turn_nat()
-        for i in (0, 1):
-            first_product(acc[i], i, 2)
-        for i in range(4, 8):
-            first_product(acc[i], i, 2)
-            first_product(acc[i], i, 3)
-        for i in range(4):
-            if i > 1:
-                first_product(acc[i], i, 2)
-            first_product(acc[i], i, 3)
-        for i in range(4, 8):
-            if i in (4, 6):
-                move_late_words(2, i // 2 - 2)
+        move_late_words(2)
+        side_drain(4)
+        drain(0)
+        drain(1)
+        spread_packed_scales(3)
+        nc.sync.dma_start(out=rho_some[0:P:8, :], in_=rho.partition_broadcast(P // 8))
+        side_drain(5)
+        side_drain(6)
+        for i in (2, 3, 7):
             drain(i)
-        interleave_w(1)
-        for i in range(4):
-            drain(i)
-        interleave_w(0)
         spread_rho()
+        interleave_w(1)
+        interleave_w(0)
         for i in range(8, 12):
-            whole_tile(i, i - 4)
-            if i in (8, 9):
-                move_late_words(3, i - 8)
+            whole_tile(i, (4, 0, 1, 5)[i - 8])
+            if i == 9:
+                move_late_words(3)
+            if i == 11:
+                quantize_w(1)
             drain(i)
         for i in range(12, 16):
-            whole_tile(i, i - 12)
-            if i in (12, 14):
-                quantize_w(1 if i == 12 else 0)
-            if i == 15:
+            whole_tile(i, (2, 6, 3, 7)[i - 12])
+            if i == 13:
                 interleave_shared(w_mix[2], w_raw[2], V_W2)
+            if i == 14:
+                quantize_w(0)
+            if i == 15:
+                quantize_w(2)
             drain(i)
-        h_acc = [bank(4 + m) for m in range(4)]
+        h_acc = [bank(b) for b in (4, 0, 1, 5)]
         for j in (1, 0):
             for m in range(4):
                 second_product(h_acc[m], m, j, j == 1, False)
-        quantize_w(2)
         interleave_urgent(w_mix[3], w_raw[3])
         quantize_halves(w_codes[3], w_scales[3], w_mix[3], E5M2X4)
         for m in range(4):

@@ -27,9 +27,9 @@ LAST = len(GROUPS) - 1
 HALF = K // 2
 MOVED = (1, 2, 3)
 UNMOVED = (0,)
-V_SHARE = (320, 320, 256, 128)
+V_SHARE = (320, 320, 256, 192)
 V_URGENT = 320
-V_W2 = 256
+V_W2 = 192
 SIDE = (4, 5, 6)
 
 
@@ -61,8 +61,8 @@ def tile_scaled_block_projection_s9_kernel(tc, dirs, a_words, a_scales, pot, rho
         a_moved = {j: sb([P, len(GROUPS), 2 * G], U8, "a_moved%d" % j) for j in MOVED}
         s_early = [sb([P, 2, HALF], U8, "s_early%d" % x) for x in (0, 1)]
         s_one = [sb([P, 2, G], U8, "s_one%d" % x) for x in (0, 1)]
-        s_packed = sb([P, G], U8, "s_packed")
-        s_packed_moved = sb([P, G], U8, "s_packed_moved")
+        s_packed = sb([P, 2, G], U8, "s_packed")
+        s_packed_moved = sb([P, 2, G], U8, "s_packed_moved")
         s_late = {j: sb([P, len(GROUPS), G], U8, "s_late%d" % j) for j in (2, 3)}
         nat_rows = sb([P, QUAD], BF16, "nat_rows")
         nat_cols = sb([P, QUAD], BF16, "nat_cols")
@@ -83,33 +83,32 @@ def tile_scaled_block_projection_s9_kernel(tc, dirs, a_words, a_scales, pot, rho
                 )
 
         def load_packed_scales():
-            for x in (0, 1):
-                lo = HALF + G * x
+            for r in range(4):
                 nc.sync.dma_start(
-                    out=s_packed[x:P:2, :].bitcast(I32),
-                    in_=a_scales[:, :, lo : lo + G].rearrange("g q n -> q g n").bitcast(I32),
+                    out=s_packed[QUAD * r : QUAD * (r + 1) : 2, :, :].rearrange("p x n -> p (x n)").bitcast(I32),
+                    in_=a_scales[:, r:16:4, HALF:].rearrange("g q n -> q g n").bitcast(I32),
                 )
 
         def move_packed_scales():
             nc.vector.tensor_copy(
-                out=s_packed_moved[:].rearrange("p (t m) -> p t m", t=SLOTS),
-                in_=s_packed[:].rearrange("p (m t) -> p t m", t=SLOTS),
+                out=s_packed_moved[:].rearrange("p x (t m) -> p x t m", t=SLOTS),
+                in_=s_packed[:].rearrange("p x (m t) -> p x t m", t=SLOTS),
             )
 
         def spread_packed_scales(j):
-            for q in (0, 2, 1, 3):
+            for r in range(4):
                 nc.sync.dma_start(
-                    out=s_late[j][QUAD * q : QUAD * q + 4, :, :].rearrange("r g n -> r (g n)").bitcast(I32),
-                    in_=s_packed_moved[QUAD * q + j - 2 : QUAD * (q + 1) : 2, :].bitcast(I32),
+                    out=s_late[j][r:P:QUAD, :, :].rearrange("q g n -> q (g n)").bitcast(I32),
+                    in_=s_packed_moved[QUAD * r : QUAD * (r + 1) : 2, j - 2, :].bitcast(I32),
                 )
 
         def load_a_early(g):
             nc.sync.dma_start(out=a_early[g][:].bitcast(I32), in_=a_words[g][:, 0 : 2 * HALF].bitcast(I32))
 
-        def load_a_late(j):
+        def load_a_late(j, lo=0, hi=len(GROUPS)):
             nc.sync.dma_start(
-                out=a_late[j][:].bitcast(I32),
-                in_=a_words[:, :, 2 * G * j : 2 * G * (j + 1)].rearrange("g p n -> p g n").bitcast(I32),
+                out=a_late[j][:, lo:hi, :].bitcast(I32),
+                in_=a_words[lo:hi, :, 2 * G * j : 2 * G * (j + 1)].rearrange("g p n -> p g n").bitcast(I32),
             )
 
         def load_d(g):
@@ -207,8 +206,7 @@ def tile_scaled_block_projection_s9_kernel(tc, dirs, a_words, a_scales, pot, rho
                 dst, src, factor = w_nat[j][u][:], d_nat[u // 2][:, u % 2, :], nat_cols[:, 8 * u : 8 * u + 1]
             nc.vector.scalar_tensor_tensor(out=dst, in0=src, scalar=factor, in1=acc[i][:], op0=MULT, op1=ADD)
             if j in UNMOVED:
-                queue = nc.sync if u < 2 else nc.scalar
-                queue.dma_start(out=w_raw[j][QUAD * u : QUAD * (u + 1), :, :], in_=w_nat[j][u][:])
+                nc.sync.dma_start(out=w_raw[j][QUAD * u : QUAD * (u + 1), :, :], in_=w_nat[j][u][:])
 
         def potential(i):
             j, u = divmod(i, SLOTS)
@@ -275,6 +273,7 @@ def tile_scaled_block_projection_s9_kernel(tc, dirs, a_words, a_scales, pot, rho
             zero(s_early[x][:].rearrange("p g n -> p (g n)"))
         for j in (2, 3):
             zero(s_late[j][:].rearrange("p g n -> p (g n)"))
+        zero(s_packed[:].rearrange("p x n -> p (x n)"))
         nc.scalar.copy(out=nat_rows[:], in_=s_late[2][:, 0, 0 : 2 * QUAD].bitcast(BF16))
 
         load_d(0)
@@ -282,17 +281,18 @@ def tile_scaled_block_projection_s9_kernel(tc, dirs, a_words, a_scales, pot, rho
         load_early_scales(0)
         load_a_early(0)
         load_d(1)
-        load_packed_scales()
         load_a_early(1)
         load_d(2)
         load_d(3)
         load_early_scales(1)
         load_a_early(2)
         load_a_early(3)
+        load_packed_scales()
         load_a_late(2)
         load_nat()
         load_d_nat(0)
         load_d_nat(1)
+        load_a_late(3, 0, 2)
 
         for i in range(8):
             acc[i] = bank(i)
@@ -307,11 +307,8 @@ def tile_scaled_block_projection_s9_kernel(tc, dirs, a_words, a_scales, pot, rho
         interleave_shared(d_mix[1], d_raw[1], V_SHARE[1])
         nc.scalar.copy(out=seg_f32[:], in_=seg_cols[:])
         potential(4)
-        move_packed_scales()
-        spread_packed_scales(2)
-        load_a_late(3)
-        quantize_d(1)
         move_words(1, 1)
+        quantize_d(1)
         for i in range(8):
             first_product(acc[i], i, 1)
         interleave_shared(d_mix[2], d_raw[2], V_SHARE[2])
@@ -323,24 +320,27 @@ def tile_scaled_block_projection_s9_kernel(tc, dirs, a_words, a_scales, pot, rho
         move_words(1, 2)
         quantize_d(3)
         move_words(1, 3)
-        for i in (0, 1, 4):
+        for i in (0, 1, 4, 5):
             first_product(acc[i], i, 2)
-        for i in (4, 0, 1):
+        for i in (4, 0, 1, 5):
             first_product(acc[i], i, 3)
-        for i in (5, 2, 6, 3, 7):
+        for i in (2, 6, 3, 7):
             first_product(acc[i], i, 2)
             first_product(acc[i], i, 3)
+        move_packed_scales()
+        spread_packed_scales(2)
+        load_a_late(3, 2, 4)
+        spread_packed_scales(3)
         turn_nat()
         move_late_words(2)
         side_drain(4)
         drain(0)
         drain(1)
-        spread_packed_scales(3)
-        nc.sync.dma_start(out=rho_some[0:P:8, :], in_=rho.partition_broadcast(P // 8))
         side_drain(5)
         side_drain(6)
         for i in (2, 3, 7):
             drain(i)
+        nc.sync.dma_start(out=rho_some[0:P:8, :], in_=rho.partition_broadcast(P // 8))
         spread_rho()
         interleave_w(1)
         interleave_w(0)

@@ -29,6 +29,7 @@ MOVED = (1, 2, 3)
 UNMOVED = (0,)
 V_SHARE = (320, 320, 256, 192)
 V_URGENT = 320
+WARM_UPS = 4
 V_W2 = 192
 SIDE = (4, 5, 6)
 
@@ -63,7 +64,9 @@ def tile_scaled_block_projection_s9_kernel(tc, dirs, a_words, a_scales, pot, rho
         s_one = [sb([P, 2, G], U8, "s_one%d" % x) for x in (0, 1)]
         s_packed = sb([P, 2, G], U8, "s_packed")
         s_packed_moved = sb([P, 2, G], U8, "s_packed_moved")
-        s_late = {j: sb([P, len(GROUPS), G], U8, "s_late%d" % j) for j in (2, 3)}
+        s_late = sb([P, 2, len(GROUPS), G], U8, "s_late")
+        idle_codes = [sb([P, n], U32, "idle_codes%d" % n) for n in (P, B)]
+        idle_scales = [sb([P, n], U8, "idle_scales%d" % n) for n in (P, B)]
         nat_rows = sb([P, QUAD], BF16, "nat_rows")
         nat_cols = sb([P, QUAD], BF16, "nat_cols")
         seg_rows = sb([P, P], BF16, "seg_rows")
@@ -98,7 +101,7 @@ def tile_scaled_block_projection_s9_kernel(tc, dirs, a_words, a_scales, pot, rho
         def spread_packed_scales(j):
             for r in range(4):
                 nc.sync.dma_start(
-                    out=s_late[j][r:P:QUAD, :, :].rearrange("q g n -> q (g n)").bitcast(I32),
+                    out=s_late[r:P:QUAD, j - 2, :, :].rearrange("q g n -> q (g n)").bitcast(I32),
                     in_=s_packed_moved[QUAD * r : QUAD * (r + 1) : 2, j - 2, :].bitcast(I32),
                 )
 
@@ -163,7 +166,7 @@ def tile_scaled_block_projection_s9_kernel(tc, dirs, a_words, a_scales, pot, rho
         def plane(j, g):
             if j == 0:
                 return s_early[g // 2][:, g % 2, 0:G]
-            return s_one[g // 2][:, g % 2, :] if j == 1 else s_late[j][:, g, :]
+            return s_one[g // 2][:, g % 2, :] if j == 1 else s_late[:, j - 2, g, :]
 
         def move_words(j, g):
             nc.vector.tensor_copy(
@@ -177,10 +180,10 @@ def tile_scaled_block_projection_s9_kernel(tc, dirs, a_words, a_scales, pot, rho
                 in_=a_late[j][:].bitcast(U16).rearrange("p g (m t) -> p g t m", t=SLOTS),
             )
 
-        def move_scales(x):
+        def move_scales(x, lo=0, hi=2):
             nc.vector.tensor_copy(
-                out=s_one[x][:].rearrange("p g (t m) -> p g t m", t=SLOTS),
-                in_=s_early[x][:, :, G:].rearrange("p g (m t) -> p g t m", t=SLOTS),
+                out=s_one[x][:, lo:hi, :].rearrange("p g (t m) -> p g t m", t=SLOTS),
+                in_=s_early[x][:, lo:hi, G:].rearrange("p g (m t) -> p g t m", t=SLOTS),
             )
 
         def first_product(acc, i, g):
@@ -269,12 +272,26 @@ def tile_scaled_block_projection_s9_kernel(tc, dirs, a_words, a_scales, pot, rho
                 first_product(acc[i], i, g)
 
         zero(seg_rows[:])
-        for x in (0, 1):
-            zero(s_early[x][:].rearrange("p g n -> p (g n)"))
-        for j in (2, 3):
-            zero(s_late[j][:].rearrange("p g n -> p (g n)"))
+        zero(s_early[0][:].rearrange("p g n -> p (g n)"))
+        zeros = s_late[:].rearrange("p x g n -> p (x g n)")
+        zero(zeros)
+        zero(s_early[1][:].rearrange("p g n -> p (g n)"))
+        nc.scalar.copy(out=nat_rows[:], in_=zeros[:, 0 : 2 * QUAD].bitcast(BF16))
+        nc.vector.quantize_mx(out=idle_codes[1][:].bitcast(E5M2X4), scales=idle_scales[1][:], in_=zeros.bitcast(BF16))
+        nc.vector.quantize_mx(
+            out=idle_codes[0][:].bitcast(E4M3X4), scales=idle_scales[0][:], in_=zeros[:, 0 : 2 * G].bitcast(BF16)
+        )
+        for w in range(WARM_UPS):
+            nc.tensor.matmul_mx(
+                out=bank(7 - w)[:],
+                lhsT=idle_codes[0][:].bitcast(E4M3X4),
+                lhsT_scale=idle_scales[0][:],
+                rhs=idle_codes[1][:].bitcast(E5M2X4),
+                rhs_scale=idle_scales[1][:],
+                start=True,
+                stop=True,
+            )
         zero(s_packed[:].rearrange("p x n -> p (x n)"))
-        nc.scalar.copy(out=nat_rows[:], in_=s_late[2][:, 0, 0 : 2 * QUAD].bitcast(BF16))
 
         load_d(0)
         load_seg()
@@ -300,15 +317,16 @@ def tile_scaled_block_projection_s9_kernel(tc, dirs, a_words, a_scales, pot, rho
         sort_seg()
         quantize_halves(d_codes[0], d_scales[0], d_mix[0], E4M3X4)
         move_words(1, 0)
-        move_scales(0)
+        move_scales(0, 0, 1)
         turn_seg()
         for i in range(8):
             first_product(acc[i], i, 0)
         interleave_shared(d_mix[1], d_raw[1], V_SHARE[1])
         nc.scalar.copy(out=seg_f32[:], in_=seg_cols[:])
         potential(4)
-        move_words(1, 1)
+        move_scales(0, 1, 2)
         quantize_d(1)
+        move_words(1, 1)
         for i in range(8):
             first_product(acc[i], i, 1)
         interleave_shared(d_mix[2], d_raw[2], V_SHARE[2])
@@ -320,11 +338,11 @@ def tile_scaled_block_projection_s9_kernel(tc, dirs, a_words, a_scales, pot, rho
         move_words(1, 2)
         quantize_d(3)
         move_words(1, 3)
-        for i in (0, 1, 4, 5):
+        for i in (0, 1, 2, 4, 5):
             first_product(acc[i], i, 2)
-        for i in (4, 0, 1, 5):
+        for i in (4, 0, 1, 5, 2):
             first_product(acc[i], i, 3)
-        for i in (2, 6, 3, 7):
+        for i in (6, 3, 7):
             first_product(acc[i], i, 2)
             first_product(acc[i], i, 3)
         move_packed_scales()
@@ -348,9 +366,8 @@ def tile_scaled_block_projection_s9_kernel(tc, dirs, a_words, a_scales, pot, rho
             whole_tile(i, (4, 0, 1, 5)[i - 8])
             if i == 9:
                 move_late_words(3)
-            if i == 11:
-                quantize_w(1)
             drain(i)
+        quantize_w(1)
         for i in range(12, 16):
             whole_tile(i, (2, 6, 3, 7)[i - 12])
             if i == 13:

@@ -30,7 +30,7 @@ UNMOVED = (0,)
 V_SHARE = (320, 320, 256, 192)
 V_URGENT = 320
 WARM_UPS = 4
-V_W2 = 192
+V_W2 = 256
 SIDE = (4, 5, 6)
 
 
@@ -272,10 +272,9 @@ def tile_scaled_block_projection_s9_kernel(tc, dirs, a_words, a_scales, pot, rho
                 first_product(acc[i], i, g)
 
         zero(seg_rows[:])
-        zero(s_early[0][:].rearrange("p g n -> p (g n)"))
         zeros = s_late[:].rearrange("p x g n -> p (x g n)")
         zero(zeros)
-        zero(s_early[1][:].rearrange("p g n -> p (g n)"))
+        zero(s_early[0][:].rearrange("p g n -> p (g n)"))
         nc.scalar.copy(out=nat_rows[:], in_=zeros[:, 0 : 2 * QUAD].bitcast(BF16))
         nc.vector.quantize_mx(out=idle_codes[1][:].bitcast(E5M2X4), scales=idle_scales[1][:], in_=zeros.bitcast(BF16))
         nc.vector.quantize_mx(
@@ -291,12 +290,13 @@ def tile_scaled_block_projection_s9_kernel(tc, dirs, a_words, a_scales, pot, rho
                 start=True,
                 stop=True,
             )
+        zero(s_early[1][:].rearrange("p g n -> p (g n)"))
         zero(s_packed[:].rearrange("p x n -> p (x n)"))
 
         load_d(0)
         load_seg()
-        load_early_scales(0)
         load_a_early(0)
+        load_early_scales(0)
         load_d(1)
         load_a_early(1)
         load_d(2)
@@ -323,7 +323,6 @@ def tile_scaled_block_projection_s9_kernel(tc, dirs, a_words, a_scales, pot, rho
             first_product(acc[i], i, 0)
         interleave_shared(d_mix[1], d_raw[1], V_SHARE[1])
         nc.scalar.copy(out=seg_f32[:], in_=seg_cols[:])
-        potential(4)
         move_scales(0, 1, 2)
         quantize_d(1)
         move_words(1, 1)
@@ -331,18 +330,18 @@ def tile_scaled_block_projection_s9_kernel(tc, dirs, a_words, a_scales, pot, rho
             first_product(acc[i], i, 1)
         interleave_shared(d_mix[2], d_raw[2], V_SHARE[2])
         interleave_shared(d_mix[3], d_raw[3], V_SHARE[3])
-        for i in SIDE[1:]:
+        for i in SIDE:
             potential(i)
         quantize_d(2)
         move_scales(1)
         move_words(1, 2)
         quantize_d(3)
         move_words(1, 3)
-        for i in (0, 1, 2, 4, 5):
+        for i in (0, 1, 2, 3, 4, 5):
             first_product(acc[i], i, 2)
-        for i in (4, 0, 1, 5, 2):
+        for i in (4, 0, 1, 5, 2, 3):
             first_product(acc[i], i, 3)
-        for i in (6, 3, 7):
+        for i in (6, 7):
             first_product(acc[i], i, 2)
             first_product(acc[i], i, 3)
         move_packed_scales()
@@ -369,7 +368,7 @@ def tile_scaled_block_projection_s9_kernel(tc, dirs, a_words, a_scales, pot, rho
             drain(i)
         quantize_w(1)
         for i in range(12, 16):
-            whole_tile(i, (2, 6, 3, 7)[i - 12])
+            whole_tile(i, (2, 3, 6, 7)[i - 12])
             if i == 13:
                 interleave_shared(w_mix[2], w_raw[2], V_W2)
             if i == 14:

@@ -29,7 +29,6 @@ MOVED = (1, 2, 3)
 UNMOVED = (0,)
 V_SHARE = (320, 320, 256, 192)
 V_URGENT = 320
-WARM_UPS = 4
 V_W2 = 256
 SIDE = (4, 5, 6)
 
@@ -65,8 +64,6 @@ def tile_scaled_block_projection_s9_kernel(tc, dirs, a_words, a_scales, pot, rho
         s_packed = sb([P, 2, G], U8, "s_packed")
         s_packed_moved = sb([P, 2, G], U8, "s_packed_moved")
         s_late = sb([P, 2, len(GROUPS), G], U8, "s_late")
-        idle_codes = [sb([P, n], U32, "idle_codes%d" % n) for n in (P, B)]
-        idle_scales = [sb([P, n], U8, "idle_scales%d" % n) for n in (P, B)]
         nat_rows = sb([P, QUAD], BF16, "nat_rows")
         nat_cols = sb([P, QUAD], BF16, "nat_cols")
         seg_rows = sb([P, P], BF16, "seg_rows")
@@ -276,20 +273,6 @@ def tile_scaled_block_projection_s9_kernel(tc, dirs, a_words, a_scales, pot, rho
         zero(zeros)
         zero(s_early[0][:].rearrange("p g n -> p (g n)"))
         nc.scalar.copy(out=nat_rows[:], in_=zeros[:, 0 : 2 * QUAD].bitcast(BF16))
-        nc.vector.quantize_mx(out=idle_codes[1][:].bitcast(E5M2X4), scales=idle_scales[1][:], in_=zeros.bitcast(BF16))
-        nc.vector.quantize_mx(
-            out=idle_codes[0][:].bitcast(E4M3X4), scales=idle_scales[0][:], in_=zeros[:, 0 : 2 * G].bitcast(BF16)
-        )
-        for w in range(WARM_UPS):
-            nc.tensor.matmul_mx(
-                out=bank(7 - w)[:],
-                lhsT=idle_codes[0][:].bitcast(E4M3X4),
-                lhsT_scale=idle_scales[0][:],
-                rhs=idle_codes[1][:].bitcast(E5M2X4),
-                rhs_scale=idle_scales[1][:],
-                start=True,
-                stop=True,
-            )
         zero(s_early[1][:].rearrange("p g n -> p (g n)"))
         zero(s_packed[:].rearrange("p x n -> p (x n)"))
 

@@ -27,10 +27,10 @@ LAST = len(GROUPS) - 1
 HALF = K // 2
 MOVED = (1, 2, 3)
 UNMOVED = (0,)
-V_SHARE = (320, 320, 256, 192)
-V_URGENT = 320
-V_W2 = 256
-SIDE = (4, 5, 6)
+V_D = (352, 352, 320, 256)
+SIDE = (6, 7)
+P_W2 = 256
+P_PIECE = 128
 
 
 def tile_scaled_block_projection_s9_kernel(tc, dirs, a_words, a_scales, pot, rho, out):
@@ -52,13 +52,15 @@ def tile_scaled_block_projection_s9_kernel(tc, dirs, a_words, a_scales, pot, rho
         d_scales = [sb([P, B], U8, "d_scales%d" % g) for g in GROUPS]
         d_nat = [sb([P, 2, B], BF16, "d_nat%d" % x) for x in (0, 1)]
         w_nat = {j: [sb([P, B], BF16, "w_nat%d_%d" % (j, u)) for u in range(SLOTS)] for j in UNMOVED}
-        w_raw = [sb([P, SLOTS, B], BF16, "w_raw%d" % j) for j in GROUPS]
+        w_raw = [sb([P, SLOTS, B], BF16, "w_raw%d" % j) for j in range(LAST)]
+        w_last = sb([P, 2, SLOTS, B // 2], BF16, "w_last")
         w_mix = [sb([P, B, SLOTS], BF16, "w_mix%d" % j) for j in GROUPS]
         w_codes = [sb([P, B], U32, "w_codes%d" % j) for j in GROUPS]
         w_scales = [sb([P, B], U8, "w_scales%d" % j) for j in GROUPS]
         a_early = [sb([P, 2 * HALF], U8, "a_early%d" % g) for g in GROUPS]
         a_late = {j: sb([P, len(GROUPS), 2 * G], U8, "a_late%d" % j) for j in (2, 3)}
-        a_moved = {j: sb([P, len(GROUPS), 2 * G], U8, "a_moved%d" % j) for j in MOVED}
+        a_moved = {1: sb([P, len(GROUPS), 2 * G], U8, "a_moved1")}
+        a_tile = {j: [sb([P, len(GROUPS), 2 * P], U8, "a_tile%d_%d" % (j, t)) for t in range(SLOTS)] for j in (2, 3)}
         s_early = [sb([P, 2, HALF], U8, "s_early%d" % x) for x in (0, 1)]
         s_one = [sb([P, 2, G], U8, "s_one%d" % x) for x in (0, 1)]
         s_packed = sb([P, 2, G], U8, "s_packed")
@@ -148,6 +150,9 @@ def tile_scaled_block_projection_s9_kernel(tc, dirs, a_words, a_scales, pot, rho
                 in_=raw[:, :, lo:hi].rearrange("p t (c i) -> p c t i", i=4),
             )
 
+        def interleave_last(copy, x, lo, hi):
+            interleave(copy, w_mix[LAST][:, x * B // 2 : (x + 1) * B // 2, :], w_last[:, x], lo, hi)
+
         def interleave_shared(mix, raw, v_cols):
             interleave(nc.vector.tensor_copy, mix, raw, 0, v_cols)
             interleave(nc.scalar.copy, mix, raw, v_cols, B)
@@ -166,15 +171,15 @@ def tile_scaled_block_projection_s9_kernel(tc, dirs, a_words, a_scales, pot, rho
             return s_one[g // 2][:, g % 2, :] if j == 1 else s_late[:, j - 2, g, :]
 
         def move_words(j, g):
-            nc.vector.tensor_copy(
+            nc.scalar.copy(
                 out=a_moved[j][:, g, :].bitcast(U16).rearrange("p (t m) -> p t m", t=SLOTS),
                 in_=loaded_words(j, g).bitcast(U16).rearrange("p (m t) -> p t m", t=SLOTS),
             )
 
-        def move_late_words(j):
-            nc.vector.tensor_copy(
-                out=a_moved[j][:].bitcast(U16).rearrange("p g (t m) -> p g t m", t=SLOTS),
-                in_=a_late[j][:].bitcast(U16).rearrange("p g (m t) -> p g t m", t=SLOTS),
+        def move_tile_words(j, t):
+            nc.scalar.copy(
+                out=a_tile[j][t][:].bitcast(U16),
+                in_=a_late[j][:].bitcast(U16).rearrange("p g (m t) -> p t g m", t=SLOTS)[:, t],
             )
 
         def move_scales(x, lo=0, hi=2):
@@ -183,28 +188,36 @@ def tile_scaled_block_projection_s9_kernel(tc, dirs, a_words, a_scales, pot, rho
                 in_=s_early[x][:, lo:hi, G:].rearrange("p g (m t) -> p g t m", t=SLOTS),
             )
 
-        def first_product(acc, i, g):
+        def first_product(acc, i, g, lo=0, hi=B, start=None):
             j, u = divmod(i, SLOTS)
-            words = a_moved[j][:, g, :] if j in MOVED else loaded_words(j, g)
-            scales = plane(j, g)
             c = P * u
+            if j < 2:
+                words = (a_moved[j][:, g, :] if j in MOVED else loaded_words(j, g))[:, 2 * c : 2 * (c + P)]
+            else:
+                words = a_tile[j][u][:, g, :]
             nc.tensor.matmul_mx(
-                out=acc[:],
-                lhsT=words[:, 2 * c : 2 * (c + P)].bitcast(E2M1X4),
-                lhsT_scale=scales[:, c : c + P],
-                rhs=d_codes[g][:].bitcast(E4M3X4),
-                rhs_scale=d_scales[g][:],
-                start=(g == 0),
+                out=acc[:, lo:hi],
+                lhsT=words.bitcast(E2M1X4),
+                lhsT_scale=plane(j, g)[:, c : c + P],
+                rhs=d_codes[g][:, lo:hi].bitcast(E4M3X4),
+                rhs_scale=d_scales[g][:, lo:hi],
+                start=(g == 0) if start is None else start,
                 stop=(g == LAST),
             )
 
-        def drain(i):
+        def drain(acc, i, lo=0, hi=B):
             j, u = divmod(i, SLOTS)
             if j in MOVED:
-                dst, src, factor = w_raw[j][:, u, :], d_raw[j][:, u, :], seg_cols[:, u, 8 * j : 8 * j + 1]
+                src, factor = d_raw[j][:, u, lo:hi], seg_cols[:, u, 8 * j : 8 * j + 1]
             else:
-                dst, src, factor = w_nat[j][u][:], d_nat[u // 2][:, u % 2, :], nat_cols[:, 8 * u : 8 * u + 1]
-            nc.vector.scalar_tensor_tensor(out=dst, in0=src, scalar=factor, in1=acc[i][:], op0=MULT, op1=ADD)
+                src, factor = d_nat[u // 2][:, u % 2, :], nat_cols[:, 8 * u : 8 * u + 1]
+            sums_in = acc[:, lo:hi]
+            if j == LAST:
+                dst = w_last[:, 2 * lo // B : 2 * hi // B, u, :]
+                src, sums_in = (x.rearrange("p (x b) -> p x b", b=B // 2) for x in (src, sums_in))
+            else:
+                dst = w_raw[j][:, u, :] if j in MOVED else w_nat[j][u][:]
+            nc.vector.scalar_tensor_tensor(out=dst, in0=src, scalar=factor, in1=sums_in, op0=MULT, op1=ADD)
             if j in UNMOVED:
                 nc.sync.dma_start(out=w_raw[j][QUAD * u : QUAD * (u + 1), :, :], in_=w_nat[j][u][:])
 
@@ -219,38 +232,47 @@ def tile_scaled_block_projection_s9_kernel(tc, dirs, a_words, a_scales, pot, rho
             nc.scalar.copy(out=sums[i][:], in_=acc[i][:])
             nc.gpsimd.tensor_tensor(out=w_raw[j][:, u, :], in0=sums[i][:], in1=pot_d[i][:], op=ADD)
 
-        def second_product(acc, m, j, start, stop):
+        def second_product(acc, m, j, lo, hi, start, stop):
             sl = slice(P * m, P * (m + 1))
             nc.tensor.matmul_mx(
-                out=acc[:],
+                out=acc[:, lo:hi],
                 lhsT=d_codes[j][:, sl].bitcast(E4M3X4),
                 lhsT_scale=d_scales[j][:, sl],
-                rhs=w_codes[j][:].bitcast(E5M2X4),
-                rhs_scale=w_scales[j][:],
+                rhs=w_codes[j][:, lo:hi].bitcast(E5M2X4),
+                rhs_scale=w_scales[j][:, lo:hi],
                 start=start,
                 stop=stop,
             )
 
-        def finish(acc, m):
-            res = sb([P, B], F32, "res%d" % m)
+        def finish(acc, m, lo, hi):
+            res = sb([P, hi - lo], F32, "res%d_%d" % (m, lo))
             nc.vector.scalar_tensor_tensor(
-                out=res[:], in0=acc[:], scalar=nat_cols[:, 8 * m + 1 : 8 * m + 2], in1=rho_all[:], op0=MULT, op1=MULT
+                out=res[:],
+                in0=acc[:, lo:hi],
+                scalar=nat_cols[:, 8 * m + 1 : 8 * m + 2],
+                in1=rho_all[:, lo:hi],
+                op0=MULT,
+                op1=MULT,
             )
-            nc.sync.dma_start(out=out[P * m : P * (m + 1), :], in_=res[:])
+            nc.sync.dma_start(out=out[P * m : P * (m + 1), lo:hi], in_=res[:])
 
-        def quantize_halves(codes, scales, mix, fmt):
-            for lo in (0, B // 2):
-                hi = lo + B // 2
-                nc.vector.quantize_mx(
-                    out=codes[:, lo:hi].bitcast(fmt),
-                    scales=scales[:, lo:hi],
-                    in_=mix[:, lo:hi, :].rearrange("p b t -> p (b t)"),
+        def quantize_part(codes, scales, mix, fmt, lo, hi):
+            nc.vector.quantize_mx(
+                out=codes[:, lo:hi].bitcast(fmt),
+                scales=scales[:, lo:hi],
+                in_=mix[:, lo:hi, :].rearrange("p b t -> p (b t)"),
+            )
+
+        def interleave_pool(j, lo, hi):
+            for c in range(lo, hi, P_PIECE):
+                nc.gpsimd.tensor_scalar(
+                    out=w_mix[j][:, c : c + P_PIECE, :],
+                    in0=w_raw[j][:, :, c : c + P_PIECE].rearrange("p t b -> p b t"),
+                    scalar1=1.0,
+                    scalar2=0.0,
+                    op0=MULT,
+                    op1=ADD,
                 )
-
-        def interleave_urgent(mix, raw):
-            interleave(nc.vector.tensor_copy, mix, raw, 0, B // 2)
-            interleave(nc.vector.tensor_copy, mix, raw, B // 2, V_URGENT)
-            interleave(nc.scalar.copy, mix, raw, V_URGENT, B)
 
         def quantize_d(g):
             quantize(d_codes[g], d_scales[g], d_mix[g], E4M3X4)
@@ -258,29 +280,27 @@ def tile_scaled_block_projection_s9_kernel(tc, dirs, a_words, a_scales, pot, rho
         def quantize_w(j):
             quantize(w_codes[j], w_scales[j], w_mix[j], E5M2X4)
 
-        def interleave_w(j):
-            interleave(nc.scalar.copy, w_mix[j], w_raw[j], 0, B)
-
         acc = {}
+        HB = B // 2
 
         def whole_tile(i, b):
             acc[i] = bank(b)
             for g in GROUPS:
                 first_product(acc[i], i, g)
 
+        zero(s_early[0][:].rearrange("p g n -> p (g n)"))
         zero(seg_rows[:])
+        zero(s_early[1][:].rearrange("p g n -> p (g n)"))
         zeros = s_late[:].rearrange("p x g n -> p (x g n)")
         zero(zeros)
-        zero(s_early[0][:].rearrange("p g n -> p (g n)"))
-        nc.scalar.copy(out=nat_rows[:], in_=zeros[:, 0 : 2 * QUAD].bitcast(BF16))
-        zero(s_early[1][:].rearrange("p g n -> p (g n)"))
         zero(s_packed[:].rearrange("p x n -> p (x n)"))
+        nc.scalar.copy(out=nat_rows[:], in_=zeros[:, 0 : 2 * QUAD].bitcast(BF16))
 
         load_d(0)
-        load_seg()
         load_a_early(0)
         load_early_scales(0)
         load_d(1)
+        load_seg()
         load_a_early(1)
         load_d(2)
         load_d(3)
@@ -291,81 +311,107 @@ def tile_scaled_block_projection_s9_kernel(tc, dirs, a_words, a_scales, pot, rho
         load_a_late(2)
         load_nat()
         load_d_nat(0)
-        load_d_nat(1)
-        load_a_late(3, 0, 2)
 
         for i in range(8):
             acc[i] = bank(i)
-        interleave_urgent(d_mix[0], d_raw[0])
-        sort_seg()
-        quantize_halves(d_codes[0], d_scales[0], d_mix[0], E4M3X4)
+        v0 = V_D[0] // 2
+        interleave(nc.vector.tensor_copy, d_mix[0], d_raw[0], 0, v0)
+        interleave(nc.scalar.copy, d_mix[0], d_raw[0], v0, HB)
+        interleave(nc.vector.tensor_copy, d_mix[0], d_raw[0], HB, HB + v0)
+        interleave(nc.scalar.copy, d_mix[0], d_raw[0], HB + v0, B)
+        quantize_part(d_codes[0], d_scales[0], d_mix[0], E4M3X4, 0, HB)
+        quantize_part(d_codes[0], d_scales[0], d_mix[0], E4M3X4, HB, B)
         move_words(1, 0)
-        move_scales(0, 0, 1)
-        turn_seg()
-        for i in range(8):
+        move_scales(0)
+        for i in range(4):
+            first_product(acc[i], i, 0, 0, HB)
+        for i in range(4):
+            first_product(acc[i], i, 0, HB, B, False)
+        for i in range(4, 8):
             first_product(acc[i], i, 0)
-        interleave_shared(d_mix[1], d_raw[1], V_SHARE[1])
-        nc.scalar.copy(out=seg_f32[:], in_=seg_cols[:])
-        move_scales(0, 1, 2)
-        quantize_d(1)
+        interleave_shared(d_mix[1], d_raw[1], V_D[1])
         move_words(1, 1)
+        sort_seg()
+        quantize_d(1)
         for i in range(8):
             first_product(acc[i], i, 1)
-        interleave_shared(d_mix[2], d_raw[2], V_SHARE[2])
-        interleave_shared(d_mix[3], d_raw[3], V_SHARE[3])
-        for i in SIDE:
-            potential(i)
+        interleave_shared(d_mix[2], d_raw[2], V_D[2])
+        turn_seg()
         quantize_d(2)
+        interleave_shared(d_mix[3], d_raw[3], V_D[3])
         move_scales(1)
         move_words(1, 2)
-        quantize_d(3)
         move_words(1, 3)
-        for i in (0, 1, 2, 3, 4, 5):
-            first_product(acc[i], i, 2)
-        for i in (4, 0, 1, 5, 2, 3):
-            first_product(acc[i], i, 3)
-        for i in (6, 7):
-            first_product(acc[i], i, 2)
-            first_product(acc[i], i, 3)
+        nc.scalar.copy(out=seg_f32[:], in_=seg_cols[:])
+        potential(6)
+        potential(7)
+        quantize_d(3)
         move_packed_scales()
         spread_packed_scales(2)
-        load_a_late(3, 2, 4)
+        load_d_nat(1)
+        load_a_late(3)
         spread_packed_scales(3)
+        for i in range(4):
+            first_product(acc[i], i, 2)
+        for pair in ((4, 6), (5, 7)):
+            for g in (2, 3):
+                for i in pair:
+                    first_product(acc[i], i, g)
+        for i in range(4):
+            first_product(acc[i], i, 3)
+        drain(acc[4], 4)
         turn_nat()
-        move_late_words(2)
-        side_drain(4)
-        drain(0)
-        drain(1)
-        side_drain(5)
         side_drain(6)
-        for i in (2, 3, 7):
-            drain(i)
+        move_tile_words(2, 0)
+        drain(acc[5], 5)
+        side_drain(7)
+        for t in (1, 2, 3):
+            move_tile_words(2, t)
+        interleave_pool(1, 0, HB)
+        for i in range(4):
+            drain(acc[i], i)
         nc.sync.dma_start(out=rho_some[0:P:8, :], in_=rho.partition_broadcast(P // 8))
         spread_rho()
-        interleave_w(1)
-        interleave_w(0)
-        for i in range(8, 12):
-            whole_tile(i, (4, 0, 1, 5)[i - 8])
-            if i == 9:
-                move_late_words(3)
-            drain(i)
-        quantize_w(1)
-        for i in range(12, 16):
-            whole_tile(i, (2, 3, 6, 7)[i - 12])
+        interleave(nc.scalar.copy, w_mix[1], w_raw[1], HB, B)
+        for t in (0, 1):
+            move_tile_words(3, t)
+        for i, b in zip(range(8, 12), (4, 6, 5, 7)):
+            whole_tile(i, b)
+            if i == 10:
+                quantize_w(1)
+            drain(acc[i], i)
+        interleave_pool(0, 0, HB)
+        interleave(nc.scalar.copy, w_mix[0], w_raw[0], HB, B)
+        for t in (2, 3):
+            move_tile_words(3, t)
+        interleave_pool(2, 0, P_W2)
+        interleave(nc.scalar.copy, w_mix[2], w_raw[2], P_W2, B)
+        halves = ((0, HB), (HB, B))
+        for i in (12, 13):
+            whole_tile(i, i - 12)
             if i == 13:
-                interleave_shared(w_mix[2], w_raw[2], V_W2)
-            if i == 14:
                 quantize_w(0)
-            if i == 15:
-                quantize_w(2)
-            drain(i)
-        h_acc = [bank(b) for b in (4, 0, 1, 5)]
-        for j in (1, 0):
+            drain(acc[i], i)
+        for x, banks in enumerate(((2, 3), (4, 6))):
+            for i, b in zip((14, 15), banks):
+                half = bank(b)
+                for g in GROUPS:
+                    first_product(half, i, g, *halves[x])
+                if (i, x) == (14, 1):
+                    quantize_w(2)
+                drain(half, i, *halves[x])
+            interleave_last(nc.scalar.copy, x, 0, HB)
+        quantize_part(w_codes[3], w_scales[3], w_mix[3], E5M2X4, 0, HB)
+        h_acc = [bank(b) for b in (5, 7, 0, 1)]
+        for j in (1, 0, 2, 3):
             for m in range(4):
-                second_product(h_acc[m], m, j, j == 1, False)
-        interleave_urgent(w_mix[3], w_raw[3])
-        quantize_halves(w_codes[3], w_scales[3], w_mix[3], E5M2X4)
-        for m in range(4):
-            second_product(h_acc[m], m, 2, False, False)
-            second_product(h_acc[m], m, 3, False, True)
-            finish(h_acc[m], m)
+                second_product(h_acc[m], m, j, 0, HB, j == 1, j == 3)
+        finish(h_acc[0], 0, 0, HB)
+        quantize_part(w_codes[3], w_scales[3], w_mix[3], E5M2X4, HB, B)
+        for m in range(1, 4):
+            finish(h_acc[m], m, 0, HB)
+        for m, b in enumerate((2, 3, 4, 6)):
+            h_acc = bank(b)
+            for j in (1, 0, 2, 3):
+                second_product(h_acc, m, j, HB, B, j == 1, j == 3)
+            finish(h_acc, m, HB, B)

@@ -16,7 +16,6 @@ E5M2X4 = mybir.dt.float8_e5m2_x4
 E2M1X4 = mybir.dt.float4_e2m1fn_x4
 MULT = mybir.AluOpType.mult
 ADD = mybir.AluOpType.add
-COPY = mybir.ActivationFunctionType.Copy
 
 P = 128
 QUAD = 32
@@ -25,11 +24,9 @@ G = P * SLOTS
 GROUPS = range(K // G)
 LAST = len(GROUPS) - 1
 HALF = K // 2
-MOVED = (1, 2, 3)
-UNMOVED = (0,)
-V_D = (352, 352, 320, 256)
-SIDE = (6, 7)
-P_W2 = 256
+HB = B // 2
+HALVES = ((0, HB), (HB, B))
+V_D = (352, 320, 320, 320)
 P_PIECE = 128
 
 
@@ -50,38 +47,33 @@ def tile_scaled_block_projection_s9_kernel(tc, dirs, a_words, a_scales, pot, rho
         d_mix = [sb([P, B, SLOTS], BF16, "d_mix%d" % g) for g in GROUPS]
         d_codes = [sb([P, B], U32, "d_codes%d" % g) for g in GROUPS]
         d_scales = [sb([P, B], U8, "d_scales%d" % g) for g in GROUPS]
-        d_nat = [sb([P, 2, B], BF16, "d_nat%d" % x) for x in (0, 1)]
-        w_nat = {j: [sb([P, B], BF16, "w_nat%d_%d" % (j, u)) for u in range(SLOTS)] for j in UNMOVED}
         w_raw = [sb([P, SLOTS, B], BF16, "w_raw%d" % j) for j in range(LAST)]
-        w_last = sb([P, 2, SLOTS, B // 2], BF16, "w_last")
+        w_last = sb([P, 2, SLOTS, HB], BF16, "w_last")
         w_mix = [sb([P, B, SLOTS], BF16, "w_mix%d" % j) for j in GROUPS]
         w_codes = [sb([P, B], U32, "w_codes%d" % j) for j in GROUPS]
         w_scales = [sb([P, B], U8, "w_scales%d" % j) for j in GROUPS]
         a_early = [sb([P, 2 * HALF], U8, "a_early%d" % g) for g in GROUPS]
         a_late = {j: sb([P, len(GROUPS), 2 * G], U8, "a_late%d" % j) for j in (2, 3)}
-        a_moved = {1: sb([P, len(GROUPS), 2 * G], U8, "a_moved1")}
+        a_dealt = {(j, g): sb([P, 2 * G], U8, "a_dealt%d_%d" % (j, g)) for j in (0, 1) for g in GROUPS}
         a_tile = {j: [sb([P, len(GROUPS), 2 * P], U8, "a_tile%d_%d" % (j, t)) for t in range(SLOTS)] for j in (2, 3)}
-        s_early = [sb([P, 2, HALF], U8, "s_early%d" % x) for x in (0, 1)]
-        s_one = [sb([P, 2, G], U8, "s_one%d" % x) for x in (0, 1)]
+        s_early = sb([P, len(GROUPS), HALF], U8, "s_early")
+        s_dealt = [sb([P, 2, G], U8, "s_dealt%d" % g) for g in GROUPS]
         s_packed = sb([P, 2, G], U8, "s_packed")
-        s_packed_moved = sb([P, 2, G], U8, "s_packed_moved")
+        s_packed_dealt = sb([P, 2, G], U8, "s_packed_dealt")
         s_late = sb([P, 2, len(GROUPS), G], U8, "s_late")
-        nat_rows = sb([P, QUAD], BF16, "nat_rows")
-        nat_cols = sb([P, QUAD], BF16, "nat_cols")
+        rho_rows = sb([P, QUAD], BF16, "rho_rows")
+        rho_cols = sb([P, QUAD], BF16, "rho_cols")
         seg_rows = sb([P, P], BF16, "seg_rows")
         seg_slots = sb([P, SLOTS, QUAD], BF16, "seg_slots")
         seg_cols = sb([P, SLOTS, QUAD], BF16, "seg_cols")
-        seg_f32 = sb([P, SLOTS, QUAD], F32, "seg_f32")
-        pot_d = {i: sb([P, B], F32, "pot_d%d" % i) for i in SIDE}
-        sums = {i: sb([P, B], F32, "sums%d" % i) for i in SIDE}
         rho_some = sb([P, B], BF16, "rho_some")
         rho_all = sb([P, B], BF16, "rho_all")
 
-        def load_early_scales(x):
+        def load_early_scales(lo, hi):
             for r in range(4):
                 nc.sync.dma_start(
-                    out=s_early[x][r:P:QUAD, :, :].bitcast(I32),
-                    in_=a_scales[2 * x : 2 * x + 2, r:16:4, 0:HALF].rearrange("g q n -> q g n").bitcast(I32),
+                    out=s_early[r:P:QUAD, lo:hi, :].bitcast(I32),
+                    in_=a_scales[lo:hi, r:16:4, 0:HALF].rearrange("g q n -> q g n").bitcast(I32),
                 )
 
         def load_packed_scales():
@@ -91,43 +83,37 @@ def tile_scaled_block_projection_s9_kernel(tc, dirs, a_words, a_scales, pot, rho
                     in_=a_scales[:, r:16:4, HALF:].rearrange("g q n -> q g n").bitcast(I32),
                 )
 
-        def move_packed_scales():
+        def deal_packed_scales(j):
             nc.vector.tensor_copy(
-                out=s_packed_moved[:].rearrange("p x (t m) -> p x t m", t=SLOTS),
-                in_=s_packed[:].rearrange("p x (m t) -> p x t m", t=SLOTS),
+                out=s_packed_dealt[:, j - 2, :].rearrange("p (t m) -> p t m", t=SLOTS),
+                in_=s_packed[:, j - 2, :].rearrange("p (m t) -> p t m", t=SLOTS),
             )
 
         def spread_packed_scales(j):
             for r in range(4):
                 nc.sync.dma_start(
                     out=s_late[r:P:QUAD, j - 2, :, :].rearrange("q g n -> q (g n)").bitcast(I32),
-                    in_=s_packed_moved[QUAD * r : QUAD * (r + 1) : 2, j - 2, :].bitcast(I32),
+                    in_=s_packed_dealt[QUAD * r : QUAD * (r + 1) : 2, j - 2, :].bitcast(I32),
                 )
 
         def load_a_early(g):
             nc.sync.dma_start(out=a_early[g][:].bitcast(I32), in_=a_words[g][:, 0 : 2 * HALF].bitcast(I32))
 
-        def load_a_late(j, lo=0, hi=len(GROUPS)):
+        def load_a_late(j):
             nc.sync.dma_start(
-                out=a_late[j][:, lo:hi, :].bitcast(I32),
-                in_=a_words[lo:hi, :, 2 * G * j : 2 * G * (j + 1)].rearrange("g p n -> p g n").bitcast(I32),
+                out=a_late[j][:].bitcast(I32),
+                in_=a_words[:, :, 2 * G * j : 2 * G * (j + 1)].rearrange("g p n -> p g n").bitcast(I32),
             )
 
         def load_d(g):
             nc.sync.dma_start(out=d_raw[g][:], in_=dirs[G * g : G * (g + 1), :].rearrange("(p t) b -> p t b", t=SLOTS))
 
-        def load_d_nat(x):
-            rows = dirs[2 * P * x : 2 * P * (x + 1), :]
-            nc.sync.dma_start(out=d_nat[x][:], in_=rows.rearrange("(u p) b -> p u b", p=P))
-
         def load_seg():
             nc.sync.dma_start(out=seg_rows[0:P:8, :], in_=pot.rearrange("(j q x) -> q j x", q=4, x=P))
 
-        def load_nat():
-            nc.sync.dma_start(out=nat_rows[0:P:8, :], in_=pot[0:G].rearrange("(u q c) -> q u c", q=4, c=QUAD))
-            nc.sync.dma_start(out=nat_rows[1:P:8, :], in_=rho.rearrange("(m q c) -> q m c", q=4, c=QUAD))
-
-        def spread_rho():
+        def load_rho():
+            nc.sync.dma_start(out=rho_rows[0:P:8, :], in_=rho.rearrange("(m q c) -> q m c", q=4, c=QUAD))
+            nc.sync.dma_start(out=rho_some[0:P:8, :], in_=rho.partition_broadcast(P // 8))
             nc.sync.dma_start(out=rho_all[:], in_=rho_some[0:P:8, :].unsqueeze(1).to_broadcast([P // 8, 8, B]))
 
         def sort_seg():
@@ -138,9 +124,6 @@ def tile_scaled_block_projection_s9_kernel(tc, dirs, a_words, a_scales, pot, rho
                 out=seg_cols[:].rearrange("p t k -> p (t k)"), in_=seg_slots[:].rearrange("p t c -> p (t c)")
             )
 
-        def turn_nat():
-            nc.vector.transpose(out=nat_cols[:], in_=nat_rows[:])
-
         def zero(tile):
             nc.vector.memset(tile.bitcast(I32), 0)
 
@@ -150,55 +133,63 @@ def tile_scaled_block_projection_s9_kernel(tc, dirs, a_words, a_scales, pot, rho
                 in_=raw[:, :, lo:hi].rearrange("p t (c i) -> p c t i", i=4),
             )
 
-        def interleave_last(copy, x, lo, hi):
-            interleave(copy, w_mix[LAST][:, x * B // 2 : (x + 1) * B // 2, :], w_last[:, x], lo, hi)
+        def interleave_shared(mix, raw, lo, mid, hi):
+            interleave(nc.vector.tensor_copy, mix, raw, lo, mid)
+            interleave(nc.scalar.copy, mix, raw, mid, hi)
 
-        def interleave_shared(mix, raw, v_cols):
-            interleave(nc.vector.tensor_copy, mix, raw, 0, v_cols)
-            interleave(nc.scalar.copy, mix, raw, v_cols, B)
+        def interleave_pool(j, lo, hi):
+            for c in range(lo, hi, P_PIECE):
+                nc.gpsimd.tensor_scalar(
+                    out=w_mix[j][:, c : c + P_PIECE, :],
+                    in0=w_raw[j][:, :, c : c + P_PIECE].rearrange("p t b -> p b t"),
+                    scalar1=1.0,
+                    scalar2=0.0,
+                    op0=MULT,
+                    op1=ADD,
+                )
 
-        def quantize(codes, scales, mix, fmt):
+        def quantize(codes, scales, mix, fmt, lo, hi):
             nc.vector.quantize_mx(
-                out=codes[:].bitcast(fmt), scales=scales[:], in_=mix[:].rearrange("p b t -> p (b t)")
+                out=codes[:, lo:hi].bitcast(fmt),
+                scales=scales[:, lo:hi],
+                in_=mix[:, lo:hi, :].rearrange("p b t -> p (b t)"),
             )
 
-        def loaded_words(j, g):
-            return a_early[g][:, 2 * G * j : 2 * G * (j + 1)] if j < 2 else a_late[j][:, g, :]
+        def quantize_d(g, lo=0, hi=B):
+            quantize(d_codes[g], d_scales[g], d_mix[g], E4M3X4, lo, hi)
 
-        def plane(j, g):
-            if j == 0:
-                return s_early[g // 2][:, g % 2, 0:G]
-            return s_one[g // 2][:, g % 2, :] if j == 1 else s_late[:, j - 2, g, :]
+        def quantize_w(j, lo=0, hi=B):
+            quantize(w_codes[j], w_scales[j], w_mix[j], E5M2X4, lo, hi)
 
-        def move_words(j, g):
+        def deal_words(j, g):
             nc.scalar.copy(
-                out=a_moved[j][:, g, :].bitcast(U16).rearrange("p (t m) -> p t m", t=SLOTS),
-                in_=loaded_words(j, g).bitcast(U16).rearrange("p (m t) -> p t m", t=SLOTS),
+                out=a_dealt[j, g][:].bitcast(U16).rearrange("p (t m) -> p t m", t=SLOTS),
+                in_=a_early[g][:, 2 * G * j : 2 * G * (j + 1)].bitcast(U16).rearrange("p (m t) -> p t m", t=SLOTS),
             )
 
-        def move_tile_words(j, t):
+        def deal_tile_words(j, t):
             nc.scalar.copy(
                 out=a_tile[j][t][:].bitcast(U16),
                 in_=a_late[j][:].bitcast(U16).rearrange("p g (m t) -> p t g m", t=SLOTS)[:, t],
             )
 
-        def move_scales(x, lo=0, hi=2):
+        def deal_scales(g, lo=0, hi=2):
             nc.vector.tensor_copy(
-                out=s_one[x][:, lo:hi, :].rearrange("p g (t m) -> p g t m", t=SLOTS),
-                in_=s_early[x][:, lo:hi, G:].rearrange("p g (m t) -> p g t m", t=SLOTS),
+                out=s_dealt[g][:, lo:hi, :].rearrange("p j (t m) -> p j t m", t=SLOTS),
+                in_=s_early[:, g, G * lo : G * hi].rearrange("p (j m t) -> p j t m", t=SLOTS, m=P),
             )
 
         def first_product(acc, i, g, lo=0, hi=B, start=None):
             j, u = divmod(i, SLOTS)
             c = P * u
             if j < 2:
-                words = (a_moved[j][:, g, :] if j in MOVED else loaded_words(j, g))[:, 2 * c : 2 * (c + P)]
+                words, scales = a_dealt[j, g][:, 2 * c : 2 * (c + P)], s_dealt[g][:, j, c : c + P]
             else:
-                words = a_tile[j][u][:, g, :]
+                words, scales = a_tile[j][u][:, g, :], s_late[:, j - 2, g, c : c + P]
             nc.tensor.matmul_mx(
                 out=acc[:, lo:hi],
                 lhsT=words.bitcast(E2M1X4),
-                lhsT_scale=plane(j, g)[:, c : c + P],
+                lhsT_scale=scales,
                 rhs=d_codes[g][:, lo:hi].bitcast(E4M3X4),
                 rhs_scale=d_scales[g][:, lo:hi],
                 start=(g == 0) if start is None else start,
@@ -207,30 +198,15 @@ def tile_scaled_block_projection_s9_kernel(tc, dirs, a_words, a_scales, pot, rho
 
         def drain(acc, i, lo=0, hi=B):
             j, u = divmod(i, SLOTS)
-            if j in MOVED:
-                src, factor = d_raw[j][:, u, lo:hi], seg_cols[:, u, 8 * j : 8 * j + 1]
-            else:
-                src, factor = d_nat[u // 2][:, u % 2, :], nat_cols[:, 8 * u : 8 * u + 1]
-            sums_in = acc[:, lo:hi]
+            src, sums = d_raw[j][:, u, lo:hi], acc[:, lo:hi]
             if j == LAST:
-                dst = w_last[:, 2 * lo // B : 2 * hi // B, u, :]
-                src, sums_in = (x.rearrange("p (x b) -> p x b", b=B // 2) for x in (src, sums_in))
+                dst = w_last[:, lo // HB : hi // HB, u, :]
+                src, sums = (x.rearrange("p (x b) -> p x b", b=HB) for x in (src, sums))
             else:
-                dst = w_raw[j][:, u, :] if j in MOVED else w_nat[j][u][:]
-            nc.vector.scalar_tensor_tensor(out=dst, in0=src, scalar=factor, in1=sums_in, op0=MULT, op1=ADD)
-            if j in UNMOVED:
-                nc.sync.dma_start(out=w_raw[j][QUAD * u : QUAD * (u + 1), :, :], in_=w_nat[j][u][:])
-
-        def potential(i):
-            j, u = divmod(i, SLOTS)
-            nc.scalar.activation(
-                out=pot_d[i][:], in_=d_raw[j][:, u, :], func=COPY, scale=seg_f32[:, u, 8 * j : 8 * j + 1]
+                dst = w_raw[j][:, u, :]
+            nc.vector.scalar_tensor_tensor(
+                out=dst, in0=src, scalar=seg_cols[:, u, 8 * j : 8 * j + 1], in1=sums, op0=MULT, op1=ADD
             )
-
-        def side_drain(i):
-            j, u = divmod(i, SLOTS)
-            nc.scalar.copy(out=sums[i][:], in_=acc[i][:])
-            nc.gpsimd.tensor_tensor(out=w_raw[j][:, u, :], in0=sums[i][:], in1=pot_d[i][:], op=ADD)
 
         def second_product(acc, m, j, lo, hi, start, stop):
             sl = slice(P * m, P * (m + 1))
@@ -249,169 +225,116 @@ def tile_scaled_block_projection_s9_kernel(tc, dirs, a_words, a_scales, pot, rho
             nc.vector.scalar_tensor_tensor(
                 out=res[:],
                 in0=acc[:, lo:hi],
-                scalar=nat_cols[:, 8 * m + 1 : 8 * m + 2],
+                scalar=rho_cols[:, 8 * m : 8 * m + 1],
                 in1=rho_all[:, lo:hi],
                 op0=MULT,
                 op1=MULT,
             )
             nc.sync.dma_start(out=out[P * m : P * (m + 1), lo:hi], in_=res[:])
 
-        def quantize_part(codes, scales, mix, fmt, lo, hi):
-            nc.vector.quantize_mx(
-                out=codes[:, lo:hi].bitcast(fmt),
-                scales=scales[:, lo:hi],
-                in_=mix[:, lo:hi, :].rearrange("p b t -> p (b t)"),
-            )
-
-        def interleave_pool(j, lo, hi):
-            for c in range(lo, hi, P_PIECE):
-                nc.gpsimd.tensor_scalar(
-                    out=w_mix[j][:, c : c + P_PIECE, :],
-                    in0=w_raw[j][:, :, c : c + P_PIECE].rearrange("p t b -> p b t"),
-                    scalar1=1.0,
-                    scalar2=0.0,
-                    op0=MULT,
-                    op1=ADD,
-                )
-
-        def quantize_d(g):
-            quantize(d_codes[g], d_scales[g], d_mix[g], E4M3X4)
-
-        def quantize_w(j):
-            quantize(w_codes[j], w_scales[j], w_mix[j], E5M2X4)
-
         acc = {}
-        HB = B // 2
 
         def whole_tile(i, b):
             acc[i] = bank(b)
             for g in GROUPS:
                 first_product(acc[i], i, g)
 
-        zero(s_early[0][:].rearrange("p g n -> p (g n)"))
+        zero(s_early[:, 0, :])
+        zero(s_early[:, 1:, :].rearrange("p g n -> p (g n)"))
         zero(seg_rows[:])
-        zero(s_early[1][:].rearrange("p g n -> p (g n)"))
         zeros = s_late[:].rearrange("p x g n -> p (x g n)")
         zero(zeros)
         zero(s_packed[:].rearrange("p x n -> p (x n)"))
-        nc.scalar.copy(out=nat_rows[:], in_=zeros[:, 0 : 2 * QUAD].bitcast(BF16))
+        nc.scalar.copy(out=rho_rows[:], in_=zeros[:, 0 : 2 * QUAD].bitcast(BF16))
 
-        load_d(0)
         load_a_early(0)
-        load_early_scales(0)
+        load_early_scales(0, 1)
+        load_d(0)
         load_d(1)
         load_seg()
         load_a_early(1)
+        load_early_scales(1, 2)
         load_d(2)
-        load_d(3)
-        load_early_scales(1)
         load_a_early(2)
+        load_early_scales(2, 4)
+        load_d(3)
         load_a_early(3)
         load_packed_scales()
         load_a_late(2)
-        load_nat()
-        load_d_nat(0)
 
         for i in range(8):
             acc[i] = bank(i)
-        v0 = V_D[0] // 2
-        interleave(nc.vector.tensor_copy, d_mix[0], d_raw[0], 0, v0)
-        interleave(nc.scalar.copy, d_mix[0], d_raw[0], v0, HB)
-        interleave(nc.vector.tensor_copy, d_mix[0], d_raw[0], HB, HB + v0)
-        interleave(nc.scalar.copy, d_mix[0], d_raw[0], HB + v0, B)
-        quantize_part(d_codes[0], d_scales[0], d_mix[0], E4M3X4, 0, HB)
-        quantize_part(d_codes[0], d_scales[0], d_mix[0], E4M3X4, HB, B)
-        move_words(1, 0)
-        move_scales(0)
-        for i in range(4):
-            first_product(acc[i], i, 0, 0, HB)
-        for i in range(4):
-            first_product(acc[i], i, 0, HB, B, False)
-        for i in range(4, 8):
-            first_product(acc[i], i, 0)
-        interleave_shared(d_mix[1], d_raw[1], V_D[1])
-        move_words(1, 1)
-        sort_seg()
-        quantize_d(1)
-        for i in range(8):
-            first_product(acc[i], i, 1)
-        interleave_shared(d_mix[2], d_raw[2], V_D[2])
-        turn_seg()
-        quantize_d(2)
-        interleave_shared(d_mix[3], d_raw[3], V_D[3])
-        move_scales(1)
-        move_words(1, 2)
-        move_words(1, 3)
-        nc.scalar.copy(out=seg_f32[:], in_=seg_cols[:])
-        potential(6)
-        potential(7)
-        quantize_d(3)
-        move_packed_scales()
+        deal_words(0, 0)
+        deal_words(1, 0)
+        deal_scales(0)
+        for lo, hi in HALVES:
+            interleave_shared(d_mix[0], d_raw[0], lo, lo + V_D[0] // 2, hi)
+        for lo, hi in HALVES:
+            quantize_d(0, lo, hi)
+            for i in range(8):
+                first_product(acc[i], i, 0, lo, hi, lo == 0)
+        for g in (1, 2, 3):
+            interleave_shared(d_mix[g], d_raw[g], 0, V_D[g], B)
+            deal_scales(g, 0, 1 if g == LAST else 2)
+            deal_words(0, g)
+            deal_words(1, g)
+            if g == LAST:
+                deal_packed_scales(2)
+            quantize_d(g)
+            if g == LAST:
+                deal_scales(g, 1, 2)
+            if g == 1:
+                sort_seg()
+            if g == 2:
+                turn_seg()
+            for i in range(8):
+                first_product(acc[i], i, g)
         spread_packed_scales(2)
-        load_d_nat(1)
+        deal_packed_scales(3)
         load_a_late(3)
         spread_packed_scales(3)
-        for i in range(4):
-            first_product(acc[i], i, 2)
-        for pair in ((4, 6), (5, 7)):
-            for g in (2, 3):
-                for i in pair:
-                    first_product(acc[i], i, g)
-        for i in range(4):
-            first_product(acc[i], i, 3)
-        drain(acc[4], 4)
-        turn_nat()
-        side_drain(6)
-        move_tile_words(2, 0)
-        drain(acc[5], 5)
-        side_drain(7)
-        for t in (1, 2, 3):
-            move_tile_words(2, t)
-        interleave_pool(1, 0, HB)
+        load_rho()
+        for t in range(SLOTS):
+            deal_tile_words(2, t)
         for i in range(4):
             drain(acc[i], i)
-        nc.sync.dma_start(out=rho_some[0:P:8, :], in_=rho.partition_broadcast(P // 8))
-        spread_rho()
-        interleave(nc.scalar.copy, w_mix[1], w_raw[1], HB, B)
-        for t in (0, 1):
-            move_tile_words(3, t)
-        for i, b in zip(range(8, 12), (4, 6, 5, 7)):
-            whole_tile(i, b)
-            if i == 10:
-                quantize_w(1)
+        interleave_pool(0, 0, B)
+        for i in range(4, 8):
             drain(acc[i], i)
-        interleave_pool(0, 0, HB)
-        interleave(nc.scalar.copy, w_mix[0], w_raw[0], HB, B)
-        for t in (2, 3):
-            move_tile_words(3, t)
-        interleave_pool(2, 0, P_W2)
-        interleave(nc.scalar.copy, w_mix[2], w_raw[2], P_W2, B)
-        halves = ((0, HB), (HB, B))
+        for t in range(SLOTS):
+            deal_tile_words(3, t)
+        interleave(nc.scalar.copy, w_mix[1], w_raw[1], 0, B)
+        for i in range(8, 12):
+            whole_tile(i, i - 8)
+            drain(acc[i], i)
+        interleave(nc.scalar.copy, w_mix[2], w_raw[2], 0, HB)
+        interleave(nc.scalar.copy, w_mix[2], w_raw[2], HB, B)
+        quantize_w(0)
         for i in (12, 13):
-            whole_tile(i, i - 12)
-            if i == 13:
-                quantize_w(0)
+            whole_tile(i, i - 8)
             drain(acc[i], i)
-        for x, banks in enumerate(((2, 3), (4, 6))):
+            quantize_w(i - 11, 0, HB)
+        for x, banks in enumerate(((6, 7), (0, 1))):
             for i, b in zip((14, 15), banks):
                 half = bank(b)
                 for g in GROUPS:
-                    first_product(half, i, g, *halves[x])
-                if (i, x) == (14, 1):
-                    quantize_w(2)
-                drain(half, i, *halves[x])
-            interleave_last(nc.scalar.copy, x, 0, HB)
-        quantize_part(w_codes[3], w_scales[3], w_mix[3], E5M2X4, 0, HB)
-        h_acc = [bank(b) for b in (5, 7, 0, 1)]
-        for j in (1, 0, 2, 3):
+                    first_product(half, i, g, *HALVES[x])
+                drain(half, i, *HALVES[x])
+            interleave(nc.scalar.copy, w_mix[LAST][:, HB * x : HB * (x + 1), :], w_last[:, x], 0, HB)
+        nc.vector.transpose(out=rho_cols[:], in_=rho_rows[:])
+        quantize_w(1, HB, B)
+        quantize_w(LAST, 0, HB)
+        quantize_w(2, HB, B)
+        h_acc = [bank(b) for b in (2, 3, 4, 5)]
+        for j in GROUPS:
             for m in range(4):
-                second_product(h_acc[m], m, j, 0, HB, j == 1, j == 3)
+                second_product(h_acc[m], m, j, 0, HB, j == 0, j == LAST)
         finish(h_acc[0], 0, 0, HB)
-        quantize_part(w_codes[3], w_scales[3], w_mix[3], E5M2X4, HB, B)
+        quantize_w(LAST, HB, B)
         for m in range(1, 4):
             finish(h_acc[m], m, 0, HB)
-        for m, b in enumerate((2, 3, 4, 6)):
+        for m, b in enumerate((6, 7, 0, 1)):
             h_acc = bank(b)
-            for j in (1, 0, 2, 3):
-                second_product(h_acc, m, j, HB, B, j == 1, j == 3)
+            for j in GROUPS:
+                second_product(h_acc, m, j, HB, B, j == 0, j == LAST)
             finish(h_acc, m, HB, B)

@@ -27,6 +27,7 @@ HALF = K // 2
 HB = B // 2
 HALVES = ((0, HB), (HB, B))
 V_D = (352, 320, 320, 320)
+WARM_UPS = 5
 P_PIECE = 128
 
 
@@ -61,6 +62,8 @@ def tile_scaled_block_projection_s9_kernel(tc, dirs, a_words, a_scales, pot, rho
         s_packed = sb([P, 2, G], U8, "s_packed")
         s_packed_dealt = sb([P, 2, G], U8, "s_packed_dealt")
         s_late = sb([P, 2, len(GROUPS), G], U8, "s_late")
+        idle_codes = sb([P, B], U32, "idle_codes")
+        idle_scales = sb([P, B], U8, "idle_scales")
         rho_rows = sb([P, QUAD], BF16, "rho_rows")
         rho_cols = sb([P, QUAD], BF16, "rho_cols")
         seg_rows = sb([P, P], BF16, "seg_rows")
@@ -244,6 +247,7 @@ def tile_scaled_block_projection_s9_kernel(tc, dirs, a_words, a_scales, pot, rho
         zero(seg_rows[:])
         zeros = s_late[:].rearrange("p x g n -> p (x g n)")
         zero(zeros)
+        nc.vector.quantize_mx(out=idle_codes[:].bitcast(E4M3X4), scales=idle_scales[:], in_=zeros.bitcast(BF16))
         zero(s_packed[:].rearrange("p x n -> p (x n)"))
         nc.scalar.copy(out=rho_rows[:], in_=zeros[:, 0 : 2 * QUAD].bitcast(BF16))
 
@@ -262,6 +266,16 @@ def tile_scaled_block_projection_s9_kernel(tc, dirs, a_words, a_scales, pot, rho
         load_packed_scales()
         load_a_late(2)
 
+        for w in range(WARM_UPS):
+            nc.tensor.matmul_mx(
+                out=bank(7 - w)[:],
+                lhsT=a_early[0][:, 0 : 2 * P].bitcast(E2M1X4),
+                lhsT_scale=idle_scales[:, 0:P],
+                rhs=idle_codes[:].bitcast(E4M3X4),
+                rhs_scale=idle_scales[:],
+                start=True,
+                stop=True,
+            )
         for i in range(8):
             acc[i] = bank(i)
         deal_words(0, 0)

@@ -27,7 +27,9 @@ HALF = K // 2
 HB = B // 2
 HALVES = ((0, HB), (HB, B))
 V_D = (352, 320, 320, 320)
-WARM_UPS = 5
+WARM_UPS = (3, 2)
+V_LAST = 96
+P_W0 = 384
 P_PIECE = 128
 
 
@@ -53,7 +55,8 @@ def tile_scaled_block_projection_s9_kernel(tc, dirs, a_words, a_scales, pot, rho
         w_mix = [sb([P, B, SLOTS], BF16, "w_mix%d" % j) for j in GROUPS]
         w_codes = [sb([P, B], U32, "w_codes%d" % j) for j in GROUPS]
         w_scales = [sb([P, B], U8, "w_scales%d" % j) for j in GROUPS]
-        a_early = [sb([P, 2 * HALF], U8, "a_early%d" % g) for g in GROUPS]
+        a_first = [sb([P, 2 * G], U8, "a_first%d" % j) for j in (0, 1)]
+        a_early = {g: sb([P, 2 * HALF], U8, "a_early%d" % g) for g in GROUPS[1:]}
         a_late = {j: sb([P, len(GROUPS), 2 * G], U8, "a_late%d" % j) for j in (2, 3)}
         a_dealt = {(j, g): sb([P, 2 * G], U8, "a_dealt%d_%d" % (j, g)) for j in (0, 1) for g in GROUPS}
         a_tile = {j: [sb([P, len(GROUPS), 2 * P], U8, "a_tile%d_%d" % (j, t)) for t in range(SLOTS)] for j in (2, 3)}
@@ -62,8 +65,8 @@ def tile_scaled_block_projection_s9_kernel(tc, dirs, a_words, a_scales, pot, rho
         s_packed = sb([P, 2, G], U8, "s_packed")
         s_packed_dealt = sb([P, 2, G], U8, "s_packed_dealt")
         s_late = sb([P, 2, len(GROUPS), G], U8, "s_late")
-        idle_codes = sb([P, B], U32, "idle_codes")
-        idle_scales = sb([P, B], U8, "idle_scales")
+        idle_codes = [sb([P, n], U32, "idle_codes%d" % n) for n in (P, B)]
+        idle_scales = [sb([P, n], U8, "idle_scales%d" % n) for n in (P, B)]
         rho_rows = sb([P, QUAD], BF16, "rho_rows")
         rho_cols = sb([P, QUAD], BF16, "rho_cols")
         seg_rows = sb([P, P], BF16, "seg_rows")
@@ -98,6 +101,9 @@ def tile_scaled_block_projection_s9_kernel(tc, dirs, a_words, a_scales, pot, rho
                     out=s_late[r:P:QUAD, j - 2, :, :].rearrange("q g n -> q (g n)").bitcast(I32),
                     in_=s_packed_dealt[QUAD * r : QUAD * (r + 1) : 2, j - 2, :].bitcast(I32),
                 )
+
+        def load_a_first(j):
+            nc.sync.dma_start(out=a_first[j][:].bitcast(I32), in_=a_words[0][:, 2 * G * j : 2 * G * (j + 1)].bitcast(I32))
 
         def load_a_early(g):
             nc.sync.dma_start(out=a_early[g][:].bitcast(I32), in_=a_words[g][:, 0 : 2 * HALF].bitcast(I32))
@@ -165,9 +171,10 @@ def tile_scaled_block_projection_s9_kernel(tc, dirs, a_words, a_scales, pot, rho
             quantize(w_codes[j], w_scales[j], w_mix[j], E5M2X4, lo, hi)
 
         def deal_words(j, g):
+            words = a_first[j][:] if g == 0 else a_early[g][:, 2 * G * j : 2 * G * (j + 1)]
             nc.scalar.copy(
                 out=a_dealt[j, g][:].bitcast(U16).rearrange("p (t m) -> p t m", t=SLOTS),
-                in_=a_early[g][:, 2 * G * j : 2 * G * (j + 1)].bitcast(U16).rearrange("p (m t) -> p t m", t=SLOTS),
+                in_=words.bitcast(U16).rearrange("p (m t) -> p t m", t=SLOTS),
             )
 
         def deal_tile_words(j, t):
@@ -211,6 +218,9 @@ def tile_scaled_block_projection_s9_kernel(tc, dirs, a_words, a_scales, pot, rho
                 out=dst, in0=src, scalar=seg_cols[:, u, 8 * j : 8 * j + 1], in1=sums, op0=MULT, op1=ADD
             )
 
+        def store(res, m, lo, hi):
+            nc.sync.dma_start(out=out[P * m : P * (m + 1), lo:hi], in_=res[:])
+
         def second_product(acc, m, j, lo, hi, start, stop):
             sl = slice(P * m, P * (m + 1))
             nc.tensor.matmul_mx(
@@ -233,7 +243,7 @@ def tile_scaled_block_projection_s9_kernel(tc, dirs, a_words, a_scales, pot, rho
                 op0=MULT,
                 op1=MULT,
             )
-            nc.sync.dma_start(out=out[P * m : P * (m + 1), lo:hi], in_=res[:])
+            return res
 
         acc = {}
 
@@ -242,22 +252,25 @@ def tile_scaled_block_projection_s9_kernel(tc, dirs, a_words, a_scales, pot, rho
             for g in GROUPS:
                 first_product(acc[i], i, g)
 
-        zero(s_early[:, 0, :])
-        zero(s_early[:, 1:, :].rearrange("p g n -> p (g n)"))
-        zero(seg_rows[:])
         zeros = s_late[:].rearrange("p x g n -> p (x g n)")
         zero(zeros)
-        nc.vector.quantize_mx(out=idle_codes[:].bitcast(E4M3X4), scales=idle_scales[:], in_=zeros.bitcast(BF16))
+        zero(s_early[:, 0:2, :].rearrange("p g n -> p (g n)"))
+        nc.vector.quantize_mx(out=idle_codes[1][:].bitcast(E4M3X4), scales=idle_scales[1][:], in_=zeros.bitcast(BF16))
+        nc.vector.quantize_mx(
+            out=idle_codes[0][:].bitcast(E5M2X4), scales=idle_scales[0][:], in_=zeros[:, 0 : 2 * G].bitcast(BF16)
+        )
+        zero(seg_rows[:])
+        zero(s_early[:, 2:, :].rearrange("p g n -> p (g n)"))
         zero(s_packed[:].rearrange("p x n -> p (x n)"))
         nc.scalar.copy(out=rho_rows[:], in_=zeros[:, 0 : 2 * QUAD].bitcast(BF16))
 
-        load_a_early(0)
-        load_early_scales(0, 1)
         load_d(0)
+        load_a_first(0)
+        load_early_scales(0, 2)
+        load_a_first(1)
         load_d(1)
         load_seg()
         load_a_early(1)
-        load_early_scales(1, 2)
         load_d(2)
         load_a_early(2)
         load_early_scales(2, 4)
@@ -266,40 +279,47 @@ def tile_scaled_block_projection_s9_kernel(tc, dirs, a_words, a_scales, pot, rho
         load_packed_scales()
         load_a_late(2)
 
-        for w in range(WARM_UPS):
+        idle_words = [idle_codes[0][:].bitcast(E5M2X4)] * WARM_UPS[0]
+        idle_words = idle_words + [a_first[0][:, 0 : 2 * P].bitcast(E2M1X4)] * WARM_UPS[1]
+        for w, words in enumerate(idle_words):
             nc.tensor.matmul_mx(
                 out=bank(7 - w)[:],
-                lhsT=a_early[0][:, 0 : 2 * P].bitcast(E2M1X4),
-                lhsT_scale=idle_scales[:, 0:P],
-                rhs=idle_codes[:].bitcast(E4M3X4),
-                rhs_scale=idle_scales[:],
+                lhsT=words,
+                lhsT_scale=idle_scales[0][:],
+                rhs=idle_codes[1][:].bitcast(E4M3X4),
+                rhs_scale=idle_scales[1][:],
                 start=True,
                 stop=True,
             )
         for i in range(8):
             acc[i] = bank(i)
-        deal_words(0, 0)
-        deal_words(1, 0)
-        deal_scales(0)
         for lo, hi in HALVES:
             interleave_shared(d_mix[0], d_raw[0], lo, lo + V_D[0] // 2, hi)
-        for lo, hi in HALVES:
-            quantize_d(0, lo, hi)
-            for i in range(8):
-                first_product(acc[i], i, 0, lo, hi, lo == 0)
+        deal_words(0, 0)
+        deal_words(1, 0)
+        quantize_d(0, 0, HB)
+        deal_scales(0, 0, 1)
+        quantize_d(0, HB, B)
+        deal_scales(0, 1, 2)
+        for i in range(4):
+            first_product(acc[i], i, 0, 0, HB)
+        for i in range(4):
+            first_product(acc[i], i, 0, HB, B, False)
+        for i in range(4, 8):
+            first_product(acc[i], i, 0)
         for g in (1, 2, 3):
             interleave_shared(d_mix[g], d_raw[g], 0, V_D[g], B)
-            deal_scales(g, 0, 1 if g == LAST else 2)
+            deal_scales(g, 0, 1 if g == 1 else 2)
             deal_words(0, g)
             deal_words(1, g)
             if g == LAST:
                 deal_packed_scales(2)
             quantize_d(g)
-            if g == LAST:
+            if g == 1:
                 deal_scales(g, 1, 2)
             if g == 1:
                 sort_seg()
-            if g == 2:
+            if g == LAST:
                 turn_seg()
             for i in range(8):
                 first_product(acc[i], i, g)
@@ -312,15 +332,18 @@ def tile_scaled_block_projection_s9_kernel(tc, dirs, a_words, a_scales, pot, rho
             deal_tile_words(2, t)
         for i in range(4):
             drain(acc[i], i)
-        interleave_pool(0, 0, B)
+        interleave_pool(0, 0, P_W0)
         for i in range(4, 8):
             drain(acc[i], i)
         for t in range(SLOTS):
             deal_tile_words(3, t)
+        interleave(nc.scalar.copy, w_mix[0], w_raw[0], P_W0, B)
         interleave(nc.scalar.copy, w_mix[1], w_raw[1], 0, B)
         for i in range(8, 12):
             whole_tile(i, i - 8)
             drain(acc[i], i)
+            if i == 9:
+                nc.vector.transpose(out=rho_cols[:], in_=rho_rows[:])
         interleave(nc.scalar.copy, w_mix[2], w_raw[2], 0, HB)
         interleave(nc.scalar.copy, w_mix[2], w_raw[2], HB, B)
         quantize_w(0)
@@ -334,21 +357,20 @@ def tile_scaled_block_projection_s9_kernel(tc, dirs, a_words, a_scales, pot, rho
                 for g in GROUPS:
                     first_product(half, i, g, *HALVES[x])
                 drain(half, i, *HALVES[x])
-            interleave(nc.scalar.copy, w_mix[LAST][:, HB * x : HB * (x + 1), :], w_last[:, x], 0, HB)
-        nc.vector.transpose(out=rho_cols[:], in_=rho_rows[:])
+            interleave(nc.scalar.copy, w_mix[LAST][:, HB * x : HB * (x + 1), :], w_last[:, x], x * V_LAST, HB)
         quantize_w(1, HB, B)
+        interleave(nc.vector.tensor_copy, w_mix[LAST][:, HB:, :], w_last[:, 1], 0, V_LAST)
         quantize_w(LAST, 0, HB)
         quantize_w(2, HB, B)
+        quantize_w(LAST, HB, B)
         h_acc = [bank(b) for b in (2, 3, 4, 5)]
         for j in GROUPS:
             for m in range(4):
                 second_product(h_acc[m], m, j, 0, HB, j == 0, j == LAST)
-        finish(h_acc[0], 0, 0, HB)
-        quantize_w(LAST, HB, B)
-        for m in range(1, 4):
-            finish(h_acc[m], m, 0, HB)
+        for m in range(4):
+            store(finish(h_acc[m], m, 0, HB), m, 0, HB)
         for m, b in enumerate((6, 7, 0, 1)):
             h_acc = bank(b)
             for j in GROUPS:
                 second_product(h_acc, m, j, HB, B, j == 0, j == LAST)
-            finish(h_acc, m, HB, B)
+            store(finish(h_acc, m, HB, B), m, HB, B)

@@ -25,6 +25,8 @@ GROUPS = range(K // G)
 LAST = len(GROUPS) - 1
 HALF = K // 2
 HB = B // 2
+LINE = 256
+SHIFT = LINE // 2
 HALVES = ((0, HB), (HB, B))
 V_D = (352, 320, 320, 320)
 WARM_UPS = (3, 2)
@@ -41,7 +43,7 @@ def tile_scaled_block_projection_s9_kernel(tc, dirs, a_words, a_scales, pot, rho
         ctx.enter_context(tc.manual_schedule())
 
         def sb(shape, dtype, name):
-            return keep.tile(shape, dtype, name=name, tag=name, align_bytes=64)
+            return keep.tile(shape, dtype, name=name, tag=name, align_bytes=LINE)
 
         def bank(i):
             return psum.tile([P, B], F32, name="bank%d" % i, tag="bank%d" % i)
@@ -49,17 +51,17 @@ def tile_scaled_block_projection_s9_kernel(tc, dirs, a_words, a_scales, pot, rho
         d_raw = [sb([P, SLOTS, B], BF16, "d_raw%d" % g) for g in GROUPS]
         d_mix = [sb([P, B, SLOTS], BF16, "d_mix%d" % g) for g in GROUPS]
         d_codes = [sb([P, B], U32, "d_codes%d" % g) for g in GROUPS]
-        d_scales = [sb([P, B], U8, "d_scales%d" % g) for g in GROUPS]
+        d_scales = [sb([P, SHIFT + B], U8, "d_scales%d" % g)[:, SHIFT:] for g in GROUPS]
         w_raw = [sb([P, SLOTS, B], BF16, "w_raw%d" % j) for j in range(LAST)]
         w_last = sb([P, 2, SLOTS, HB], BF16, "w_last")
         w_mix = [sb([P, B, SLOTS], BF16, "w_mix%d" % j) for j in GROUPS]
         w_codes = [sb([P, B], U32, "w_codes%d" % j) for j in GROUPS]
-        w_scales = [sb([P, B], U8, "w_scales%d" % j) for j in GROUPS]
+        w_scales = [sb([P, SHIFT + B], U8, "w_scales%d" % j)[:, SHIFT:] for j in GROUPS]
         a_first = [sb([P, 2 * G], U8, "a_first%d" % j) for j in (0, 1)]
         a_early = {g: sb([P, 2 * HALF], U8, "a_early%d" % g) for g in GROUPS[1:]}
         a_late = {j: sb([P, len(GROUPS), 2 * G], U8, "a_late%d" % j) for j in (2, 3)}
-        a_dealt = {(j, g): sb([P, 2 * G], U8, "a_dealt%d_%d" % (j, g)) for j in (0, 1) for g in GROUPS}
-        a_tile = {j: [sb([P, len(GROUPS), 2 * P], U8, "a_tile%d_%d" % (j, t)) for t in range(SLOTS)] for j in (2, 3)}
+        a_dealt = {(j, g): sb([P, 2, 3 * LINE], U8, "a_dealt%d_%d" % (j, g)) for j in (0, 1) for g in GROUPS}
+        a_tile = {j: [sb([P, 5 * LINE], U8, "a_tile%d_%d" % (j, t)) for t in range(SLOTS)] for j in (2, 3)}
         s_early = sb([P, len(GROUPS), HALF], U8, "s_early")
         s_dealt = [sb([P, 2, G], U8, "s_dealt%d" % g) for g in GROUPS]
         s_packed = sb([P, 2, G], U8, "s_packed")
@@ -173,13 +175,17 @@ def tile_scaled_block_projection_s9_kernel(tc, dirs, a_words, a_scales, pot, rho
         def deal_words(j, g):
             words = a_first[j][:] if g == 0 else a_early[g][:, 2 * G * j : 2 * G * (j + 1)]
             nc.scalar.copy(
-                out=a_dealt[j, g][:].bitcast(U16).rearrange("p (t m) -> p t m", t=SLOTS),
-                in_=words.bitcast(U16).rearrange("p (m t) -> p t m", t=SLOTS),
+                out=a_dealt[j, g][:].bitcast(U16).rearrange("p a (b m) -> p a b m", b=2)[:, :, :, 0:P],
+                in_=words.bitcast(U16).rearrange("p (m a b) -> p a b m", a=2, b=2),
             )
+
+        def tile_words(j, t):
+            lo = SHIFT * (t % 2)
+            return a_tile[j][t][:, lo : lo + 4 * LINE].rearrange("p (g n) -> p g n", n=LINE)
 
         def deal_tile_words(j, t):
             nc.scalar.copy(
-                out=a_tile[j][t][:].bitcast(U16),
+                out=tile_words(j, t).bitcast(U16),
                 in_=a_late[j][:].bitcast(U16).rearrange("p g (m t) -> p t g m", t=SLOTS)[:, t],
             )
 
@@ -193,9 +199,10 @@ def tile_scaled_block_projection_s9_kernel(tc, dirs, a_words, a_scales, pot, rho
             j, u = divmod(i, SLOTS)
             c = P * u
             if j < 2:
-                words, scales = a_dealt[j, g][:, 2 * c : 2 * (c + P)], s_dealt[g][:, j, c : c + P]
+                lo_byte = (LINE + SHIFT) * (u % 2)
+                words, scales = a_dealt[j, g][:, u // 2, lo_byte : lo_byte + LINE], s_dealt[g][:, j, c : c + P]
             else:
-                words, scales = a_tile[j][u][:, g, :], s_late[:, j - 2, g, c : c + P]
+                words, scales = tile_words(j, u)[:, g, :], s_late[:, j - 2, g, c : c + P]
             nc.tensor.matmul_mx(
                 out=acc[:, lo:hi],
                 lhsT=words.bitcast(E2M1X4),

@@ -31,7 +31,7 @@ HALVES = ((0, HB), (HB, B))
 V_D = (352, 320, 320, 320)
 WARM_UPS = (3, 2)
 V_LAST = 96
-P_W0 = 384
+P_W0 = 512
 P_PIECE = 128
 
 
@@ -65,7 +65,7 @@ def tile_scaled_block_projection_s9_kernel(tc, dirs, a_words, a_scales, pot, rho
         s_early = sb([P, len(GROUPS), HALF], U8, "s_early")
         s_dealt = [sb([P, 2, G], U8, "s_dealt%d" % g) for g in GROUPS]
         s_packed = sb([P, 2, G], U8, "s_packed")
-        s_packed_dealt = sb([P, 2, G], U8, "s_packed_dealt")
+        s_packed_dealt = {2: sb([P, G], U8, "s_packed_dealt")[:], 3: s_early[:, LAST, G:]}
         s_late = sb([P, 2, len(GROUPS), G], U8, "s_late")
         idle_codes = [sb([P, n], U32, "idle_codes%d" % n) for n in (P, B)]
         idle_scales = [sb([P, n], U8, "idle_scales%d" % n) for n in (P, B)]
@@ -91,9 +91,9 @@ def tile_scaled_block_projection_s9_kernel(tc, dirs, a_words, a_scales, pot, rho
                     in_=a_scales[:, r:16:4, HALF:].rearrange("g q n -> q g n").bitcast(I32),
                 )
 
-        def deal_packed_scales(j):
-            nc.vector.tensor_copy(
-                out=s_packed_dealt[:, j - 2, :].rearrange("p (t m) -> p t m", t=SLOTS),
+        def deal_packed_scales(j, engine):
+            engine.tensor_copy(
+                out=s_packed_dealt[j].rearrange("p (t m) -> p t m", t=SLOTS),
                 in_=s_packed[:, j - 2, :].rearrange("p (m t) -> p t m", t=SLOTS),
             )
 
@@ -101,7 +101,7 @@ def tile_scaled_block_projection_s9_kernel(tc, dirs, a_words, a_scales, pot, rho
             for r in range(4):
                 nc.sync.dma_start(
                     out=s_late[r:P:QUAD, j - 2, :, :].rearrange("q g n -> q (g n)").bitcast(I32),
-                    in_=s_packed_dealt[QUAD * r : QUAD * (r + 1) : 2, j - 2, :].bitcast(I32),
+                    in_=s_packed_dealt[j][QUAD * r : QUAD * (r + 1) : 2, :].bitcast(I32),
                 )
 
         def load_a_first(j):
@@ -316,13 +316,13 @@ def tile_scaled_block_projection_s9_kernel(tc, dirs, a_words, a_scales, pot, rho
             first_product(acc[i], i, 0)
         for g in (1, 2, 3):
             interleave_shared(d_mix[g], d_raw[g], 0, V_D[g], B)
-            deal_scales(g, 0, 1 if g == 1 else 2)
+            deal_scales(g, 0, 2 if g == 2 else 1)
             deal_words(0, g)
             deal_words(1, g)
             if g == LAST:
-                deal_packed_scales(2)
+                deal_packed_scales(2, nc.vector)
             quantize_d(g)
-            if g == 1:
+            if g != 2:
                 deal_scales(g, 1, 2)
             if g == 1:
                 sort_seg()
@@ -331,20 +331,20 @@ def tile_scaled_block_projection_s9_kernel(tc, dirs, a_words, a_scales, pot, rho
             for i in range(8):
                 first_product(acc[i], i, g)
         spread_packed_scales(2)
-        deal_packed_scales(3)
         load_a_late(3)
-        spread_packed_scales(3)
-        load_rho()
         for t in range(SLOTS):
             deal_tile_words(2, t)
-        for i in range(4):
+        drain(acc[0], 0)
+        deal_packed_scales(3, nc.gpsimd)
+        spread_packed_scales(3)
+        load_rho()
+        for i in (1, 2, 3):
             drain(acc[i], i)
         interleave_pool(0, 0, P_W0)
         for i in range(4, 8):
             drain(acc[i], i)
         for t in range(SLOTS):
             deal_tile_words(3, t)
-        interleave(nc.scalar.copy, w_mix[0], w_raw[0], P_W0, B)
         interleave(nc.scalar.copy, w_mix[1], w_raw[1], 0, B)
         for i in range(8, 12):
             whole_tile(i, i - 8)
@@ -353,17 +353,19 @@ def tile_scaled_block_projection_s9_kernel(tc, dirs, a_words, a_scales, pot, rho
                 nc.vector.transpose(out=rho_cols[:], in_=rho_rows[:])
         interleave(nc.scalar.copy, w_mix[2], w_raw[2], 0, HB)
         interleave(nc.scalar.copy, w_mix[2], w_raw[2], HB, B)
-        quantize_w(0)
         for i in (12, 13):
             whole_tile(i, i - 8)
             drain(acc[i], i)
-            quantize_w(i - 11, 0, HB)
+            if i == 12:
+                quantize_w(0)
         for x, banks in enumerate(((6, 7), (0, 1))):
             for i, b in zip((14, 15), banks):
                 half = bank(b)
                 for g in GROUPS:
                     first_product(half, i, g, *HALVES[x])
                 drain(half, i, *HALVES[x])
+                if x == 0:
+                    quantize_w(i - 13, 0, HB)
             interleave(nc.scalar.copy, w_mix[LAST][:, HB * x : HB * (x + 1), :], w_last[:, x], x * V_LAST, HB)
         quantize_w(1, HB, B)
         interleave(nc.vector.tensor_copy, w_mix[LAST][:, HB:, :], w_last[:, 1], 0, V_LAST)
@@ -376,8 +378,9 @@ def tile_scaled_block_projection_s9_kernel(tc, dirs, a_words, a_scales, pot, rho
                 second_product(h_acc[m], m, j, 0, HB, j == 0, j == LAST)
         for m in range(4):
             store(finish(h_acc[m], m, 0, HB), m, 0, HB)
-        for m, b in enumerate((6, 7, 0, 1)):
+        pieces = [(0, HB, B, 6), (1, HB, B, 7), (2, HB, B, 0), (3, HB, B - P, 1), (3, B - P, B, 2)]
+        for m, lo, hi, b in pieces:
             h_acc = bank(b)
             for j in GROUPS:
-                second_product(h_acc, m, j, HB, B, j == 0, j == LAST)
-            store(finish(h_acc, m, HB, B), m, HB, B)
+                second_product(h_acc, m, j, lo, hi, j == 0, j == LAST)
+            store(finish(h_acc, m, lo, hi), m, lo, hi)

@@ -27,6 +27,7 @@ HALF = K // 2
 HB = B // 2
 LINE = 256
 SHIFT = LINE // 2
+QUARTER = LINE // 4
 HALVES = ((0, HB), (HB, B))
 V_D = (352, 320, 320, 320)
 WARM_UPS = (3, 2)
@@ -60,13 +61,15 @@ def tile_scaled_block_projection_s9_kernel(tc, dirs, a_words, a_scales, pot, rho
         a_first = [sb([P, 2 * G], U8, "a_first%d" % j) for j in (0, 1)]
         a_early = {g: sb([P, 2 * HALF], U8, "a_early%d" % g) for g in GROUPS[1:]}
         a_late = {j: sb([P, len(GROUPS), 2 * G], U8, "a_late%d" % j) for j in (2, 3)}
-        a_dealt = {(j, g): sb([P, 2, 3 * LINE], U8, "a_dealt%d_%d" % (j, g)) for j in (0, 1) for g in GROUPS}
+        a_dealt = {(j, g): sb([P, 7 * LINE], U8, "a_dealt%d_%d" % (j, g))[:, 3 * QUARTER : 3 * QUARTER + 6 * LINE].rearrange("p (a n) -> p a n", a=2) for j in (0, 1) for g in GROUPS}
         a_tile = {j: [sb([P, 5 * LINE], U8, "a_tile%d_%d" % (j, t)) for t in range(SLOTS)] for j in (2, 3)}
         s_early = sb([P, len(GROUPS), HALF], U8, "s_early")
-        s_dealt = [sb([P, 2, G], U8, "s_dealt%d" % g) for g in GROUPS]
+        s_dealt = [
+            sb([P, QUARTER + 2 * G], U8, "s_dealt%d" % g)[:, QUARTER:].rearrange("p (j n) -> p j n", j=2) for g in GROUPS
+        ]
         s_packed = sb([P, 2, G], U8, "s_packed")
         s_packed_dealt = {2: sb([P, G], U8, "s_packed_dealt")[:], 3: s_early[:, LAST, G:]}
-        s_late = sb([P, 2, len(GROUPS), G], U8, "s_late")
+        s_late = sb([P, QUARTER + 2 * K], U8, "s_late")[:, QUARTER:].rearrange("p (x g n) -> p x g n", x=2, n=G)
         idle_codes = [sb([P, n], U32, "idle_codes%d" % n) for n in (P, B)]
         idle_scales = [sb([P, n], U8, "idle_scales%d" % n) for n in (P, B)]
         rho_rows = sb([P, QUAD], BF16, "rho_rows")
@@ -180,7 +183,7 @@ def tile_scaled_block_projection_s9_kernel(tc, dirs, a_words, a_scales, pot, rho
             )
 
         def tile_words(j, t):
-            lo = SHIFT * (t % 2)
+            lo = 3 * QUARTER - SHIFT * (t % 2)
             return a_tile[j][t][:, lo : lo + 4 * LINE].rearrange("p (g n) -> p g n", n=LINE)
 
         def deal_tile_words(j, t):

@@ -29,7 +29,7 @@ LINE = 256
 SHIFT = LINE // 2
 QUARTER = LINE // 4
 HALVES = ((0, HB), (HB, B))
-V_D = (352, 320, 320, 320)
+V_D = (352, 368, 368, 368)
 WARM_UPS = (3, 2)
 V_LAST = 96
 P_W0 = 512

@@ -24,15 +24,19 @@ G = P * SLOTS
 GROUPS = range(K // G)
 LAST = len(GROUPS) - 1
 HALF = K // 2
+SPLIT = (0,)
 HB = B // 2
 LINE = 256
 SHIFT = LINE // 2
 QUARTER = LINE // 4
 HALVES = ((0, HB), (HB, B))
-V_D = (352, 368, 368, 368)
+V_D = (352, 336, 336, 336)
 WARM_UPS = (3, 2)
 V_LAST = 96
 P_W0 = 512
+P_W2 = 128
+SPLIT_TILES = {1: 8, 2: 8, 3: 4}
+IN_PLACE = 2
 P_PIECE = 128
 
 
@@ -58,8 +62,8 @@ def tile_scaled_block_projection_s9_kernel(tc, dirs, a_words, a_scales, pot, rho
         w_mix = [sb([P, B, SLOTS], BF16, "w_mix%d" % j) for j in GROUPS]
         w_codes = [sb([P, B], U32, "w_codes%d" % j) for j in GROUPS]
         w_scales = [sb([P, SHIFT + B], U8, "w_scales%d" % j)[:, SHIFT:] for j in GROUPS]
-        a_first = [sb([P, 2 * G], U8, "a_first%d" % j) for j in (0, 1)]
-        a_early = {g: sb([P, 2 * HALF], U8, "a_early%d" % g) for g in GROUPS[1:]}
+        a_first = {(j, g): sb([P, 2 * G], U8, "a_first%d_%d" % (j, g)) for j in (0, 1) for g in SPLIT}
+        a_early = {g: sb([P, 2 * HALF], U8, "a_early%d" % g) for g in GROUPS if g not in SPLIT}
         a_late = {j: sb([P, len(GROUPS), 2 * G], U8, "a_late%d" % j) for j in (2, 3)}
         a_dealt = {(j, g): sb([P, 7 * LINE], U8, "a_dealt%d_%d" % (j, g))[:, 3 * QUARTER : 3 * QUARTER + 6 * LINE].rearrange("p (a n) -> p a n", a=2) for j in (0, 1) for g in GROUPS}
         a_tile = {j: [sb([P, 5 * LINE], U8, "a_tile%d_%d" % (j, t)) for t in range(SLOTS)] for j in (2, 3)}
@@ -70,8 +74,8 @@ def tile_scaled_block_projection_s9_kernel(tc, dirs, a_words, a_scales, pot, rho
         s_packed = sb([P, 2, G], U8, "s_packed")
         s_packed_dealt = {2: sb([P, G], U8, "s_packed_dealt")[:], 3: s_early[:, LAST, G:]}
         s_late = sb([P, QUARTER + 2 * K], U8, "s_late")[:, QUARTER:].rearrange("p (x g n) -> p x g n", x=2, n=G)
-        idle_codes = [sb([P, n], U32, "idle_codes%d" % n) for n in (P, B)]
-        idle_scales = [sb([P, n], U8, "idle_scales%d" % n) for n in (P, B)]
+        idle_codes = sb([P, B + P], U32, "idle_codes")
+        idle_scales = sb([P, B + P], U8, "idle_scales")
         rho_rows = sb([P, QUAD], BF16, "rho_rows")
         rho_cols = sb([P, QUAD], BF16, "rho_cols")
         seg_rows = sb([P, P], BF16, "seg_rows")
@@ -90,7 +94,7 @@ def tile_scaled_block_projection_s9_kernel(tc, dirs, a_words, a_scales, pot, rho
         def load_packed_scales():
             for r in range(4):
                 nc.sync.dma_start(
-                    out=s_packed[QUAD * r : QUAD * (r + 1) : 2, :, :].rearrange("p x n -> p (x n)").bitcast(I32),
+                    out=s_packed[r:P:8, :, :].rearrange("p x n -> p (x n)").bitcast(I32),
                     in_=a_scales[:, r:16:4, HALF:].rearrange("g q n -> q g n").bitcast(I32),
                 )
 
@@ -104,19 +108,19 @@ def tile_scaled_block_projection_s9_kernel(tc, dirs, a_words, a_scales, pot, rho
             for r in range(4):
                 nc.sync.dma_start(
                     out=s_late[r:P:QUAD, j - 2, :, :].rearrange("q g n -> q (g n)").bitcast(I32),
-                    in_=s_packed_dealt[j][QUAD * r : QUAD * (r + 1) : 2, :].bitcast(I32),
+                    in_=s_packed_dealt[j][r:P:8, :].bitcast(I32),
                 )
 
-        def load_a_first(j):
-            nc.sync.dma_start(out=a_first[j][:].bitcast(I32), in_=a_words[0][:, 2 * G * j : 2 * G * (j + 1)].bitcast(I32))
+        def load_a_first(j, g):
+            nc.sync.dma_start(out=a_first[j, g][:].bitcast(I32), in_=a_words[g][:, 2 * G * j : 2 * G * (j + 1)].bitcast(I32))
 
         def load_a_early(g):
             nc.sync.dma_start(out=a_early[g][:].bitcast(I32), in_=a_words[g][:, 0 : 2 * HALF].bitcast(I32))
 
-        def load_a_late(j):
+        def load_a_late(j, lo=0, hi=len(GROUPS)):
             nc.sync.dma_start(
-                out=a_late[j][:].bitcast(I32),
-                in_=a_words[:, :, 2 * G * j : 2 * G * (j + 1)].rearrange("g p n -> p g n").bitcast(I32),
+                out=a_late[j][:, lo:hi, :].bitcast(I32),
+                in_=a_words[lo:hi, :, 2 * G * j : 2 * G * (j + 1)].rearrange("g p n -> p g n").bitcast(I32),
             )
 
         def load_d(g):
@@ -176,7 +180,7 @@ def tile_scaled_block_projection_s9_kernel(tc, dirs, a_words, a_scales, pot, rho
             quantize(w_codes[j], w_scales[j], w_mix[j], E5M2X4, lo, hi)
 
         def deal_words(j, g):
-            words = a_first[j][:] if g == 0 else a_early[g][:, 2 * G * j : 2 * G * (j + 1)]
+            words = a_first[j, g][:] if g in SPLIT else a_early[g][:, 2 * G * j : 2 * G * (j + 1)]
             nc.scalar.copy(
                 out=a_dealt[j, g][:].bitcast(U16).rearrange("p a (b m) -> p a b m", b=2)[:, :, :, 0:P],
                 in_=words.bitcast(U16).rearrange("p (m a b) -> p a b m", a=2, b=2),
@@ -198,7 +202,7 @@ def tile_scaled_block_projection_s9_kernel(tc, dirs, a_words, a_scales, pot, rho
                 in_=s_early[:, g, G * lo : G * hi].rearrange("p (j m t) -> p j t m", t=SLOTS, m=P),
             )
 
-        def first_product(acc, i, g, lo=0, hi=B, start=None):
+        def first_product(acc, i, g, lo=0, hi=B, start=None, stop=None):
             j, u = divmod(i, SLOTS)
             c = P * u
             if j < 2:
@@ -206,6 +210,8 @@ def tile_scaled_block_projection_s9_kernel(tc, dirs, a_words, a_scales, pot, rho
                 words, scales = a_dealt[j, g][:, u // 2, lo_byte : lo_byte + LINE], s_dealt[g][:, j, c : c + P]
             else:
                 words, scales = tile_words(j, u)[:, g, :], s_late[:, j - 2, g, c : c + P]
+                if g == 0 and i < 8 + IN_PLACE:
+                    scales = s_packed_dealt[j][:, c : c + P]
             nc.tensor.matmul_mx(
                 out=acc[:, lo:hi],
                 lhsT=words.bitcast(E2M1X4),
@@ -213,7 +219,7 @@ def tile_scaled_block_projection_s9_kernel(tc, dirs, a_words, a_scales, pot, rho
                 rhs=d_codes[g][:, lo:hi].bitcast(E4M3X4),
                 rhs_scale=d_scales[g][:, lo:hi],
                 start=(g == 0) if start is None else start,
-                stop=(g == LAST),
+                stop=(g == LAST) if stop is None else stop,
             )
 
         def drain(acc, i, lo=0, hi=B):
@@ -262,42 +268,43 @@ def tile_scaled_block_projection_s9_kernel(tc, dirs, a_words, a_scales, pot, rho
             for g in GROUPS:
                 first_product(acc[i], i, g)
 
-        zeros = s_late[:].rearrange("p x g n -> p (x g n)")
-        zero(zeros)
         zero(s_early[:, 0:2, :].rearrange("p g n -> p (g n)"))
-        nc.vector.quantize_mx(out=idle_codes[1][:].bitcast(E4M3X4), scales=idle_scales[1][:], in_=zeros.bitcast(BF16))
-        nc.vector.quantize_mx(
-            out=idle_codes[0][:].bitcast(E5M2X4), scales=idle_scales[0][:], in_=zeros[:, 0 : 2 * G].bitcast(BF16)
-        )
+        zero(idle_codes[:])
+        zero(idle_scales[:])
         zero(seg_rows[:])
+        zeros = idle_codes[:, P : P + P // 2].bitcast(BF16)
+        nc.vector.quantize_mx(out=idle_codes[:, 0:QUAD].bitcast(E4M3X4), scales=idle_scales[:, 0:QUAD], in_=zeros)
+        nc.vector.quantize_mx(out=idle_codes[:, B : B + QUAD].bitcast(E5M2X4), scales=idle_scales[:, B : B + QUAD], in_=zeros)
+        nc.scalar.copy(out=rho_rows[:], in_=zeros[:, 0:QUAD])
         zero(s_early[:, 2:, :].rearrange("p g n -> p (g n)"))
         zero(s_packed[:].rearrange("p x n -> p (x n)"))
-        nc.scalar.copy(out=rho_rows[:], in_=zeros[:, 0 : 2 * QUAD].bitcast(BF16))
+        zero(s_late[:].rearrange("p x g n -> p (x g n)"))
 
         load_d(0)
-        load_a_first(0)
+        load_a_first(0, 0)
         load_early_scales(0, 2)
-        load_a_first(1)
+        load_a_first(1, 0)
         load_d(1)
         load_seg()
         load_a_early(1)
         load_d(2)
-        load_a_early(2)
         load_early_scales(2, 4)
+        load_a_early(2)
         load_d(3)
         load_a_early(3)
         load_packed_scales()
         load_a_late(2)
+        load_a_late(3, 0, 2)
 
-        idle_words = [idle_codes[0][:].bitcast(E5M2X4)] * WARM_UPS[0]
-        idle_words = idle_words + [a_first[0][:, 0 : 2 * P].bitcast(E2M1X4)] * WARM_UPS[1]
+        idle_words = [idle_codes[:, B:].bitcast(E5M2X4)] * WARM_UPS[0]
+        idle_words = idle_words + [a_first[0, 0][:, 0 : 2 * P].bitcast(E2M1X4)] * WARM_UPS[1]
         for w, words in enumerate(idle_words):
             nc.tensor.matmul_mx(
                 out=bank(7 - w)[:],
                 lhsT=words,
-                lhsT_scale=idle_scales[0][:],
-                rhs=idle_codes[1][:].bitcast(E4M3X4),
-                rhs_scale=idle_scales[1][:],
+                lhsT_scale=idle_scales[:, B:],
+                rhs=idle_codes[:, 0:B].bitcast(E4M3X4),
+                rhs_scale=idle_scales[:, 0:B],
                 start=True,
                 stop=True,
             )
@@ -318,23 +325,32 @@ def tile_scaled_block_projection_s9_kernel(tc, dirs, a_words, a_scales, pot, rho
         for i in range(4, 8):
             first_product(acc[i], i, 0)
         for g in (1, 2, 3):
-            interleave_shared(d_mix[g], d_raw[g], 0, V_D[g], B)
-            deal_scales(g, 0, 2 if g == 2 else 1)
+            split = SPLIT_TILES[g]
+            interleave(nc.vector.tensor_copy, d_mix[g], d_raw[g], 0, HB)
+            interleave(nc.scalar.copy, d_mix[g], d_raw[g], V_D[g], B)
             deal_words(0, g)
             deal_words(1, g)
+            deal_scales(g, 0, 1)
+            quantize_d(g, 0, HB)
+            interleave(nc.vector.tensor_copy, d_mix[g], d_raw[g], HB, V_D[g])
             if g == LAST:
                 deal_packed_scales(2, nc.vector)
-            quantize_d(g)
-            if g != 2:
+                quantize_d(g, HB, B)
                 deal_scales(g, 1, 2)
+            else:
+                deal_scales(g, 1, 2)
+                quantize_d(g, HB, B)
             if g == 1:
                 sort_seg()
             if g == LAST:
                 turn_seg()
-            for i in range(8):
+            for x, (lo, hi) in enumerate(HALVES):
+                for i in range(split):
+                    first_product(acc[i], i, g, lo, hi, False, g == LAST and x == 1)
+            for i in range(split, 8):
                 first_product(acc[i], i, g)
         spread_packed_scales(2)
-        load_a_late(3)
+        load_a_late(3, 2, 4)
         for t in range(SLOTS):
             deal_tile_words(2, t)
         drain(acc[0], 0)
@@ -349,27 +365,40 @@ def tile_scaled_block_projection_s9_kernel(tc, dirs, a_words, a_scales, pot, rho
         for t in range(SLOTS):
             deal_tile_words(3, t)
         interleave(nc.scalar.copy, w_mix[1], w_raw[1], 0, B)
-        for i in range(8, 12):
-            whole_tile(i, i - 8)
+        for i in range(8, 8 + IN_PLACE):
+            acc[i] = bank(i - 8)
+            first_product(acc[i], i, 0)
+        for i in range(8, 11):
+            if i < 8 + IN_PLACE:
+                for g in GROUPS[1:]:
+                    first_product(acc[i], i, g)
+            else:
+                whole_tile(i, i - 8)
             drain(acc[i], i)
-            if i == 9:
-                nc.vector.transpose(out=rho_cols[:], in_=rho_rows[:])
-        interleave(nc.scalar.copy, w_mix[2], w_raw[2], 0, HB)
-        interleave(nc.scalar.copy, w_mix[2], w_raw[2], HB, B)
-        for i in (12, 13):
+        for i in range(11, 14):
             whole_tile(i, i - 8)
-            drain(acc[i], i)
-            if i == 12:
-                quantize_w(0)
+        halves = {}
         for x, banks in enumerate(((6, 7), (0, 1))):
             for i, b in zip((14, 15), banks):
-                half = bank(b)
+                halves[i, x] = bank(b)
                 for g in GROUPS:
-                    first_product(half, i, g, *HALVES[x])
-                drain(half, i, *HALVES[x])
-                if x == 0:
-                    quantize_w(i - 13, 0, HB)
-            interleave(nc.scalar.copy, w_mix[LAST][:, HB * x : HB * (x + 1), :], w_last[:, x], x * V_LAST, HB)
+                    first_product(halves[i, x], i, g, *HALVES[x])
+        drain(acc[11], 11)
+        interleave(nc.scalar.copy, w_mix[2], w_raw[2], 0, HB)
+        interleave(nc.scalar.copy, w_mix[2], w_raw[2], HB, B - P_W2)
+        interleave_pool(2, B - P_W2, B)
+        nc.vector.transpose(out=rho_cols[:], in_=rho_rows[:])
+        quantize_w(0)
+        drain(acc[12], 12)
+        drain(acc[13], 13)
+        drain(halves[14, 0], 14, 0, HB)
+        quantize_w(1, 0, HB)
+        drain(halves[15, 0], 15, 0, HB)
+        interleave(nc.scalar.copy, w_mix[LAST][:, 0:HB, :], w_last[:, 0], 0, HB)
+        quantize_w(2, 0, HB)
+        drain(halves[14, 1], 14, HB, B)
+        drain(halves[15, 1], 15, HB, B)
+        interleave(nc.scalar.copy, w_mix[LAST][:, HB:, :], w_last[:, 1], V_LAST, HB)
         quantize_w(1, HB, B)
         interleave(nc.vector.tensor_copy, w_mix[LAST][:, HB:, :], w_last[:, 1], 0, V_LAST)
         quantize_w(LAST, 0, HB)

from contextlib import ExitStack

import concourse.mybir as mybir

K, B = 2048, 512
FLOPS = 2 * K * K * B + 2 * K * B * B

F32 = mybir.dt.float32
BF16 = mybir.dt.bfloat16
U32 = mybir.dt.uint32
U16 = mybir.dt.uint16
I32 = mybir.dt.int32
U8 = mybir.dt.uint8
E4M3X4 = mybir.dt.float8_e4m3fn_x4
E5M2X4 = mybir.dt.float8_e5m2_x4
E2M1X4 = mybir.dt.float4_e2m1fn_x4
MULT = mybir.AluOpType.mult
ADD = mybir.AluOpType.add

P = 128
QUAD = 32
SLOTS = 4
G = P * SLOTS
GROUPS = range(K // G)
LAST = len(GROUPS) - 1
HALF = K // 2
SPLIT = (0,)
HB = B // 2
LINE = 256
SHIFT = LINE // 2
QUARTER = LINE // 4
HALVES = ((0, HB), (HB, B))
V_D = (352, 336, 336, 336)
WARM_UPS = (3, 2)
V_LAST = 96
P_W0 = 512
P_W2 = 128
SPLIT_TILES = {1: 8, 2: 8, 3: 4}
IN_PLACE = 2
P_PIECE = 128


def tile_scaled_block_projection_s9_kernel(tc, dirs, a_words, a_scales, pot, rho, out):
    nc = tc.nc
    with ExitStack() as ctx:
        keep = ctx.enter_context(tc.tile_pool(name="keep", bufs=1))
        psum = ctx.enter_context(tc.psum_pool(name="psum", bufs=1))
        ctx.enter_context(tc.manual_schedule())

        def sb(shape, dtype, name):
            return keep.tile(shape, dtype, name=name, tag=name, align_bytes=LINE)

        def bank(i):
            return psum.tile([P, B], F32, name="bank%d" % i, tag="bank%d" % i)

        d_raw = [sb([P, SLOTS, B], BF16, "d_raw%d" % g) for g in GROUPS]
        d_mix = [sb([P, B, SLOTS], BF16, "d_mix%d" % g) for g in GROUPS]
        d_codes = [sb([P, B], U32, "d_codes%d" % g) for g in GROUPS]
        d_scales = [sb([P, SHIFT + B], U8, "d_scales%d" % g)[:, SHIFT:] for g in GROUPS]
        w_raw = [sb([P, SLOTS, B], BF16, "w_raw%d" % j) for j in range(LAST)]
        w_last = sb([P, 2, SLOTS, HB], BF16, "w_last")
        w_mix = [sb([P, B, SLOTS], BF16, "w_mix%d" % j) for j in GROUPS]
        w_codes = [sb([P, B], U32, "w_codes%d" % j) for j in GROUPS]
        w_scales = [sb([P, SHIFT + B], U8, "w_scales%d" % j)[:, SHIFT:] for j in GROUPS]
        a_first = {(j, g): sb([P, 2 * G], U8, "a_first%d_%d" % (j, g)) for j in (0, 1) for g in SPLIT}
        a_early = {g: sb([P, 2 * HALF], U8, "a_early%d" % g) for g in GROUPS if g not in SPLIT}
        a_late = {j: sb([P, len(GROUPS), 2 * G], U8, "a_late%d" % j) for j in (2, 3)}
        a_dealt = {(j, g): sb([P, 7 * LINE], U8, "a_dealt%d_%d" % (j, g))[:, 3 * QUARTER : 3 * QUARTER + 6 * LINE].rearrange("p (a n) -> p a n", a=2) for j in (0, 1) for g in GROUPS}
        a_tile = {j: [sb([P, 5 * LINE], U8, "a_tile%d_%d" % (j, t)) for t in range(SLOTS)] for j in (2, 3)}
        s_early = sb([P, len(GROUPS), HALF], U8, "s_early")
        s_dealt = [
            sb([P, QUARTER + 2 * G], U8, "s_dealt%d" % g)[:, QUARTER:].rearrange("p (j n) -> p j n", j=2) for g in GROUPS
        ]
        s_packed = sb([P, 2, G], U8, "s_packed")
        s_packed_dealt = {2: sb([P, G], U8, "s_packed_dealt")[:], 3: s_early[:, LAST, G:]}
        s_late = sb([P, QUARTER + 2 * K], U8, "s_late")[:, QUARTER:].rearrange("p (x g n) -> p x g n", x=2, n=G)
        idle_codes = sb([P, B + P], U32, "idle_codes")
        idle_scales = sb([P, B + P], U8, "idle_scales")
        rho_rows = sb([P, QUAD], BF16, "rho_rows")
        rho_cols = sb([P, QUAD], BF16, "rho_cols")
        seg_rows = sb([P, P], BF16, "seg_rows")
        seg_slots = sb([P, SLOTS, QUAD], BF16, "seg_slots")
        seg_cols = sb([P, SLOTS, QUAD], BF16, "seg_cols")
        rho_some = sb([P, B], BF16, "rho_some")
        rho_all = sb([P, B], BF16, "rho_all")

        def load_early_scales(lo, hi):
            for r in range(4):
                nc.sync.dma_start(
                    out=s_early[r:P:QUAD, lo:hi, :].bitcast(I32),
                    in_=a_scales[lo:hi, r:16:4, 0:HALF].rearrange("g q n -> q g n").bitcast(I32),
                )

        def load_packed_scales():
            for r in range(4):
                nc.sync.dma_start(
                    out=s_packed[r:P:8, :, :].rearrange("p x n -> p (x n)").bitcast(I32),
                    in_=a_scales[:, r:16:4, HALF:].rearrange("g q n -> q g n").bitcast(I32),
                )

        def deal_packed_scales(j, engine):
            engine.tensor_copy(
                out=s_packed_dealt[j].rearrange("p (t m) -> p t m", t=SLOTS),
                in_=s_packed[:, j - 2, :].rearrange("p (m t) -> p t m", t=SLOTS),
            )

        def spread_packed_scales(j):
            for r in range(4):
                nc.sync.dma_start(
                    out=s_late[r:P:QUAD, j - 2, :, :].rearrange("q g n -> q (g n)").bitcast(I32),
                    in_=s_packed_dealt[j][r:P:8, :].bitcast(I32),
                )

        def load_a_first(j, g):
            nc.sync.dma_start(out=a_first[j, g][:].bitcast(I32), in_=a_words[g][:, 2 * G * j : 2 * G * (j + 1)].bitcast(I32))

        def load_a_early(g):
            nc.sync.dma_start(out=a_early[g][:].bitcast(I32), in_=a_words[g][:, 0 : 2 * HALF].bitcast(I32))

        def load_a_late(j, lo=0, hi=len(GROUPS)):
            nc.sync.dma_start(
                out=a_late[j][:, lo:hi, :].bitcast(I32),
                in_=a_words[lo:hi, :, 2 * G * j : 2 * G * (j + 1)].rearrange("g p n -> p g n").bitcast(I32),
            )

        def load_d(g):
            nc.sync.dma_start(out=d_raw[g][:], in_=dirs[G * g : G * (g + 1), :].rearrange("(p t) b -> p t b", t=SLOTS))

        def load_seg():
            nc.sync.dma_start(out=seg_rows[0:P:8, :], in_=pot.rearrange("(j q x) -> q j x", q=4, x=P))

        def load_rho():
            nc.sync.dma_start(out=rho_rows[0:P:8, :], in_=rho.rearrange("(m q c) -> q m c", q=4, c=QUAD))
            nc.sync.dma_start(out=rho_some[0:P:8, :], in_=rho.partition_broadcast(P // 8))
            nc.sync.dma_start(out=rho_all[:], in_=rho_some[0:P:8, :].unsqueeze(1).to_broadcast([P // 8, 8, B]))

        def sort_seg():
            nc.scalar.copy(out=seg_slots[:], in_=seg_rows[:].rearrange("p (c t) -> p t c", t=SLOTS))

        def turn_seg():
            nc.vector.transpose(
                out=seg_cols[:].rearrange("p t k -> p (t k)"), in_=seg_slots[:].rearrange("p t c -> p (t c)")
            )

        def zero(tile):
            nc.vector.memset(tile.bitcast(I32), 0)

        def interleave(copy, mix, raw, lo, hi):
            copy(
                out=mix[:, lo:hi, :].rearrange("p (c i) t -> p c t i", i=4),
                in_=raw[:, :, lo:hi].rearrange("p t (c i) -> p c t i", i=4),
            )

        def interleave_shared(mix, raw, lo, mid, hi):
            interleave(nc.vector.tensor_copy, mix, raw, lo, mid)
            interleave(nc.scalar.copy, mix, raw, mid, hi)

        def interleave_pool(j, lo, hi):
            for c in range(lo, hi, P_PIECE):
                nc.gpsimd.tensor_scalar(
                    out=w_mix[j][:, c : c + P_PIECE, :],
                    in0=w_raw[j][:, :, c : c + P_PIECE].rearrange("p t b -> p b t"),
                    scalar1=1.0,
                    scalar2=0.0,
                    op0=MULT,
                    op1=ADD,
                )

        def quantize(codes, scales, mix, fmt, lo, hi):
            nc.vector.quantize_mx(
                out=codes[:, lo:hi].bitcast(fmt),
                scales=scales[:, lo:hi],
                in_=mix[:, lo:hi, :].rearrange("p b t -> p (b t)"),
            )

        def quantize_d(g, lo=0, hi=B):
            quantize(d_codes[g], d_scales[g], d_mix[g], E4M3X4, lo, hi)

        def quantize_w(j, lo=0, hi=B):
            quantize(w_codes[j], w_scales[j], w_mix[j], E5M2X4, lo, hi)

        def deal_words(j, g):
            words = a_first[j, g][:] if g in SPLIT else a_early[g][:, 2 * G * j : 2 * G * (j + 1)]
            nc.scalar.copy(
                out=a_dealt[j, g][:].bitcast(U16).rearrange("p a (b m) -> p a b m", b=2)[:, :, :, 0:P],
                in_=words.bitcast(U16).rearrange("p (m a b) -> p a b m", a=2, b=2),
            )

        def tile_words(j, t):
            lo = 3 * QUARTER - SHIFT * (t % 2)
            return a_tile[j][t][:, lo : lo + 4 * LINE].rearrange("p (g n) -> p g n", n=LINE)

        def deal_tile_words(j, t):
            nc.scalar.copy(
                out=tile_words(j, t).bitcast(U16),
                in_=a_late[j][:].bitcast(U16).rearrange("p g (m t) -> p t g m", t=SLOTS)[:, t],
            )

        def deal_scales(g, lo=0, hi=2):
            nc.vector.tensor_copy(
                out=s_dealt[g][:, lo:hi, :].rearrange("p j (t m) -> p j t m", t=SLOTS),
                in_=s_early[:, g, G * lo : G * hi].rearrange("p (j m t) -> p j t m", t=SLOTS, m=P),
            )

        def first_product(acc, i, g, lo=0, hi=B, start=None, stop=None):
            j, u = divmod(i, SLOTS)
            c = P * u
            if j < 2:
                lo_byte = (LINE + SHIFT) * (u % 2)
                words, scales = a_dealt[j, g][:, u // 2, lo_byte : lo_byte + LINE], s_dealt[g][:, j, c : c + P]
            else:
                words, scales = tile_words(j, u)[:, g, :], s_late[:, j - 2, g, c : c + P]
                if g == 0 and i < 8 + IN_PLACE:
                    scales = s_packed_dealt[j][:, c : c + P]
            nc.tensor.matmul_mx(
                out=acc[:, lo:hi],
                lhsT=words.bitcast(E2M1X4),
                lhsT_scale=scales,
                rhs=d_codes[g][:, lo:hi].bitcast(E4M3X4),
                rhs_scale=d_scales[g][:, lo:hi],
                start=(g == 0) if start is None else start,
                stop=(g == LAST) if stop is None else stop,
            )

        def drain(acc, i, lo=0, hi=B):
            j, u = divmod(i, SLOTS)
            src, sums = d_raw[j][:, u, lo:hi], acc[:, lo:hi]
            if j == LAST:
                dst = w_last[:, lo // HB : hi // HB, u, :]
                src, sums = (x.rearrange("p (x b) -> p x b", b=HB) for x in (src, sums))
            else:
                dst = w_raw[j][:, u, :]
            nc.vector.scalar_tensor_tensor(
                out=dst, in0=src, scalar=seg_cols[:, u, 8 * j : 8 * j + 1], in1=sums, op0=MULT, op1=ADD
            )

        def store(res, m, lo, hi):
            nc.sync.dma_start(out=out[P * m : P * (m + 1), lo:hi], in_=res[:])

        def second_product(acc, m, j, lo, hi, start, stop):
            sl = slice(P * m, P * (m + 1))
            nc.tensor.matmul_mx(
                out=acc[:, lo:hi],
                lhsT=d_codes[j][:, sl].bitcast(E4M3X4),
                lhsT_scale=d_scales[j][:, sl],
                rhs=w_codes[j][:, lo:hi].bitcast(E5M2X4),
                rhs_scale=w_scales[j][:, lo:hi],
                start=start,
                stop=stop,
            )

        def finish(acc, m, lo, hi):
            res = sb([P, hi - lo], F32, "res%d_%d" % (m, lo))
            nc.vector.scalar_tensor_tensor(
                out=res[:],
                in0=acc[:, lo:hi],
                scalar=rho_cols[:, 8 * m : 8 * m + 1],
                in1=rho_all[:, lo:hi],
                op0=MULT,
                op1=MULT,
            )
            return res

        acc = {}

        def whole_tile(i, b):
            acc[i] = bank(b)
            for g in GROUPS:
                first_product(acc[i], i, g)

        zero(s_early[:, 0:2, :].rearrange("p g n -> p (g n)"))
        zero(idle_codes[:])
        zero(idle_scales[:])
        zero(seg_rows[:])
        zeros = idle_codes[:, P : P + P // 2].bitcast(BF16)
        nc.vector.quantize_mx(out=idle_codes[:, 0:QUAD].bitcast(E4M3X4), scales=idle_scales[:, 0:QUAD], in_=zeros)
        nc.vector.quantize_mx(out=idle_codes[:, B : B + QUAD].bitcast(E5M2X4), scales=idle_scales[:, B : B + QUAD], in_=zeros)
        nc.scalar.copy(out=rho_rows[:], in_=zeros[:, 0:QUAD])
        zero(s_early[:, 2:, :].rearrange("p g n -> p (g n)"))
        zero(s_packed[:].rearrange("p x n -> p (x n)"))
        zero(s_late[:].rearrange("p x g n -> p (x g n)"))

        load_d(0)
        load_a_first(0, 0)
        load_early_scales(0, 2)
        load_a_first(1, 0)
        load_d(1)
        load_seg()
        load_a_early(1)
        load_d(2)
        load_early_scales(2, 4)
        load_a_early(2)
        load_d(3)
        load_a_early(3)
        load_packed_scales()
        load_a_late(2)
        load_a_late(3, 0, 2)

        idle_words = [idle_codes[:, B:].bitcast(E5M2X4)] * WARM_UPS[0]
        idle_words = idle_words + [a_first[0, 0][:, 0 : 2 * P].bitcast(E2M1X4)] * WARM_UPS[1]
        for w, words in enumerate(idle_words):
            nc.tensor.matmul_mx(
                out=bank(7 - w)[:],
                lhsT=words,
                lhsT_scale=idle_scales[:, B:],
                rhs=idle_codes[:, 0:B].bitcast(E4M3X4),
                rhs_scale=idle_scales[:, 0:B],
                start=True,
                stop=True,
            )
        for i in range(8):
            acc[i] = bank(i)
        for lo, hi in HALVES:
            interleave_shared(d_mix[0], d_raw[0], lo, lo + V_D[0] // 2, hi)
        deal_words(0, 0)
        deal_words(1, 0)
        quantize_d(0, 0, HB)
        deal_scales(0, 0, 1)
        quantize_d(0, HB, B)
        deal_scales(0, 1, 2)
        for i in range(4):
            first_product(acc[i], i, 0, 0, HB)
        for i in range(4):
            first_product(acc[i], i, 0, HB, B, False)
        for i in range(4, 8):
            first_product(acc[i], i, 0)
        for g in (1, 2, 3):
            split = SPLIT_TILES[g]
            interleave(nc.vector.tensor_copy, d_mix[g], d_raw[g], 0, HB)
            interleave(nc.scalar.copy, d_mix[g], d_raw[g], V_D[g], B)
            deal_words(0, g)
            deal_words(1, g)
            deal_scales(g, 0, 1)
            quantize_d(g, 0, HB)
            interleave(nc.vector.tensor_copy, d_mix[g], d_raw[g], HB, V_D[g])
            if g == LAST:
                deal_packed_scales(2, nc.vector)
                quantize_d(g, HB, B)
                deal_scales(g, 1, 2)
            else:
                deal_scales(g, 1, 2)
                quantize_d(g, HB, B)
            if g == 1:
                sort_seg()
            if g == LAST:
                turn_seg()
            for x, (lo, hi) in enumerate(HALVES):
                for i in range(split):
                    first_product(acc[i], i, g, lo, hi, False, g == LAST and x == 1)
            for i in range(split, 8):
                first_product(acc[i], i, g)
        spread_packed_scales(2)
        load_a_late(3, 2, 4)
        for t in range(SLOTS):
            deal_tile_words(2, t)
        drain(acc[0], 0)
        deal_packed_scales(3, nc.gpsimd)
        spread_packed_scales(3)
        load_rho()
        for i in (1, 2, 3):
            drain(acc[i], i)
        interleave_pool(0, 0, P_W0)
        for i in range(4, 8):
            drain(acc[i], i)
        for t in range(SLOTS):
            deal_tile_words(3, t)
        interleave(nc.scalar.copy, w_mix[1], w_raw[1], 0, B)
        for i in range(8, 8 + IN_PLACE):
            acc[i] = bank(i - 8)
            first_product(acc[i], i, 0)
        for i in range(8, 11):
            if i < 8 + IN_PLACE:
                for g in GROUPS[1:]:
                    first_product(acc[i], i, g)
            else:
                whole_tile(i, i - 8)
            drain(acc[i], i)
        for i in range(11, 14):
            whole_tile(i, i - 8)
        halves = {}
        for x, banks in enumerate(((6, 7), (0, 1))):
            for i, b in zip((14, 15), banks):
                halves[i, x] = bank(b)
                for g in GROUPS:
                    first_product(halves[i, x], i, g, *HALVES[x])
        drain(acc[11], 11)
        interleave(nc.scalar.copy, w_mix[2], w_raw[2], 0, HB)
        interleave(nc.scalar.copy, w_mix[2], w_raw[2], HB, B - P_W2)
        interleave_pool(2, B - P_W2, B)
        nc.vector.transpose(out=rho_cols[:], in_=rho_rows[:])
        quantize_w(0)
        drain(acc[12], 12)
        drain(acc[13], 13)
        drain(halves[14, 0], 14, 0, HB)
        quantize_w(1, 0, HB)
        drain(halves[15, 0], 15, 0, HB)
        interleave(nc.scalar.copy, w_mix[LAST][:, 0:HB, :], w_last[:, 0], 0, HB)
        quantize_w(2, 0, HB)
        drain(halves[14, 1], 14, HB, B)
        drain(halves[15, 1], 15, HB, B)
        interleave(nc.scalar.copy, w_mix[LAST][:, HB:, :], w_last[:, 1], V_LAST, HB)
        quantize_w(1, HB, B)
        interleave(nc.vector.tensor_copy, w_mix[LAST][:, HB:, :], w_last[:, 1], 0, V_LAST)
        quantize_w(LAST, 0, HB)
        quantize_w(2, HB, B)
        quantize_w(LAST, HB, B)
        h_acc = [bank(b) for b in (2, 3, 4, 5)]
        for j in GROUPS:
            for m in range(4):
                second_product(h_acc[m], m, j, 0, HB, j == 0, j == LAST)
        for m in range(4):
            store(finish(h_acc[m], m, 0, HB), m, 0, HB)
        pieces = [(0, HB, B, 6), (1, HB, B, 7), (2, HB, B, 0), (3, HB, B - P, 1), (3, B - P, B, 2)]
        for m, lo, hi, b in pieces:
            h_acc = bank(b)
            for j in GROUPS:
                second_product(h_acc, m, j, lo, hi, j == 0, j == LAST)
            store(finish(h_acc, m, lo, hi), m, lo, hi)
